import numpy as np, ml_dtypes
CORES = [6,15,38,47]
N = 4
import mx_ref
BF = ml_dtypes.bfloat16
def gentries(a):
    return np.ascontiguousarray(a.reshape(8, 16, -1).transpose(0, 2, 1)).reshape(8, -1)
def gtable(e):
    e = np.asarray(e); return np.ascontiguousarray(e.reshape(8, -1, 16).transpose(0, 2, 1)).reshape(128, -1).astype(np.int32)
def gcols(t, e):
    v = np.concatenate([t.reshape(8, 16, -1, 4), np.zeros((8, 16, 1, 4), BF)], axis=2)
    return np.ascontiguousarray(np.stack([v[g][:, e[g]] for g in range(8)])).reshape(128, -1)
def gpick(z, e):
    return np.concatenate([z[16 * g:16 * g + 16][:, e[g]] for g in range(8)])
def tile(rs):
    return np.stack(rs, axis=2).reshape(128, -1).astype(BF)
def pick(q, e):
    c = np.concatenate([q[0].reshape(128, -1, 4), np.zeros((128, 1, 4), np.uint8)], axis=1); s = np.concatenate([q[1], np.ones((16, 1), np.uint8)], axis=1)
    return (np.ascontiguousarray(c[:, e].reshape(128, -1)), np.ascontiguousarray(s[:, e]))
def join(*qs):
    return (np.concatenate([q[0] for q in qs], axis=1), np.concatenate([q[1] for q in qs], axis=1))
def put(q, e, v):
    c, s = q[0].reshape(128, -1, 4).copy(), q[1].copy(); c[:, e] = v[0].reshape(128, -1, 4); s[:, e] = v[1]
    return (c.reshape(128, -1), s)
def pk(c, s):
    return (np.ascontiguousarray(c), mx_ref.live(s))
def emit(q):
    return q[0], q[1]
def packed(v, rng):
    q = [mx_ref.quantize(np.ascontiguousarray(v[r])) for r in range(N)]
    return np.stack([a for a, b in q]), np.stack([mx_ref.plane(b, rng) for a, b in q])
def values_of_codes():
    e, c = np.zeros((128, 128, 4), np.float32), np.zeros((128, 2, 4), np.uint8)
    e[np.arange(128), np.arange(128), 0] = 1
    c[:127, :, 0] = np.arange(256).reshape(2, 128).T[:127]
    return mx_ref.matmul(mx_ref.quantize(e.reshape(128, 512).astype(BF)), (c.reshape(128, 8), np.full((16, 2), 127, np.uint8))).T.reshape(-1).astype(np.float64)
CODE_VALUE, SCALE_VALUE = values_of_codes(), 2.0 ** (np.arange(256) - 127.0)
def decode(q):
    return (CODE_VALUE[q[0]].reshape(16, 8, -1, 4) * SCALE_VALUE[q[1]][:, None, :, None] + 0.0).reshape(128, -1).astype(np.float32)
def f(rng, *shape):
    return mx_ref.flush((rng.standard_normal(shape, dtype=np.float32) * np.exp2(rng.integers(-2, 3, shape[:-1] + (1,)))).astype(BF))
def wide(rng, *shape, cols=0):
    v = rng.standard_normal(shape, dtype=np.float32) * np.exp2(rng.integers(-12, 13, shape)).astype(np.float32)
    if cols: v *= np.repeat(np.exp2(rng.integers(-cols, cols + 1, shape[:-2] + (1, shape[-1] // 4))) * (rng.random(shape[:-2] + (1, shape[-1] // 4)) > 0.0625), 4, axis=-1).astype(np.float32)
    return mx_ref.flush(v.astype(BF))
C, L, M, R = 384, 5, 64, 3
def big(v):
    v = v.astype(np.float32)
    v[np.abs(v) < np.float32(2.0 ** -16)] = 0
    return v.astype(BF)
def numbers_of(rng):
    return {"x": big(f(rng, N, 128, 4 * C)), "u": np.array(f(rng, N, 128, 512)), "v": np.array(f(rng, N, 128, 512))}
def some_links(rng):
    w = rng.choice([8, 16, 32, C], (8, 1, 1))
    return (np.arange(C) + 1 + (rng.random((8, 2, C)) * w).astype(np.int64)) % C
def links_of(rng):
    return np.stack([gtable(some_links(rng).reshape(8, 2 * C)) for r in range(N)])
def layers(rng):
    return big(f(rng, N, 128, 2048)).reshape(N, 8, 16, 4, 8, 16, 4)
def weights(rng, w):
    c, p = packed(np.ascontiguousarray(w).reshape(N, 128, 2048), rng)
    return {"wc": c, "ws": p}
def setup_inputs(rng):
    return {**numbers_of(rng), "nb": links_of(rng), **weights(rng, layers(rng))}
def setup_inputs_ties(rng):
    d = numbers_of(rng)
    o = rng.permutation(N)
    k = rng.integers(-1, 3, (N, 8, C))
    k[o[1]] = rng.integers(-3, 0, (8, C))
    k[o[2]] = 1
    x = d["x"].reshape(N, 8, 16, C, 4)
    x[:, :, 0] = 0
    x[:, :, 0, :, 0] = k.astype(np.float32).astype(BF)
    u = d["u"].reshape(N, 128, 128, 4)
    u[:, :, ::16] = 0
    for h in range(0, 128, 16): u[:, h, h, 0] = 1
    u[o[0], :, ::16] = 0
    w = layers(rng)
    w[:, :, :, :, :, 0] = 0
    return {"x": x.reshape(N, 128, 4 * C), "u": u.reshape(N, 128, 512), "v": d["v"], "nb": links_of(rng), **weights(rng, w)}
def setup_inputs_near(rng):
    d = numbers_of(rng)
    x = d["x"].astype(np.float32).reshape(N, 8, 16, C, 4)
    x[:, :, 0] = 0
    x[:, :, 8:] = 0
    s = rng.integers(0, 16, (N, 8, C))
    s = ((s[:, :, :, None] >> np.arange(4)) & 1) * np.exp2(np.arange(4) - 23.0)
    u = d["u"].reshape(N, 128, 128, 4)
    u[:, :, ::16] = 0
    nb = np.stack([some_links(rng) for r in range(N)])
    n = np.arange(C)
    first = n // 3 * 3 % (C - C % 3)
    o = rng.permutation(N) % 4
    for r in range(N):
        k = 1.0 if o[r] == 0 else 2.0 ** -30
        if o[r] < 2:
            x[r, :, 0, :, 0] = rng.choice([-1.0, 1.0], (8, C))
            x[r, :, 11, :, 0] = 2.0 ** -10
            x[r, :, 8] = s[r]
            g, e = rng.integers(8), rng.permutation(C)
            nb[r, g, 0, e], nb[r, g, 1, e] = e[first + (n + 1) % 3], e[first + (n + 2) % 3]
            x[r, g, 0, C - 1, 0] = 1.0
            x[r, g, 8, C - 1] = np.exp2(np.arange(4) - 23.0)
        elif o[r] == 2:
            x[r, :, 8, :, 0] = rng.integers(-1, 3, (8, C)) * 2.0 ** -29
            for g in rng.permutation(8)[:4]: x[r, g, 8, rng.integers(C), 0] = rng.choice([-1.0, 1.0]) * 2.0 ** 29
        else:
            x[r, :, 0, :, 0] = rng.choice([0.0, 0.0, 0.0, 0.0, 0.0, 0.0, 1.0, -1.0], (8, C))
            x[r, :, 8] = s[r] * rng.choice([-1.0, 1.0], (8, C, 1))
        for h in range(0, 128, 16):
            u[r, h, h, 0] = 1.0 if o[r] == 3 else 0.0 if o[r] == 2 else k
            u[r, h + 8, h] = k
            if o[r] < 2: u[r, h + 11, h, 0] = k
    w = layers(rng)
    for i in [0, 8, 9, 10, 11, 12, 13, 14, 15]:
        w[:, :, i] = 0
        w[:, :, :, :, :, i] = 0
    return {"x": x.reshape(N, 128, 4 * C).astype(BF), "u": u.reshape(N, 128, 512), "v": d["v"], "nb": np.stack([gtable(nb[r].reshape(8, 2 * C)) for r in range(N)]), **weights(rng, w)}
def setup_inputs_huge(rng):
    d = numbers_of(rng)
    c = rng.choice([-1.0, 1.0], (N, 1, C, 1))
    c[rng.permutation(N)[:N // 2]] = -1.0
    x = 2.0 ** 30 * (0.6 + 0.2 * rng.random((N, 128, C, 4))) * c
    u = d["u"].reshape(N, 128, 128, 4)
    u[:, :, ::16] = (2.0 ** 30 * (1.0 - 0.1 * rng.random((N, 128, 8, 4)))).astype(np.float32).astype(BF)
    w = np.zeros((N, 128, 4, 128, 4), np.float32)
    i = np.arange(128)
    for b in range(4): w[:, i, b, i, b] = -2
    return {"x": x.astype(np.float32).reshape(N, 128, 4 * C).astype(BF), "u": u.reshape(N, 128, 512), "v": d["v"], "nb": links_of(rng), **weights(rng, w.astype(BF))}
def setup_inputs_forms(rng):
    d = numbers_of(rng)
    x = d["x"].astype(np.float32).reshape(N, 8, 16, C, 4)
    a = (1.0 + (2 * rng.integers(0, 64, (N, 8, 8, C, 4)) + 1) * 2.0 ** -7) * np.exp2(-rng.integers(8, 14, (N, 8, 8, C, 4)).astype(np.float64))
    x[:, :, :8] = a * rng.choice([-1.0, 1.0], a.shape)
    x[:, :, 0, :, 0] = rng.choice([1.875, 1.96875], (N, 8, C))
    x[:, :, 1, :, 0] = rng.integers(8, 10, (N, 8, C)) * rng.choice([-1.0, 1.0], (N, 8, C)) * 2.0 ** -16
    u = d["u"].reshape(N, 128, 128, 4)
    u[:, :, ::16] = 0
    for h in range(0, 128, 16): u[:, h + 1, h, 0] = 1
    nb = np.stack([some_links(rng) for r in range(N)])
    o = rng.permutation(N) % 4
    for r in range(N):
        count = rng.permutation([M, M, M, M - 1, M + 1, 1, 0, C])
        for g in range(8):
            if o[r] == 0: nb[r, g, 1] = nb[r, g, 0]
            if o[r] in (1, 2):
                n = rng.integers(0, 2 * L - 1, C)
                n[:2 * L - 2] = np.arange(1, 2 * L - 1)
                n[2 * L - 2] = 2 * L - 2
                if o[r] == 1: n[L - 2] = 2 * L - 2
                else: n[2 * L - 3] = 0
                m = n.copy()
                e = 2 * L - 1 + np.arange(min(int(count[g]), C - 2 * L + 1))
                if o[r] == 1: n[e] = rng.integers(0, 2, len(e)) * (L - 1)
                else: n[e] = rng.integers(0, 2 * L - 2, len(e))
                m[e] = (n[e] + L - 1) % (2 * L - 2)
                k = rng.permutation(C)
                nb[r, g, 0, k], nb[r, g, 1, k] = k[n], k[m]
    return {"x": x.reshape(N, 128, 4 * C).astype(BF), "u": u.reshape(N, 128, 512), "v": d["v"], "nb": np.stack([gtable(nb[r].reshape(8, 2 * C)) for r in range(N)]), **weights(rng, layers(rng))}
def setup_inputs_spread(rng):
    d = setup_inputs(rng)
    d["x"] = big(wide(rng, N, 128, 4 * C, cols=6))
    return d
def check_inputs(d):
    b = []
    for k in ("x", "u", "v"):
        a = np.abs(d[k].astype(np.float32))
        if not (np.isfinite(a).all() and ((a == 0) | (a >= 2.0 ** -30) & (a <= 2.0 ** 30)).all()): b.append("a value of " + k)
    if not ((d["nb"] >= 0) & (d["nb"] < C)).all(): b.append("an entry of nb")
    none, least, most = [emit(mx_ref.quantize(np.full((128, 16), k, np.float32).astype(BF)))[1][0, 0] for k in (0.0, 2.0 ** -30, 2.0 ** 30)]
    for r in range(N):
        if ((d["wc"][r] == 0x7F) | (d["wc"][r] == 0xFF)).any(): b.append("wc: a code that is no number")
        s = mx_ref.live(d["ws"][r])
        if ((s != none) & ((s < least) | (s > most))).any(): b.append("ws: a scale out of range")
    return b
def bubbles(a, s):
    at = lambda t, e: np.take_along_axis(t, e, axis=1)
    c = np.where(s > 0, a[:, C:], a[:, :C])
    p, q = [a[:, :C]], [a[:, C:]]
    for k in range(1, L):
        p.append(at(c, p[-1]))
        q.append(at(c, q[-1]))
    i, j = np.full((8, C), -1), np.full((8, C), -1)
    for n in reversed(range(2 * L - 1)):
        for k in reversed(range(max(0, n - L + 1), min(n, L - 1) + 1)):
            met = p[k] == q[n - k]
            i[met], j[met] = k, n - k
    is_bubble = (i >= 0) & (p[0] != q[0])
    o = np.lexsort((-s, ~is_bubble))[:, :M]
    filled = at(is_bubble, o)
    g, k = np.arange(8)[:, None, None], np.arange(L)
    np0 = np.stack(p, axis=2)[g, o[:, :, None], np.minimum(k, at(i, o)[:, :, None])]
    nq0 = np.stack(q, axis=2)[g, o[:, :, None], np.minimum(k, at(j, o)[:, :, None])]
    one = at(s, at(q[0], o)) > at(s, at(p[0], o))
    new = a.copy()
    h, m = np.nonzero(filled)
    new[h, (o + C * ~one)[h, m]] = np0[h, m, L - 1]
    slots = [np.where(filled[:, :, None], t, -1).reshape(8, L * M) for t in (np0, nq0, np.where(one[:, :, None], nq0, np0))]
    e = np.full((8, C), -1)
    for n in reversed(range(L * M)):
        h = np.flatnonzero(slots[2][:, n] >= 0)
        e[h, slots[2][h, n]] = n
    return slots[0], slots[1], e, new
def reference(x, u, v, nb, wc, ws):
    qu = [mx_ref.quantize(u[r]) for r in range(N)]
    lay = [pk(wc[r], ws[r]) for r in range(N)]
    now = [x[r] for r in range(N)]
    links = [gentries(nb[r]).astype(np.int64) for r in range(N)]
    for t in range(R):
        own, sent, place = [], [], []
        for r in range(N):
            q = mx_ref.quantize(now[r])
            own.append(decode(q))
            s = mx_ref.matmul(qu[r], q)[::16] + np.float32(0.0)
            a, b, e, links[r] = bubbles(links[r], s)
            place.append(e)
            w = own[r].astype(BF)
            sent.append(mx_ref.quantize(((gcols(w, a).astype(np.float32) + gcols(w, b).astype(np.float32)) * np.float32(0.5)).astype(BF)))
        for r in range(N):
            came, made = sent[(r - 1) % N], []
            for b in range(4):
                h = mx_ref.matmul(pick(lay[r], np.arange(128 * b, 128 * b + 128)), came) * np.float32(0.03125)
                made.append(gpick(np.concatenate([h, np.zeros((128, 1), np.float32)], axis=1), place[r]) + own[r][:, b::4])
            now[r] = tile(made)
    y, ol = np.zeros((N, 128, C), np.float32), np.zeros((N, 8, 2 * C), np.float32)
    oc, osc = np.zeros((N, 128, 4 * C), np.uint8), np.zeros((N, 16, C), np.uint8)
    for r in range(N):
        q = mx_ref.quantize(now[r])
        y[r] = mx_ref.matmul(mx_ref.quantize(v[r]), q)
        ol[r] = links[r]
        oc[r], osc[r] = emit(q)
    return {"y": y, "ol": ol, "oc": oc, "osc": osc}

@@ -1,0 +1,514 @@
+from concourse.mybir import dt, AluOpType as O, ActivationFunctionType as AF
+
+N, C, L, M, R = 4, 384, 5, 64, 3
+SL = L * M
+PAIRS = sorted(((i + j, i, j) for i in range(L) for j in range(L)))
+NB = len(PAIRS) + 1
+EB = SL + 2
+BIG = 1e29
+UP = 1024.0
+CUT = 224
+VROWS = 10
+AROWS = (20, 19, 18)
+TILES = [(rows, max(128, 16 * min(max(rows), 24))) for rows in ([24, 23, 22, 21], [20, 19, 18, 17], [16, 15, 14, 13],
+                                                              [12, 11, 10, 9], [8, 7, 6, 5], [4, 3, 2, 1])]
+
+F32, BF, I32, U16, F16, COD = "float32", "bfloat16", "int32", "uint16", "float16", "float8_e4m3fn_x4"
+SCRATCH, PLACE = {}, {}
+
+
+def _own(dtype, spec):
+    for item in spec.split():
+        name, cols = item.split(":")
+        SCRATCH[name] = ("sbuf", [128, int(cols)], dtype)
+
+
+def _pool(pool, dtype, spec):
+    at = 0
+    for item in spec.split():
+        name, cols = item.split(":")
+        PLACE[name] = (pool, at)
+        at += (int(cols) + 31) // 32 * 32
+    SCRATCH[pool] = ("sbuf", [128, at], dtype)
+
+
+_own(BF, "x0:1536 x1:1536 x2:1536 x3:1536 ut:512 vt:512 et:2048 ones:512 za:1280 zt:1280")
+_own(BF, "fb0:384 fb1:384 fb2:384 fb3:384 db0:400 db1:400 db2:400 db3:400 bd:512 bd1:512 mt:5632")
+_own(F32, "hs0:328 hs1:328 hs2:328 hs3:328 lrep:768 ys:384")
+_own(I32, "nbl:48 nbw:768")
+for _n, _k in (("w", 512), ("v", 128), ("u0", 128), ("u", 128), ("e", 512), ("z", 320), ("bd", 128), ("m", 1408)):
+    _own(COD, "q%s:%d" % (_n, _k))
+    _own("uint8", "s%s:%d" % (_n, _k))
+for _t in range(R):
+    _own(COD, "lc%d:384" % _t)
+    _own("uint8", "ls%d:384" % _t)
+    _own(U16, "own%d:40 came%d:40" % (_t, _t))
+for _t in range(R + 1):
+    _own(COD, "qx%d:384" % _t)
+    _own("uint8", "sx%d:384" % _t)
+_pool("poolf", F32, "jm16:768 jz:768 jy:768 md:384 r16:384 da:768 db:768 mk:384 d0f:384 idr:384 b0:384 col:32 nl:24 nm:24 "
+      "nbias:24 cc:40 cd:40 ce:40 ll:48 l2:48 dl:24 la:768 lb:768 smd:384 sn:384 ssb:384 sp:768 fl:24 fx:24 ix:24 cm:24 "
+      "cl:24 v0:384 v1:384 v2:384 v3:384 vb:384 npos:24 rk2:24 cx:384 cs:384 ms:384 mi:384 ff:384 cnt:24 rk:24 order:384 "
+      "o1:64 ol:64 pm:64 qn:64 sc:128 on:64 pab:128 ht:384 htt:384 ab:128 w:320 pp:64 pe:320 pr:320 pl:320 ps:320 k1:64 "
+      "kl:64 po:8 n64:320")
+_pool("poolb", BF, "gg:768 gt:768 r16b:384 d1k:624 one6:1932 ne:624 st:624 ex:384 kr:384 tm:384 sg:1536 eqs:384 "
+      "junk:1536 xp:320 d0e:7728")
+_pool("pooli", I32, "pi:2 li:48 li2:24 li3:20 li4:24 li5:8 ca:40 cb:40 kai:64 jm:64 pi3:60 pri:320 xri:320")
+_pool("poolu", U16, "upl:8 inl:48 exr:24 exp:20 pz:40 lu:48 ixu:24 cu:24 rku:24 ou:4 eu:24 pu:4")
+_pool("poolh", F16, "ste:7728")
+PSUM = ("pS", "pC", "pF0", "pF1", "pF2", "pF3")
+for _n in PSUM:
+    SCRATCH[_n] = ("psum", [128, 512], F32)
+NDMA = 40
+SEMAPHORES = (["qv_", "qa_", "qt_", "qp_", "lsent"] + ["arx%d" % t for t in range(R)] + ["arl%d" % t for t in range(R)]
+              + ["d%d" % k for k in range(NDMA)])
+
+
+def rank_program(g, core, T, topo):
+    rank = T.rank_of(core)
+    if rank is None:
+        return
+    nxt = T.cores[(rank + 1) % N]
+    rid, pid = topo.addr(nxt)[:2]
+    mask, width = topo.mask(core, nxt), len(topo.engines(core, nxt))
+
+    eng = {"v": g.vector, "a": g.scalar, "t": g.tensor, "p": g, "s": g.sync}
+    semof = {"v": "qv_", "a": "qa_", "t": "qt_", "p": "qp_"}
+    count, known = {}, {q: {} for q in eng}
+    clocks, hist = {}, {}
+    ndma = [0]
+
+    def need(q, src, val):
+        if known[q].get(src, 0) >= val:
+            return
+        eng[q].wait_ge(T.sem[src], val)
+        for s, n in clocks.get((src, val), {src: val}).items():
+            if n > known[q].get(s, 0):
+                known[q][s] = n
+
+    def meet(x, y):
+        return x[0] < y[1] and y[0] < x[1] and not (x[2] == y[2] and (x[0] - y[0]) % x[2])
+
+    def covers(x, y):
+        return x[0] <= y[0] and y[1] <= x[1] and (x[2] == 1 or x[2] == y[2] and (x[0] - y[0]) % x[2] == 0)
+
+    def order(q, reads, writes):
+        todo = {}
+        mine = semof.get(q)
+        for r, w in [(r, False) for r in reads] + [(r, True) for r in writes]:
+            for piece, src, val, wrote in hist.get(r[0], ()):
+                if meet(r[1:], piece) and (w or wrote or (r[0] in PSUM and src != mine)):
+                    todo[src] = max(todo.get(src, 0), val)
+        for src in sorted(todo, key=lambda s: s != mine):
+            need(q, src, todo[src])
+
+    def note(src, val, reads, writes):
+        for r in writes:
+            h = [x for x in hist.get(r[0], ()) if not covers(r[1:], x[0])]
+            hist[r[0]] = h + [(r[1:], src, val, True)]
+        for r in reads:
+            if r not in writes:
+                h = [x for x in hist.get(r[0], ()) if not (x[0] == r[1:] and x[1] == src and not x[3])]
+                hist[r[0]] = h + [(r[1:], src, val, False)]
+
+    def emit(q, fn, reads, writes):
+        order(q, reads, writes)
+        src = semof[q]
+        count[src] = count.get(src, 0) + 1
+        fn().then_inc(T.sem[src], 1)
+        clocks[(src, count[src])] = {**known[q], src: count[src]}
+        note(src, count[src], reads, writes)
+
+    def dma(q, out, in_):
+        order(q, in_[1], out[1])
+        src = "d%d" % ndma[0]
+        ndma[0] += 1
+        eng[q].dma_start(out[0], in_[0]).then_inc(T.sem[src], 16)
+        count[src] = 16
+        clocks[(src, 16)] = {**known[q], src: 16}
+        note(src, 16, in_[1], out[1])
+
+    def send(out, in_, sem):
+        order("p", in_[1], [])
+        g.remote_dma(out, in_[0], T.sem[sem], T.sem.lsent, pid, rid, mask)
+
+    def A(n, a, b, s=1):
+        buf, o = PLACE.get(n, (n, 0))
+        return (T[buf][:, o + a:o + b:s] if s > 1 else T[buf][:, o + a:o + b], [(n, a, b, s)])
+
+    def U8(n, a, b):
+        return (T[n][:, a:b].bitcast(dt.uint8), [(n, a, b, 1)])
+
+    def U32(n, a, b):
+        return (T[n][:, a:b].bitcast(dt.uint32), [(n, a, b, 1)])
+
+    def I(win, off):
+        return (win[0].indirect(off[0]), win[1] + off[1])
+
+    def ext(v):
+        return (v, [])
+
+    def ap(x):
+        return x[0] if isinstance(x, tuple) else x
+
+    def rd(*xs):
+        return [r for x in xs if isinstance(x, tuple) for r in x[1]]
+
+    V = g.vector
+
+    def tc(out, in_):
+        emit("v", lambda: V.tensor_copy(out[0], in_[0]), rd(in_), out[1])
+
+    def scatter(win, off, in_):
+        emit("v", lambda: V.tensor_copy(win[0].indirect(off[0]), in_[0]), rd(off, in_), win[1])
+
+    def tt(out, a, b, op):
+        emit("v", lambda: V.tensor_tensor(out[0], a[0], b[0], op), rd(a, b), out[1])
+
+    def ts(out, a, s1, op0, s2=None, op1=None):
+        if op1 is None:
+            emit("v", lambda: V.tensor_scalar(out[0], a[0], ap(s1), None, op0), rd(a, s1), out[1])
+        else:
+            emit("v", lambda: V.tensor_scalar(out[0], a[0], ap(s1), ap(s2), op0, op1), rd(a, s1, s2), out[1])
+
+    def scan(out, d0, d1, op0, op1):
+        emit("v", lambda: V.tensor_tensor_scan(out[0], d0[0], d1[0], 0.0, op0, op1), rd(d0, d1), out[1])
+
+    def turn(out, in_):
+        emit("v", lambda: V.transpose(out[0], in_[0]), rd(in_), out[1])
+
+    def fill(out, k):
+        emit("v", lambda: V.memset(out[0], k), [], out[1])
+
+    def quant(q, s, x):
+        emit("v", lambda: V.quantize_mx(q[0], s[0], x[0]), rd(x), q[1] + s[1])
+
+    def act(out, in_, func=AF.Copy, bias=None, scale=None, accum=None):
+        kw = {}
+        if bias is not None:
+            kw["bias"] = ap(bias)
+        if scale is not None:
+            kw["scale"] = ap(scale)
+        if accum is not None:
+            kw["accum_out"] = accum[0]
+        emit("a", lambda: g.scalar.activation(out[0], in_[0], func, **kw), rd(in_, bias, scale),
+             out[1] + (accum[1] if accum is not None else []))
+
+    def mm(out, w, ws, x, xs, start=True, stop=True):
+        emit("t", lambda: g.tensor.matmul_mx(out[0], w[0], ws[0], x[0], xs[0], start, stop), rd(w, ws, x, xs),
+             out[1] if start else [])
+        if not start:
+            note(semof["t"], count[semof["t"]], [], [("pC", 0, C, 1)])
+
+    def iota(out, pattern, base, cm, flag=False):
+        kw = {"allow_small_or_imprecise_dtypes": True} if flag else {}
+        emit("p", lambda: g.iota(out[0], pattern, base, cm, **kw), [], out[1])
+
+    def choose(out, in_, pattern, cmp, base, cm):
+        emit("p", lambda: g.affine_select(out[0], in_[0], pattern, cmp, 0.0, base, cm), in_[1], out[1])
+
+    (kI, kM0, kMU, kL0, kL1, kL2, kU0, kU1, kU2, kOff, kCA, kCA0, kCB, kCB0, kI48, kT, knot15) = [
+        A("col", k, k + 1) for k in range(17)]
+    md, r16 = lambda n: A("md", 0, n), lambda n: A("r16", 0, n)
+
+    dma("s", A("ut", 0, 512), ext(T.u[:, :]))
+    dma("a", A("x0", 0, 768), ext(T.x[:, 0:768]))
+    dma("s", A("x0", 768, 1536), ext(T.x[:, 768:1536]))
+    dma("a", A("nbl", 0, 48), ext(T.nb[:, :]))
+    rows = [("nbw%d" % i, 0, 768, 1) for i in range(16)]
+    for i in range(16):
+        dma("sa"[i % 2], (T.nbw[i:128:16, :], [rows[i]]), ext(T.nb[:, :]))
+    nbw = (T.nbw[:, 0:768], rows)
+    dma("s", U8("qw", 0, 512), ext(T.wc[:, :]))
+    dma("s", A("sw", 0, 512), ext(T.ws[:, :]))
+    dma("s", A("vt", 0, 512), ext(T.v[:, :]))
+
+    iota(A("pi", 0, 1), [[1, 1]], 0, 1)
+    iota(A("li5", 0, 8), [[16, 8]], 0, 0)
+    iota(A("li2", 0, 24), [[16, 24]], 0, 0)
+    iota(A("li", 0, 48), [[1, 48]], 0, 0)
+    iota(A("jm16", 0, 768), [[0, 48], [1, 16]], 0, 0, True)
+    iota(A("idr", 0, C), [[1, C]], 0, 0, True)
+    iota(A("li3", 0, 20), [[1, 5], [16, 4]], 0, 0)
+    iota(A("li4", 0, 24), [[NB, 24]], NB - 1, 0)
+
+    def tile_constants():
+        for b in range(4):
+            iota(A("db%d" % b, C, C + 16), [[0, 16]], 0, 0, True)
+        ones, half, blocks = A("ones", 0, 512), A("bd1", 0, 512), A("bd", 0, 512)
+        iota(ones, [[0, 512]], 1, 0, True)
+        for b in range(4):
+            choose(A("et", 512 * b, 512 * b + 512), ones, [[4, 128], [1, 4]], O.is_equal, -b, -4)
+        choose(half, ones, [[-16, 8], [0, 64]], O.is_ge, 0, 1)
+        choose(blocks, half, [[16, 8], [0, 64]], O.is_ge, 15, -1)
+        for b in range(4):
+            iota(A("hs%d" % b, SL, SL + 8), [[0, 8]], 0, 0, True)
+        iota(A("one6", 0, 6 * EB), [[0, 6 * EB]], 1, 0, True)
+
+    ts(A("pi", 1, 2), A("pi", 0, 1), 15, O.bitwise_and)
+    tc(A("upl", 0, 8), A("li5", 0, 8))
+    tc(kI, A("pi", 1, 2))
+    ts(kM0, kI, 0.0, O.is_equal)
+    ts(kCB, kI, 1.0, O.add)
+    ts(kI48, kI, 48.0, O.mult)
+    ts(kMU, kI, 0.0, O.is_equal, UP, O.mult)
+    act(A("jz", 0, C), A("jm16", 0, C), AF.Square, bias=kI, scale=-1.0)
+    act(md(C), A("jz", 0, C), AF.Relu, bias=1.0, scale=-1.0)
+    act(r16(C), A("jm16", 0, C), AF.Sign)
+    act(A("b0", 0, C), A("idr", 0, C), AF.Identity, bias=kMU, scale=kM0)
+    ts(A("inl", 0, 48), A("li", 0, 48), kI48, O.add)
+    ts(A("nl", 0, 24), A("li2", 0, 24), kI, O.add)
+    for k, (stay, up) in enumerate(((kL0, kU0), (kL1, kU1), (kL2, kU2))):
+        ts(stay, kI, k + 1.5, O.is_lt)
+        ts(up, kI, k + 1.5, O.is_lt, UP, O.mult)
+    ts(kT, kI, UP, O.mult, -4 * UP, O.add)
+    ts(kCA, kI, 16.0, O.mult, 1.0, O.add)
+    ts(kCB0, kM0, -2.0, O.mult, kCB, O.add)
+    ts(kOff, kT, 0.0, O.min, -192.0, O.add)
+    ts(kCA0, kM0, -2.0, O.mult, kCA, O.add)
+    quant(A("qu0", 0, 128), A("su0", 0, 128), A("ut", 0, 512))
+    tc(U32("qu", 0, 128), I(U32("qu0", 0, 128), A("upl", 0, 8)))
+    tc(A("su", 0, 128), I(A("su0", 0, 128), A("upl", 0, 8)))
+
+    S = A("pS", 0, C)
+
+    def scores(t):
+        qx, sx = A("qx%d" % t, 0, C), A("sx%d" % t, 0, C)
+        quant(qx, sx, A("x%d" % t, 0, 4 * C))
+        mm(S, A("qu", 0, 128), A("su", 0, 128), qx, sx)
+        send(T["lc%d" % t][:, 0:C].bitcast(dt.uint8), U8("qx%d" % t, 0, C), "arx%d" % t)
+        send(T["ls%d" % t][:, 0:C], sx, "arx%d" % t)
+        note("arx%d" % t, 2 * width, [], [("lc%d" % t, 0, C, 1), ("ls%d" % t, 0, C, 1)])
+        return qx, sx
+
+    def planes(codes, plane):
+        for b in range(4):
+            mm(A("pF%d" % b, 0, C), A("qe", 128 * b, 128 * b + 128), A("se", 128 * b, 128 * b + 128), codes, plane)
+
+    def late_constants():
+        quant(A("qe", 0, 512), A("se", 0, 512), A("et", 0, 2048))
+        tc(A("exr", 0, 24), A("li4", 0, 24))
+        tc(A("exp", 0, 20), A("li3", 0, 20))
+        f = [16 * i + j + 1 for _, i, j in PAIRS]
+        f[0] = 0
+        steps = [-f[-1]] + [f[r] - f[r - 1] for r in range(len(PAIRS) - 1, 0, -1)] + [0]
+        most = max(steps, key=steps.count)
+        fill(A("d1k", 0, 24 * NB), float(most))
+        for e in range(NB):
+            if steps[e] != most:
+                fill(A("d1k", e, 24 * NB, NB), float(steps[e]))
+        fill(A("ne", 0, 24 * NB, NB), 0.0)
+        quant(A("qbd", 0, 128), A("sbd", 0, 128), A("bd", 0, 512))
+        fill(A("cnt", 0, 1), 0.0)
+        at = 0
+        for rows, w in TILES:
+            fill(A("mt", at + 64 * min(rows), at + 4 * w), 0.0)
+            at += 4 * w
+        ts(A("npos", 0, 24), A("li2", 0, 24), kI, O.subtract, 15.0, O.add)
+        ts(knot15, kI, 15.0, O.is_lt)
+        act(A("mk", 0, C), md(C), AF.Identity, bias=-2e29, scale=5e29)
+        act(A("d0f", 0, C), r16(C), AF.Identity, bias=-2e29, scale=5e29)
+        act(A("r16b", 0, C), r16(C))
+
+    def last_constants():
+        act(A("ce", 0, 20), A("nl", 0, 20))
+        act(A("ce", 20, 40), A("nl", 0, 20), AF.Identity, bias=float(SL - 1), scale=-1.0)
+        act(A("cd", 0, 40), A("ce", 0, 40), scale=64.0)
+        ts(A("ca", 0, 40), A("ce", 0, 40), 205.0, O.mult)
+        ts(A("cb", 0, 40), A("ca", 0, 40), 10, O.arith_shift_right)
+        ts(A("cc", 0, 40), A("cb", 0, 40), -319.0, O.mult)
+        tt(A("ce", 0, 40), A("cc", 0, 40), A("cd", 0, 40), O.add)
+        tc(A("pz", 0, 40), A("ce", 0, 40))
+        act(A("jz", 0, 768), A("jm16", 0, 768), AF.Square, bias=kI, scale=-1.0)
+        act(A("da", 0, 768), A("jz", 0, 768), AF.Sign)
+        act(A("jy", 0, 768), A("jm16", 0, 768), AF.Square, bias=kCB, scale=-1.0)
+        act(A("db", 0, 768), A("jy", 0, 768), AF.Sign)
+
+    def search_constants():
+        act(A("nm", 0, 24), A("nl", 0, 24), AF.Identity, bias=-192.0)
+        act(A("nbias", 0, 24), A("nl", 0, 24), AF.Identity, bias=32.0 * 192, scale=-32.0)
+        fill(A("d0e", 0, 24 * EB, EB), 0.0)
+        fill(A("d0e", 1, 24 * EB, EB), 0.0)
+        quant(A("qv", 0, 128), A("sv", 0, 128), A("vt", 0, 512))
+
+    for t in range(R):
+        last = t == R - 1
+        qx, sx = scores(t)
+        if t == 0:
+            tile_constants()
+        if t == 0:
+            tc(A("lrep", 0, 768), I(nbw, A("inl", 0, 48)))
+            tc(A("ll", 0, 48), A("nbl", 0, 48))
+        else:
+            scan(A("la", 0, 768), A("da", 0, 768), A("lrep", 0, 768), O.mult, O.add)
+            scan(A("lb", 0, 768), A("db", 0, 768), A("lrep", 0, 768), O.mult, O.add)
+            ts(A("l2", 0, 48), A("lb", 15, 768, 16), knot15, O.mult)
+            tt(A("ll", 0, 48), A("la", 15, 768, 16), A("l2", 0, 48), O.subtract)
+        tt(A("smd", 0, C), S, md(C), O.mult)
+        act(A("ssb", 0, C), S)
+        tt(A("dl", 0, 24), A("ll", 24, 48), A("ll", 0, 24), O.subtract)
+        scan(A("sn", 0, C), r16(C), A("smd", 0, C), O.mult, O.add)
+        sl = A("sn", 15, C, 16)
+        ts(A("fx", 0, 24), sl, 0.0, O.is_gt, 384.0, O.mult)
+        ts(A("fl", 0, 24), sl, 0.0, O.is_gt)
+        tt(A("ix", 0, 24), A("fx", 0, 24), A("nl", 0, 24), O.add)
+        tt(A("cm", 0, 24), A("fl", 0, 24), A("dl", 0, 24), O.mult)
+        tc(A("ixu", 0, 24), A("ix", 0, 24))
+        tt(A("cl", 0, 24), A("cm", 0, 24), A("ll", 0, 24), O.add)
+        tt(A("v0", 0, C), I(A("lrep", 0, 768), A("ixu", 0, 24)), A("b0", 0, C), O.max)
+        tc(A("cu", 0, 24), A("cl", 0, 24))
+        tc(A("lu", 0, 48), A("ll", 0, 48))
+        for k, (stay, up) in enumerate(((kL0, kU0), (kL1, kU1), (kL2, kU2))):
+            act(A("vb", 0, CUT), A("v%d" % k, 0, CUT), AF.Identity, bias=up, scale=stay)
+            ts(A("vb", CUT, C), A("v%d" % k, CUT, C), stay, O.mult, up, O.add)
+            tt(A("v%d" % (k + 1), 0, C), I(A("v%d" % k, 0, C), A("cu", 0, 24)), A("vb", 0, C), O.max)
+        act(A("gg", 0, C), I(A("v3", 0, C), A("lu", 0, 24)), AF.Identity, bias=kOff)
+        ts(A("gg", C, 2 * C), I(A("v3", 0, C), A("lu", 24, 48)), kOff, O.add)
+        if t == 0:
+            late_constants()
+        planes(qx, sx)
+        turn(A("gt", C, 2 * C), A("gg", C, 2 * C))
+        turn(A("gt", 0, C), A("gg", 0, C))
+        act(A("sp", 0, 768), I(A("ssb", 0, C), A("lu", 0, 48)))
+        for b in range(4):
+            act(A("fb%d" % b, 0, C), A("pF%d" % b, 0, C))
+        p = lambda i: A("gt", i, C, 16)
+        q = lambda j: A("gt", C + j, 2 * C, 16)
+        for r in range(len(PAIRS)):
+            tt(A("ne", 25 - r, 24 * NB, NB), p(PAIRS[r][1]), q(PAIRS[r][2]), O.not_equal)
+        scan(A("st", 0, 24 * NB), A("ne", 0, 24 * NB), A("d1k", 0, 24 * NB), O.mult, O.add)
+        tc(A("ex", 0, C), I(A("st", 0, 24 * NB), A("exr", 0, 24)))
+        turn(A("kr", 0, C), A("ex", 0, C))
+        ts(A("tm", 0, C), A("kr", 0, C), 0.0, O.is_equal, -BIG, O.mult)
+        tt(A("ms", 0, C), S, A("tm", 0, C), O.add)
+        tt(A("mi", 0, C), A("ms", 0, C), A("mk", 0, C), O.min)
+        scan(A("ff", 0, C), A("d0f", 0, C), A("mi", 0, C), O.min, O.max)
+        spot, at = {}, 0
+        for rows, w in TILES:
+            for i, c in enumerate(rows):
+                spot[c] = A("mt", at + i, at + 64 * min(c, 24), 4)
+            at += 4 * w
+        score = lambda c: A("ff", 16 * c + 15, 16 * c + 16)
+        for c in AROWS:
+            sg = A("sg", C * (c % 4), C * (c % 4) + 16 * c)
+            act(sg, A("ms", 0, 16 * c), AF.Sign, bias=score(c), scale=-1.0)
+            act(spot[c], sg, AF.Relu, accum=A("cnt", c, c + 1))
+        at = 0
+        for k, (rows, w) in enumerate(TILES):
+            for c in rows:
+                if c == 24:
+                    tt(spot[c], A("ms", 0, C), A("ff", 0, C), O.is_le)
+                    scan(A("eqs", 0, C), A("r16b", 0, C), spot[c], O.mult, O.add)
+                elif c not in AROWS:
+                    ts(spot[c], A("ms", 0, 16 * c), score(c), O.is_lt)
+                    act(A("junk", C * (c % 4), C * (c % 4) + 16 * c), spot[c], accum=A("cnt", c, c + 1))
+            a = at // 4
+            quant(A("qm", a, a + w), A("sm", a, a + w), A("mt", at, at + 4 * w))
+            mm(A("pC", 0, w), A("qbd", 0, 128), A("sbd", 0, 128), A("qm", a, a + w), A("sm", a, a + w), k == 0, k == 5)
+            at += 4 * w
+        if t == 0:
+            last_constants()
+        tt(A("rk", 0, 24), A("npos", 0, 24), A("eqs", 15, C, 16), O.subtract)
+        tt(A("cx", 0, C), A("pC", 0, C), md(C), O.mult)
+        tt(A("rk2", 0, 24), A("rk", 0, 24), A("cnt", 0, 24), O.subtract)
+        scan(A("cs", 0, C), r16(C), A("cx", 0, C), O.mult, O.add)
+        tt(A("rk", 0, 24), A("rk2", 0, 24), A("cs", 15, C, 16), O.add)
+        tc(A("rku", 0, 24), A("rk", 0, 24))
+        scatter(A("order", 0, C), A("rku", 0, 24), A("idr", 0, C))
+        tt(A("o1", 0, 64), A("order", 0, 64), md(64), O.mult)
+        scan(A("ol", 0, 64), r16(64), A("o1", 0, 64), O.mult, O.add)
+        tc(A("ou", 0, 4), A("ol", 15, 64, 16))
+        ou = A("ou", 0, 4)
+        for h in range(2):
+            act(A("sc", 64 * h, 64 * h + 64), I(A("sp", C * h, C * h + C), ou))
+        tc(A("kai", 0, 64), I(A("kr", 0, C), ou))
+        ts(A("pm", 0, 64), I(A("gg", 0, C), ou), 192.0, O.add)
+        ts(A("qn", 0, 64), I(A("gg", C, 2 * C), ou), 192.0, O.add)
+        ts(A("jm", 0, 64), A("kai", 0, 64), 15, O.bitwise_and)
+        tt(A("on", 0, 64), A("sc", 64, 128), A("sc", 0, 64), O.is_gt)
+        act(A("ht", 256, 320), A("on", 0, 64), scale=-511.0)
+        ts(A("ht", 0, 64), A("kai", 0, 64), kCA0, O.is_lt)
+        ts(A("pab", 0, 64), A("kai", 0, 64), kCA, O.is_ge)
+        ts(A("ht", 64, 128), A("jm", 0, 64), kCB0, O.is_lt)
+        ts(A("pab", 64, 128), A("jm", 0, 64), kCB, O.is_ge)
+        ts(A("ht", 320, 384), A("kai", 0, 64), 0.0, O.is_equal, float(C * 513), O.mult)
+        tt(A("ht", 128, 192), A("pab", 0, 64), A("pm", 0, 64), O.mult)
+        tt(A("ht", 192, 256), A("pab", 64, 128), A("qn", 0, 64), O.mult)
+        turn(A("htt", 0, 384), A("ht", 0, 384))
+        scan(A("ab", 0, 128), A("htt", 0, 128), A("htt", 128, 256), O.mult, O.add)
+        W = lambda k: A("w", 64 * k, 64 * k + 64)
+        tt(W(0), A("ab", 64, 128), A("ab", 0, 64), O.subtract)
+        ts(W(1), A("ab", 64, 128), 512.0, O.mult)
+        tt(W(2), A("ab", 0, 64), A("htt", 320, 384), O.add)
+        tt(W(3), W(0), A("htt", 256, 320), O.mult)
+        tt(W(4), W(1), W(2), O.add)
+        tt(A("pp", 0, 64), W(4), W(3), O.add)
+        tc(A("pe", 0, SL), I(A("pp", 0, 64), A("exp", 0, 20)))
+        turn(A("pr", 0, SL), A("pe", 0, SL))
+        tt(A("pl", 0, SL), I(A("pr", 0, SL), A("pz", 0, 20)), md(SL), O.mult)
+        scan(A("ps", 0, SL), r16(SL), A("pl", 0, SL), O.mult, O.add)
+        tc(A("pi3", 0, 20), A("ps", 15, SL, 16))
+        ts(A("pi3", 20, 40), A("pi3", 0, 20), 511, O.bitwise_and)
+        ts(A("pi3", 40, 60), A("pi3", 0, 20), 9, O.arith_shift_right)
+        tc(A("own%d" % t, 0, 20), A("pi3", 20, 40))
+        tc(A("own%d" % t, 20, 40), A("pi3", 40, 60))
+        send(T["came%d" % t][:, 0:40], A("own%d" % t, 0, 40), "arl%d" % t)
+        note("arl%d" % t, width, [], [("came%d" % t, 0, 40, 1)])
+        planes(A("lc%d" % t, 0, C), A("ls%d" % t, 0, C))
+        for b in range(4):
+            act(A("db%d" % b, 0, C), A("pF%d" % b, 0, C), scale=0.5)
+        if t == 0:
+            search_constants()
+        tc(A("pri", 0, SL), A("pr", 0, SL))
+        tt(A("k1", 0, 64), A("on", 0, 64), md(64), O.mult)
+        ts(A("xri", 0, SL), A("pri", 0, SL), 511, O.bitwise_and)
+        scan(A("kl", 0, 64), r16(64), A("k1", 0, 64), O.mult, O.add)
+        ts(A("xp", 0, SL), I(A("xri", 0, SL), A("pz", 20, 40)), -192.0, O.add)
+        for c in range(VROWS, 24):
+            act(A("d0e", EB * c + 2, EB * c + EB), A("xp", 0, SL), AF.Square, bias=A("nbias", c, c + 1), scale=32.0)
+        n64, pu = lambda k: A("n64", 64 * k, 64 * k + 64), A("pu", 0, 4)
+        between = [lambda: ts(A("po", 0, 4), A("kl", 15, 64, 16), 0.5, O.is_lt, 384.0, O.mult),
+                   lambda: tt(A("po", 4, 8), A("po", 0, 4), A("ol", 15, 64, 16), O.add),
+                   lambda: tc(pu, A("po", 4, 8)),
+                   lambda: ts(n64(0), A("kai", 0, 64), 0.0, O.is_gt)]
+        for c in range(VROWS):
+            ts(A("d0e", EB * c + 2, EB * c + EB), A("xp", 0, SL), A("nm", c, c + 1), O.not_equal, 1024.0, O.mult)
+            if c < len(between):
+                between[c]()
+        for k in range(4):
+            a, e = 6 * EB * k, 6 * EB * k + 6 * EB
+            scan(A("ste", a, e), A("d0e", a, e), A("one6", 0, 6 * EB), O.min, O.add)
+        ts(A("eu", 0, 24), A("ste", EB - 1, 24 * EB, EB), -1.0, O.add)
+        for b in range(4):
+            z, win = A("za", SL * b, SL * b + SL), A("db%d" % b, 0, C + 16)
+            act(z, I(win, A("came%d" % t, 0, 20)))
+            tt(A("zt", b, 4 * SL, 4), I(win, A("came%d" % t, 20, 40)), z, O.add)
+        quant(A("qz", 0, SL), A("sz", 0, SL), A("zt", 0, 4 * SL))
+        for b in range(4):
+            mm(A("pF%d" % b, 0, SL), A("qw", 128 * b, 128 * b + 128), A("sw", 128 * b, 128 * b + 128),
+               A("qz", 0, SL), A("sz", 0, SL))
+        tc(n64(1), I(A("lrep", 0, 768), pu))
+        tt(n64(2), A("xri", 4 * M, 5 * M), n64(1), O.subtract)
+        tt(n64(3), n64(2), n64(0), O.mult)
+        tt(n64(4), n64(3), n64(1), O.add)
+        scatter(A("lrep", 0, 768), pu, n64(4))
+        if last:
+            dma("s", ext(T.ol[:, :]), (T.lrep[0:128:16, :], [("lrep", 0, 768, 1)]))
+        for b in range(4):
+            act(A("hs%d" % b, 0, SL), A("pF%d" % b, 0, SL), scale=0.03125)
+            tt(A("x%d" % (t + 1), b, 4 * C, 4), I(A("hs%d" % b, 0, SL + 8), A("eu", 0, 24)), A("fb%d" % b, 0, C), O.add)
+
+    qx, sx = A("qx%d" % R, 0, C), A("sx%d" % R, 0, C)
+    quant(qx, sx, A("x%d" % R, 0, 4 * C))
+    mm(S, A("qv", 0, 128), A("sv", 0, 128), qx, sx)
+    dma("s", ext(T.oc[:, :]), U8("qx%d" % R, 0, C))
+    for k in range(4):
+        dma("as"[k % 2], ext(T.osc[4 * k:4 * k + 4, :]), (T["sx%d" % R][32 * k:32 * k + 4, 0:C], sx[1]))
+    act(A("ys", 0, C), S)
+    dma("a", ext(T.y[:, :]), A("ys", 0, C))
+    for src in sorted(count):
+        need("p", src, count[src])
+    g.wait_ge(T.sem.lsent, R * 3 * width)
+    for t in range(R):
+        need("p", "arx%d" % t, 2 * width)
+        need("p", "arl%d" % t, width)

@@ -1,17 +1,34 @@
-from concourse.mybir import dt, AluOpType as O, ActivationFunctionType as AF
+from concourse.mybir import dt, AluOpType as O, ActivationFunctionType as AF, AxisListType as AX
 
 N, C, L, M, R = 4, 384, 5, 64, 3
-SL = L * M
-PAIRS = sorted(((i + j, i, j) for i in range(L) for j in range(L)))
-NB = len(PAIRS) + 1
-EB = SL + 2
-BIG = 1e29
+PER = 3
+NC = (M + PER - 1) // PER
+SL = 16 * NC
+W3 = 32 * PER
+TYPES = (4, 0, 1, 2, 3, 4, 2, 1, 0, 1, 0, 3, 3, 2, 0, 1)
+MEET = [(i, j) for _, i, j in sorted(((i + j, i, j) for i in range(L) for j in range(L)), reverse=True)]
+MEET = MEET[:18] + [None] + MEET[18:] + [None]
+NB = len(MEET)
+TG = 96
 UP = 1024.0
-CUT = 224
-VROWS = 10
+KB, TINY = 2.0 ** 17, 2.0 ** -40
+HUGE = 2.0 ** 80
 AROWS = (20, 19, 18)
 TILES = [(rows, max(128, 16 * min(max(rows), 24))) for rows in ([24, 23, 22, 21], [20, 19, 18, 17], [16, 15, 14, 13],
                                                               [12, 11, 10, 9], [8, 7, 6, 5], [4, 3, 2, 1])]
+
+
+def _trios():
+    runs = {tuple(TYPES[r + s * k] for k in range(3)): (r, s) for s in range(1, 8) for r in range(16 - 2 * s)}
+    out = []
+    for x in range(NB // 3):
+        at = [x + NB // 3 * k for k in range(3)]
+        fit = [(a, b) for a in runs for b in runs
+               if all(MEET[e] == (a[k], b[k]) if MEET[e] else e == NB - 1 or MEET.index((a[k], b[k])) > e
+                      for k, e in enumerate(at))]
+        out.append((runs[fit[0][0]], runs[fit[0][1]]))
+    return out
+
 
 F32, BF, I32, U16, F16, COD = "float32", "bfloat16", "int32", "uint16", "float16", "float8_e4m3fn_x4"
 SCRATCH, PLACE = {}, {}
@@ -32,30 +49,30 @@ def _pool(pool, dtype, spec):
     SCRATCH[pool] = ("sbuf", [128, at], dtype)
 
 
-_own(BF, "x0:1536 x1:1536 x2:1536 x3:1536 ut:512 vt:512 et:2048 ones:512 za:1280 zt:1280")
+_own(BF, "x0:1536 x1:1536 x2:1536 x3:1536 ut:512 vt:512 et:2048 ones:512 za:1408 zt:1408")
 _own(BF, "fb0:384 fb1:384 fb2:384 fb3:384 db0:400 db1:400 db2:400 db3:400 bd:512 bd1:512 mt:5632")
-_own(F32, "hs0:328 hs1:328 hs2:328 hs3:328 lrep:768 ys:384")
-_own(I32, "nbl:48 nbw:768")
-for _n, _k in (("w", 512), ("v", 128), ("u0", 128), ("u", 128), ("e", 512), ("z", 320), ("bd", 128), ("m", 1408)):
+_own(F32, "hs0:352 hs1:352 hs2:352 hs3:352 ys:384 lot:64")
+_own(I32, "llr:48 lrep:1824")
+for _n, _k in (("w", 512), ("v", 128), ("u0", 128), ("u", 128), ("e", 512), ("z", SL), ("bd", 128), ("m", 1408)):
     _own(COD, "q%s:%d" % (_n, _k))
     _own("uint8", "s%s:%d" % (_n, _k))
 for _t in range(R):
     _own(COD, "lc%d:384" % _t)
     _own("uint8", "ls%d:384" % _t)
-    _own(U16, "own%d:40 came%d:40" % (_t, _t))
+    _own(U16, "own%d:64 came%d:64" % (_t, _t))
 for _t in range(R + 1):
     _own(COD, "qx%d:384" % _t)
     _own("uint8", "sx%d:384" % _t)
-_pool("poolf", F32, "jm16:768 jz:768 jy:768 md:384 r16:384 da:768 db:768 mk:384 d0f:384 idr:384 b0:384 col:32 nl:24 nm:24 "
-      "nbias:24 cc:40 cd:40 ce:40 ll:48 l2:48 dl:24 la:768 lb:768 smd:384 sn:384 ssb:384 sp:768 fl:24 fx:24 ix:24 cm:24 "
-      "cl:24 v0:384 v1:384 v2:384 v3:384 vb:384 npos:24 rk2:24 cx:384 cs:384 ms:384 mi:384 ff:384 cnt:24 rk:24 order:384 "
-      "o1:64 ol:64 pm:64 qn:64 sc:128 on:64 pab:128 ht:384 htt:384 ab:128 w:320 pp:64 pe:320 pr:320 pl:320 ps:320 k1:64 "
-      "kl:64 po:8 n64:320")
-_pool("poolb", BF, "gg:768 gt:768 r16b:384 d1k:624 one6:1932 ne:624 st:624 ex:384 kr:384 tm:384 sg:1536 eqs:384 "
-      "junk:1536 xp:320 d0e:7728")
-_pool("pooli", I32, "pi:2 li:48 li2:24 li3:20 li4:24 li5:8 ca:40 cb:40 kai:64 jm:64 pi3:60 pri:320 xri:320")
-_pool("poolu", U16, "upl:8 inl:48 exr:24 exp:20 pz:40 lu:48 ixu:24 cu:24 rku:24 ou:4 eu:24 pu:4")
-_pool("poolh", F16, "ste:7728")
+SCRATCH["gt"] = ("sbuf", [128, 48, 16], BF)
+_pool("poolf", F32, "col:32 s16:192 idr:384 posi:384 posc:384 b0:384 b1:384 b2:384 b3:384 w0:384 mk:384 d0f:384 "
+      "npos:24 tagq:24 cm:96 dl:24 fl:24 cn:24 cl:24 v0:384 v1:384 v2:384 v3:384 ssb:384 sp:768 ms:384 mi:384 ff:384 "
+      "cnt:24 rk:24 rk2:24 rk3:24 cs:384 order:384 ol:96 sc:192 hf:192 hft:192 ab:192 lt:96 ltt:96 bd0:24 bd2:24 bo:24 "
+      "ix:96 iy:96 mrow:96 lo:64")
+_pool("poolb", BF, "kt:384 r16b:384 mw:400 sgn:384 sk:384 gg:768 d1k:648 ne:648 st:648 z0:384 ex:384 kr:384 sg:1536 "
+      "eqs:384 junk:1536 hb:288 hbt:288 inv:96 wv:96 val:384 tmp:384 tab:2400 one:1152")
+_pool("pooli", I32, "pi:2 li5:8 li2:24 li3:4 li4:24 ll:48 kai:96 jm:96 li:64 lj:64 bt:24 bh:24")
+_pool("poolu", U16, "upl:8 irep:26 fin:4 lu:48 cu:24 rku:24 ou:6 pu:6 bu:24 ofu:24 eu:24")
+_pool("poolh", F16, "ste:2304")
 PSUM = ("pS", "pC", "pF0", "pF1", "pF2", "pF3")
 for _n in PSUM:
     SCRATCH[_n] = ("psum", [128, 512], F32)
@@ -171,8 +188,14 @@ def rank_program(g, core, T, topo):
         else:
             emit("v", lambda: V.tensor_scalar(out[0], a[0], ap(s1), ap(s2), op0, op1), rd(a, s1, s2), out[1])
 
-    def scan(out, d0, d1, op0, op1):
-        emit("v", lambda: V.tensor_tensor_scan(out[0], d0[0], d1[0], 0.0, op0, op1), rd(d0, d1), out[1])
+    def scan(out, d0, d1, op0, op1, first=0.0):
+        emit("v", lambda: V.tensor_tensor_scan(out[0], d0[0], d1[0], first, op0, op1), rd(d0, d1), out[1])
+
+    def listed(out, rep, n):
+        scan(out, rep, A("kt", 0, n), O.add, O.mult)
+
+    def total(out, in_):
+        emit("v", lambda: V.tensor_reduce(out[0], in_[0], AX.X, O.add), rd(in_), out[1])
 
     def turn(out, in_):
         emit("v", lambda: V.transpose(out[0], in_[0]), rd(in_), out[1])
@@ -207,180 +230,172 @@ def rank_program(g, core, T, topo):
     def choose(out, in_, pattern, cmp, base, cm):
         emit("p", lambda: g.affine_select(out[0], in_[0], pattern, cmp, 0.0, base, cm), in_[1], out[1])
 
-    (kI, kM0, kMU, kL0, kL1, kL2, kU0, kU1, kU2, kOff, kCA, kCA0, kCB, kCB0, kI48, kT, knot15) = [
+    (kI, kType, kG, kB0, kB1, kB2, kB3, kOff, kSc, kBi, kBj, kP, kS, kS24, kK, kIb, kz) = [
         A("col", k, k + 1) for k in range(17)]
-    md, r16 = lambda n: A("md", 0, n), lambda n: A("r16", 0, n)
+    s16 = lambda k: A("s16", 16 * k, 16 * k + 16)
+    row5 = (T.lrep[L:128:16, 0:2 * C], [("lrep", 0, 2 * C, 1)])
 
     dma("s", A("ut", 0, 512), ext(T.u[:, :]))
     dma("a", A("x0", 0, 768), ext(T.x[:, 0:768]))
     dma("s", A("x0", 768, 1536), ext(T.x[:, 768:1536]))
-    dma("a", A("nbl", 0, 48), ext(T.nb[:, :]))
-    rows = [("nbw%d" % i, 0, 768, 1) for i in range(16)]
-    for i in range(16):
-        dma("sa"[i % 2], (T.nbw[i:128:16, :], [rows[i]]), ext(T.nb[:, :]))
-    nbw = (T.nbw[:, 0:768], rows)
+    dma("a", A("llr", 0, 48), ext(T.nb[:, :]))
+    dma("s", row5, ext(T.nb[:, :]))
     dma("s", U8("qw", 0, 512), ext(T.wc[:, :]))
     dma("s", A("sw", 0, 512), ext(T.ws[:, :]))
     dma("s", A("vt", 0, 512), ext(T.v[:, :]))
 
     iota(A("pi", 0, 1), [[1, 1]], 0, 1)
-    iota(A("li5", 0, 8), [[16, 8]], 0, 0)
-    iota(A("li2", 0, 24), [[16, 24]], 0, 0)
-    iota(A("li", 0, 48), [[1, 48]], 0, 0)
-    iota(A("jm16", 0, 768), [[0, 48], [1, 16]], 0, 0, True)
+    iota(s16(0), [[1, 16]], 0, 0, True)
     iota(A("idr", 0, C), [[1, C]], 0, 0, True)
-    iota(A("li3", 0, 20), [[1, 5], [16, 4]], 0, 0)
-    iota(A("li4", 0, 24), [[NB, 24]], NB - 1, 0)
+    iota(A("li5", 0, 8), [[16, 8]], 0, 0)
+    iota(A("s16", 32, 47), [[32, PER], [1, L]], 1, 0, True)
+    ones, half, blocks = A("ones", 0, 512), A("bd1", 0, 512), A("bd", 0, 512)
+    iota(ones, [[0, 512]], 1, 0, True)
+    for b in range(4):
+        choose(A("et", 512 * b, 512 * b + 512), ones, [[4, 128], [1, 4]], O.is_equal, -b, -4)
+    choose(half, ones, [[-16, 8], [0, 64]], O.is_ge, 0, 1)
+    choose(blocks, half, [[16, 8], [0, 64]], O.is_ge, 15, -1)
 
-    def tile_constants():
+    def later_on_g():
+        iota(A("li2", 0, 24), [[16, 24]], 15, 0)
+        iota(A("li3", 0, 4), [[W3, 2], [16, 2]], 0, 0)
+        iota(A("li4", 0, 24), [[0, 4], [-16, 6]], TG - 1, 0)
+        iota(A("posi", 0, C), [[1, 24], [48, 16]], 24, 0, True)
         for b in range(4):
             iota(A("db%d" % b, C, C + 16), [[0, 16]], 0, 0, True)
-        ones, half, blocks = A("ones", 0, 512), A("bd1", 0, 512), A("bd", 0, 512)
-        iota(ones, [[0, 512]], 1, 0, True)
-        for b in range(4):
-            choose(A("et", 512 * b, 512 * b + 512), ones, [[4, 128], [1, 4]], O.is_equal, -b, -4)
-        choose(half, ones, [[-16, 8], [0, 64]], O.is_ge, 0, 1)
-        choose(blocks, half, [[16, 8], [0, 64]], O.is_ge, 15, -1)
-        for b in range(4):
-            iota(A("hs%d" % b, SL, SL + 8), [[0, 8]], 0, 0, True)
-        iota(A("one6", 0, 6 * EB), [[0, 6 * EB]], 1, 0, True)
+        iota(A("tab", 0, 25 * TG), [[0, 25 * TG]], 512, 0, True)
+        iota(A("one", 0, 12 * TG), [[0, 12 * TG]], 1, 0, True)
 
+    fill(s16(1), 0.0)
+    for k in range(1, L):
+        rows = [r for r in range(16) if TYPES[r] == k]
+        for a, b in zip(rows[0::2], rows[1::2] + [None]):
+            fill(A("s16", 16 + a, 16 + (b or a) + 1, b - a if b else 1), float(k))
     ts(A("pi", 1, 2), A("pi", 0, 1), 15, O.bitwise_and)
-    tc(A("upl", 0, 8), A("li5", 0, 8))
+    fill(A("s16", 47, 48), 0.0)
     tc(kI, A("pi", 1, 2))
-    ts(kM0, kI, 0.0, O.is_equal)
-    ts(kCB, kI, 1.0, O.add)
-    ts(kI48, kI, 48.0, O.mult)
-    ts(kMU, kI, 0.0, O.is_equal, UP, O.mult)
-    act(A("jz", 0, C), A("jm16", 0, C), AF.Square, bias=kI, scale=-1.0)
-    act(md(C), A("jz", 0, C), AF.Relu, bias=1.0, scale=-1.0)
-    act(r16(C), A("jm16", 0, C), AF.Sign)
-    act(A("b0", 0, C), A("idr", 0, C), AF.Identity, bias=kMU, scale=kM0)
-    ts(A("inl", 0, 48), A("li", 0, 48), kI48, O.add)
-    ts(A("nl", 0, 24), A("li2", 0, 24), kI, O.add)
-    for k, (stay, up) in enumerate(((kL0, kU0), (kL1, kU1), (kL2, kU2))):
-        ts(stay, kI, k + 1.5, O.is_lt)
-        ts(up, kI, k + 1.5, O.is_lt, UP, O.mult)
-    ts(kT, kI, UP, O.mult, -4 * UP, O.add)
-    ts(kCA, kI, 16.0, O.mult, 1.0, O.add)
-    ts(kCB0, kM0, -2.0, O.mult, kCB, O.add)
-    ts(kOff, kT, 0.0, O.min, -192.0, O.add)
-    ts(kCA0, kM0, -2.0, O.mult, kCA, O.add)
+    fill(A("r16b", 0, C), 1.0)
+    ts(s16(3), s16(0), kI, O.subtract)
+    ts(A("irep", 0, 26), A("idr", 0, 26), 0.0, O.mult, kI, O.add)
+    ts(s16(4), s16(3), 0.0, O.is_equal)
+    ts(s16(5), s16(3), -1.0, O.not_equal)
+    ts(s16(6), s16(3), 15.0, O.not_equal, TINY, O.max)
+    ts(s16(7), s16(3), 0.0, O.is_equal, KB, O.mult)
+    tt(s16(8), s16(4), s16(1), O.mult)
+    tt(s16(9), s16(5), s16(6), O.min)
+    total(kType, s16(8))
+    tt(s16(10), s16(9), s16(7), O.max)
+    for k, bias in enumerate((kB0, kB1, kB2, kB3)):
+        ts(bias, kType, L - 1.5 - k, O.is_lt, UP * (k + 2), O.mult)
+    act(A("w0", 0, C), A("idr", 0, C), AF.Identity, bias=UP)
+    act(A("kt", 0, C), I(s16(10), A("irep", 0, 24)))
+    for k, bias in enumerate((kB0, kB1, kB2, kB3)):
+        act(A("b%d" % k, 0, C), A("idr", 0, C), AF.Identity, bias=bias)
+    ts(kS, kI, 0.0, O.is_equal, 1.0 / (KB * TINY), O.mult)
+    ts(kz, kI, 0.0, O.is_equal, TINY - 1.0, O.mult)
+    tc(A("upl", 0, 8), A("li5", 0, 8))
+    ts(kS, kS, 1.0 / KB, O.max)
+    ts(kOff, kType, UP, O.mult, -L * UP - 192.0, O.add)
+    fill(A("r16b", 0, C, 16), 0.0)
     quant(A("qu0", 0, 128), A("su0", 0, 128), A("ut", 0, 512))
     tc(U32("qu", 0, 128), I(U32("qu0", 0, 128), A("upl", 0, 8)))
     tc(A("su", 0, 128), I(A("su0", 0, 128), A("upl", 0, 8)))
 
     S = A("pS", 0, C)
 
-    def scores(t):
-        qx, sx = A("qx%d" % t, 0, C), A("sx%d" % t, 0, C)
-        quant(qx, sx, A("x%d" % t, 0, 4 * C))
-        mm(S, A("qu", 0, 128), A("su", 0, 128), qx, sx)
-        send(T["lc%d" % t][:, 0:C].bitcast(dt.uint8), U8("qx%d" % t, 0, C), "arx%d" % t)
-        send(T["ls%d" % t][:, 0:C], sx, "arx%d" % t)
-        note("arx%d" % t, 2 * width, [], [("lc%d" % t, 0, C, 1), ("ls%d" % t, 0, C, 1)])
-        return qx, sx
-
     def planes(codes, plane):
         for b in range(4):
             mm(A("pF%d" % b, 0, C), A("qe", 128 * b, 128 * b + 128), A("se", 128 * b, 128 * b + 128), codes, plane)
 
-    def late_constants():
-        quant(A("qe", 0, 512), A("se", 0, 512), A("et", 0, 2048))
-        tc(A("exr", 0, 24), A("li4", 0, 24))
-        tc(A("exp", 0, 20), A("li3", 0, 20))
-        f = [16 * i + j + 1 for _, i, j in PAIRS]
-        f[0] = 0
-        steps = [-f[-1]] + [f[r] - f[r - 1] for r in range(len(PAIRS) - 1, 0, -1)] + [0]
+    def meeting_constants():
+        f = [8 * m[0] + m[1] + 1.25 if m else None for m in MEET]
+        f[NB - 2] = -0.25
+        f = [f[e] if f[e] is not None or e == NB - 1 else f[e + 1] for e in range(NB)]
+        steps = [f[e] - f[e + 1] for e in range(NB - 2)] + [f[NB - 2], -100.0]
         most = max(steps, key=steps.count)
-        fill(A("d1k", 0, 24 * NB), float(most))
+        fill(A("d1k", 0, 24 * NB), most)
+        fill(A("z0", 0, C), 0.0)
         for e in range(NB):
             if steps[e] != most:
-                fill(A("d1k", e, 24 * NB, NB), float(steps[e]))
-        fill(A("ne", 0, 24 * NB, NB), 0.0)
+                fill(A("d1k", e, 24 * NB, NB), steps[e])
+
+    def count_constants():
+        act(A("mk", 0, C), I(s16(4), A("irep", 0, 24)), AF.Identity, bias=-2e29, scale=5e29)
+        act(A("d0f", 0, C), A("r16b", 0, C), AF.Identity, bias=-2e29, scale=5e29)
         quant(A("qbd", 0, 128), A("sbd", 0, 128), A("bd", 0, 512))
         fill(A("cnt", 0, 1), 0.0)
         at = 0
         for rows, w in TILES:
             fill(A("mt", at + 64 * min(rows), at + 4 * w), 0.0)
             at += 4 * w
-        ts(A("npos", 0, 24), A("li2", 0, 24), kI, O.subtract, 15.0, O.add)
-        ts(knot15, kI, 15.0, O.is_lt)
-        act(A("mk", 0, C), md(C), AF.Identity, bias=-2e29, scale=5e29)
-        act(A("d0f", 0, C), r16(C), AF.Identity, bias=-2e29, scale=5e29)
-        act(A("r16b", 0, C), r16(C))
+        ts(kK, kI, 0.0, O.not_equal, TINY, O.max)
 
-    def last_constants():
-        act(A("ce", 0, 20), A("nl", 0, 20))
-        act(A("ce", 20, 40), A("nl", 0, 20), AF.Identity, bias=float(SL - 1), scale=-1.0)
-        act(A("cd", 0, 40), A("ce", 0, 40), scale=64.0)
-        ts(A("ca", 0, 40), A("ce", 0, 40), 205.0, O.mult)
-        ts(A("cb", 0, 40), A("ca", 0, 40), 10, O.arith_shift_right)
-        ts(A("cc", 0, 40), A("cb", 0, 40), -319.0, O.mult)
-        tt(A("ce", 0, 40), A("cc", 0, 40), A("cd", 0, 40), O.add)
-        tc(A("pz", 0, 40), A("ce", 0, 40))
-        act(A("jz", 0, 768), A("jm16", 0, 768), AF.Square, bias=kI, scale=-1.0)
-        act(A("da", 0, 768), A("jz", 0, 768), AF.Sign)
-        act(A("jy", 0, 768), A("jm16", 0, 768), AF.Square, bias=kCB, scale=-1.0)
-        act(A("db", 0, 768), A("jy", 0, 768), AF.Sign)
+    def slot_constants():
+        ts(A("npos", 0, 24), A("li2", 0, 24), kI, O.subtract)
+        ts(kK, kK, KB, O.mult)
+        tt(s16(11), s16(4), s16(2), O.mult)
+        ts(kBj, kI, 512.0, O.mult, 192.0, O.add)
+        total(kG, s16(11))
+        ts(kBi, kBj, float(C), O.max)
+        ts(kSc, kI, 0.5, O.is_gt)
+        ts(kP, kI, 8.0, O.mult, -7.0, O.add)
+        ts(kS24, kS, 24.0, O.mult)
+        ts(kIb, kI, -0.12, O.add)
+        fill(A("cm", 0, W3), 0.0)
+        ts(A("fin", 0, 4), A("li3", 0, 4), kG, O.add)
+        ts(A("tagq", 0, 24), A("li4", 0, 24), kIb, O.subtract, 16.0 / TG, O.mult)
+        for u in range(PER):
+            fill(A("cm", 32 * u, 32 * u + (M - u + PER - 1) // PER), 1.0 / HUGE)
+        act(A("mw", 0, 400), I(s16(4), A("irep", 0, 25)), AF.Identity, bias=512.0, scale=-512.0)
+        act(A("posc", 0, C), A("posi", 0, C), AF.Identity, bias=0.002, scale=1.0 / 24)
 
-    def search_constants():
-        act(A("nm", 0, 24), A("nl", 0, 24), AF.Identity, bias=-192.0)
-        act(A("nbias", 0, 24), A("nl", 0, 24), AF.Identity, bias=32.0 * 192, scale=-32.0)
-        fill(A("d0e", 0, 24 * EB, EB), 0.0)
-        fill(A("d0e", 1, 24 * EB, EB), 0.0)
-        quant(A("qv", 0, 128), A("sv", 0, 128), A("vt", 0, 512))
-
+    trios = _trios()
     for t in range(R):
         last = t == R - 1
-        qx, sx = scores(t)
+        qx, sx = A("qx%d" % t, 0, C), A("sx%d" % t, 0, C)
+        quant(qx, sx, A("x%d" % t, 0, 4 * C))
+        mm(S, A("qu", 0, 128), A("su", 0, 128), qx, sx)
+        send(T["lc%d" % t][:, 0:C].bitcast(dt.uint8), U8("qx%d" % t, 0, C), "arx%d" % t)
+        send(T["ls%d" % t][:, 0:C], sx, "arx%d" % t)
+        note("arx%d" % t, 2 * width, [], [("lc%d" % t, 0, C, 1), ("ls%d" % t, 0, C, 1)])
         if t == 0:
-            tile_constants()
-        if t == 0:
-            tc(A("lrep", 0, 768), I(nbw, A("inl", 0, 48)))
-            tc(A("ll", 0, 48), A("nbl", 0, 48))
+            later_on_g()
         else:
-            scan(A("la", 0, 768), A("da", 0, 768), A("lrep", 0, 768), O.mult, O.add)
-            scan(A("lb", 0, 768), A("db", 0, 768), A("lrep", 0, 768), O.mult, O.add)
-            ts(A("l2", 0, 48), A("lb", 15, 768, 16), knot15, O.mult)
-            tt(A("ll", 0, 48), A("la", 15, 768, 16), A("l2", 0, 48), O.subtract)
-        tt(A("smd", 0, C), S, md(C), O.mult)
+            planes(qx, sx)
+        act(A("sgn", 0, C), S, AF.Sign)
+        ts(A("ll", 0, 48), A("llr", 0, 48), 511, O.bitwise_and)
         act(A("ssb", 0, C), S)
         tt(A("dl", 0, 24), A("ll", 24, 48), A("ll", 0, 24), O.subtract)
-        scan(A("sn", 0, C), r16(C), A("smd", 0, C), O.mult, O.add)
-        sl = A("sn", 15, C, 16)
-        ts(A("fx", 0, 24), sl, 0.0, O.is_gt, 384.0, O.mult)
-        ts(A("fl", 0, 24), sl, 0.0, O.is_gt)
-        tt(A("ix", 0, 24), A("fx", 0, 24), A("nl", 0, 24), O.add)
-        tt(A("cm", 0, 24), A("fl", 0, 24), A("dl", 0, 24), O.mult)
-        tc(A("ixu", 0, 24), A("ix", 0, 24))
-        tt(A("cl", 0, 24), A("cm", 0, 24), A("ll", 0, 24), O.add)
-        tt(A("v0", 0, C), I(A("lrep", 0, 768), A("ixu", 0, 24)), A("b0", 0, C), O.max)
-        tc(A("cu", 0, 24), A("cl", 0, 24))
         tc(A("lu", 0, 48), A("ll", 0, 48))
-        for k, (stay, up) in enumerate(((kL0, kU0), (kL1, kU1), (kL2, kU2))):
-            act(A("vb", 0, CUT), A("v%d" % k, 0, CUT), AF.Identity, bias=up, scale=stay)
-            ts(A("vb", CUT, C), A("v%d" % k, CUT, C), stay, O.mult, up, O.add)
-            tt(A("v%d" % (k + 1), 0, C), I(A("v%d" % k, 0, C), A("cu", 0, 24)), A("vb", 0, C), O.max)
+        listed(A("sk", 0, C), A("sgn", 0, C), C)
+        ts(A("fl", 0, 24), A("sk", 15, C, 16), kS, O.mult, 0.5, O.is_gt)
+        tt(A("cn", 0, 24), A("fl", 0, 24), A("dl", 0, 24), O.mult)
+        tt(A("cl", 0, 24), A("cn", 0, 24), A("ll", 0, 24), O.add)
+        tc(A("cu", 0, 24), A("cl", 0, 24))
+        act(A("sp", 0, 768), I(A("ssb", 0, C), A("lu", 0, 48)))
+        for k in range(4):
+            tt(A("v%d" % k, 0, C), I(A("v%d" % (k - 1) if k else "w0", 0, C), A("cu", 0, 24)), A("b%d" % k, 0, C), O.max)
+        if t:
+            act(A("fb0", 0, C), A("pF0", 0, C))
         act(A("gg", 0, C), I(A("v3", 0, C), A("lu", 0, 24)), AF.Identity, bias=kOff)
         ts(A("gg", C, 2 * C), I(A("v3", 0, C), A("lu", 24, 48)), kOff, O.add)
         if t == 0:
-            late_constants()
-        planes(qx, sx)
-        turn(A("gt", C, 2 * C), A("gg", C, 2 * C))
-        turn(A("gt", 0, C), A("gg", 0, C))
-        act(A("sp", 0, 768), I(A("ssb", 0, C), A("lu", 0, 48)))
-        for b in range(4):
+            quant(A("qe", 0, 512), A("se", 0, 512), A("et", 0, 2048))
+            planes(qx, sx)
+            meeting_constants()
+            count_constants()
+        turn((T.gt[:, 24:48, :], [("gt", C, 2 * C, 1)]), A("gg", C, 2 * C))
+        turn((T.gt[:, 0:24, :], [("gt", 0, C, 1)]), A("gg", 0, C))
+        for b in range(1 if t else 0, 4):
             act(A("fb%d" % b, 0, C), A("pF%d" % b, 0, C))
-        p = lambda i: A("gt", i, C, 16)
-        q = lambda j: A("gt", C + j, 2 * C, 16)
-        for r in range(len(PAIRS)):
-            tt(A("ne", 25 - r, 24 * NB, NB), p(PAIRS[r][1]), q(PAIRS[r][2]), O.not_equal)
-        scan(A("st", 0, 24 * NB), A("ne", 0, 24 * NB), A("d1k", 0, 24 * NB), O.mult, O.add)
-        tc(A("ex", 0, C), I(A("st", 0, 24 * NB), A("exr", 0, 24)))
+        for x, ((r, s), (r2, s2)) in enumerate(trios):
+            tt(A("ne", x, 24 * NB, NB // 3), (T.gt[:, 0:24, r:r + 2 * s + 1:s], [("gt", 0, C, 1)]),
+               (T.gt[:, 24:48, r2:r2 + 2 * s2 + 1:s2], [("gt", C, 2 * C, 1)]), O.not_equal)
+        scan(A("st", 0, 24 * NB), A("ne", 0, 24 * NB), A("d1k", 0, 24 * NB), O.mult, O.add, -100.0)
+        ts(A("z0", 0, C, 16), A("st", NB - 2, 24 * NB, NB), -0.25, O.max, HUGE, O.mult)
+        scan(A("ex", 0, C), A("r16b", 0, C), A("z0", 0, C), O.mult, O.add)
         turn(A("kr", 0, C), A("ex", 0, C))
-        ts(A("tm", 0, C), A("kr", 0, C), 0.0, O.is_equal, -BIG, O.mult)
-        tt(A("ms", 0, C), S, A("tm", 0, C), O.add)
+        tt(A("ms", 0, C), S, A("kr", 0, C), O.min)
         tt(A("mi", 0, C), A("ms", 0, C), A("mk", 0, C), O.min)
         scan(A("ff", 0, C), A("d0f", 0, C), A("mi", 0, C), O.min, O.max)
         spot, at = {}, 0
@@ -407,96 +422,96 @@ def rank_program(g, core, T, topo):
             mm(A("pC", 0, w), A("qbd", 0, 128), A("sbd", 0, 128), A("qm", a, a + w), A("sm", a, a + w), k == 0, k == 5)
             at += 4 * w
         if t == 0:
-            last_constants()
-        tt(A("rk", 0, 24), A("npos", 0, 24), A("eqs", 15, C, 16), O.subtract)
-        tt(A("cx", 0, C), A("pC", 0, C), md(C), O.mult)
-        tt(A("rk2", 0, 24), A("rk", 0, 24), A("cnt", 0, 24), O.subtract)
-        scan(A("cs", 0, C), r16(C), A("cx", 0, C), O.mult, O.add)
-        tt(A("rk", 0, 24), A("rk2", 0, 24), A("cs", 15, C, 16), O.add)
-        tc(A("rku", 0, 24), A("rk", 0, 24))
-        scatter(A("order", 0, C), A("rku", 0, 24), A("idr", 0, C))
-        tt(A("o1", 0, 64), A("order", 0, 64), md(64), O.mult)
-        scan(A("ol", 0, 64), r16(64), A("o1", 0, 64), O.mult, O.add)
-        tc(A("ou", 0, 4), A("ol", 15, 64, 16))
-        ou = A("ou", 0, 4)
-        for h in range(2):
-            act(A("sc", 64 * h, 64 * h + 64), I(A("sp", C * h, C * h + C), ou))
-        tc(A("kai", 0, 64), I(A("kr", 0, C), ou))
-        ts(A("pm", 0, 64), I(A("gg", 0, C), ou), 192.0, O.add)
-        ts(A("qn", 0, 64), I(A("gg", C, 2 * C), ou), 192.0, O.add)
-        ts(A("jm", 0, 64), A("kai", 0, 64), 15, O.bitwise_and)
-        tt(A("on", 0, 64), A("sc", 64, 128), A("sc", 0, 64), O.is_gt)
-        act(A("ht", 256, 320), A("on", 0, 64), scale=-511.0)
-        ts(A("ht", 0, 64), A("kai", 0, 64), kCA0, O.is_lt)
-        ts(A("pab", 0, 64), A("kai", 0, 64), kCA, O.is_ge)
-        ts(A("ht", 64, 128), A("jm", 0, 64), kCB0, O.is_lt)
-        ts(A("pab", 64, 128), A("jm", 0, 64), kCB, O.is_ge)
-        ts(A("ht", 320, 384), A("kai", 0, 64), 0.0, O.is_equal, float(C * 513), O.mult)
-        tt(A("ht", 128, 192), A("pab", 0, 64), A("pm", 0, 64), O.mult)
-        tt(A("ht", 192, 256), A("pab", 64, 128), A("qn", 0, 64), O.mult)
-        turn(A("htt", 0, 384), A("ht", 0, 384))
-        scan(A("ab", 0, 128), A("htt", 0, 128), A("htt", 128, 256), O.mult, O.add)
-        W = lambda k: A("w", 64 * k, 64 * k + 64)
-        tt(W(0), A("ab", 64, 128), A("ab", 0, 64), O.subtract)
-        ts(W(1), A("ab", 64, 128), 512.0, O.mult)
-        tt(W(2), A("ab", 0, 64), A("htt", 320, 384), O.add)
-        tt(W(3), W(0), A("htt", 256, 320), O.mult)
-        tt(W(4), W(1), W(2), O.add)
-        tt(A("pp", 0, 64), W(4), W(3), O.add)
-        tc(A("pe", 0, SL), I(A("pp", 0, 64), A("exp", 0, 20)))
-        turn(A("pr", 0, SL), A("pe", 0, SL))
-        tt(A("pl", 0, SL), I(A("pr", 0, SL), A("pz", 0, 20)), md(SL), O.mult)
-        scan(A("ps", 0, SL), r16(SL), A("pl", 0, SL), O.mult, O.add)
-        tc(A("pi3", 0, 20), A("ps", 15, SL, 16))
-        ts(A("pi3", 20, 40), A("pi3", 0, 20), 511, O.bitwise_and)
-        ts(A("pi3", 40, 60), A("pi3", 0, 20), 9, O.arith_shift_right)
-        tc(A("own%d" % t, 0, 20), A("pi3", 20, 40))
-        tc(A("own%d" % t, 20, 40), A("pi3", 40, 60))
-        send(T["came%d" % t][:, 0:40], A("own%d" % t, 0, 40), "arl%d" % t)
-        note("arl%d" % t, width, [], [("came%d" % t, 0, 40, 1)])
+            slot_constants()
         planes(A("lc%d" % t, 0, C), A("ls%d" % t, 0, C))
+        tt(A("rk", 0, 24), A("npos", 0, 24), A("eqs", 15, C, 16), O.subtract)
+        listed(A("cs", 0, C), A("pC", 0, C), C)
+        tt(A("rk2", 0, 24), A("rk", 0, 24), A("cnt", 0, 24), O.subtract)
         for b in range(4):
             act(A("db%d" % b, 0, C), A("pF%d" % b, 0, C), scale=0.5)
+        ts(A("rk3", 0, 24), A("rk2", 0, 24), kK, O.mult)
+        tt(A("rk", 0, 24), A("rk3", 0, 24), A("cs", 15, C, 16), O.add)
+        ts(A("rku", 0, 24), A("rk", 0, 24), kS, O.mult)
+        scatter(A("order", 0, C), A("rku", 0, 24), A("idr", 0, C))
+        for u in range(PER):
+            listed(A("ol", 32 * u, 32 * u + 32), A("order", u, W3, PER), 32)
+        ou = A("ou", 0, 6)
+        ts(ou, A("ol", 15, W3, 16), kS, O.mult)
+        for h in range(2):
+            act(A("sc", W3 * h, W3 * h + W3), I(A("sp", C * h, C * h + C), ou))
+        for h in range(2):
+            act(A("hf", W3 * h, W3 * h + W3), I(A("gg", C * h, C * h + C), ou), AF.Identity, bias=kBi, scale=kSc)
+        kai, on = A("kai", 0, W3), A("hb", 2 * W3, 3 * W3)
+        tt(kai, I(A("kr", 0, C), ou), A("cm", 0, W3), O.mult)
+        ts(A("jm", 0, W3), kai, 7, O.bitwise_and)
+        ts(A("hb", 0, W3), kai, kP, O.is_ge, 8192.0, O.mult)
+        ts(A("inv", 0, W3), kai, 0.0, O.is_equal, 43.0, O.mult)
+        ts(A("hb", W3, 2 * W3), A("jm", 0, W3), kI, O.is_ge, 8192.0, O.mult)
+        tt(on, A("sc", W3, 2 * W3), A("sc", 0, W3), O.is_gt)
+        turn(A("hbt", 0, 3 * W3), A("hb", 0, 3 * W3))
+        turn(A("hft", 0, 2 * W3), A("hf", 0, 2 * W3))
+        tt(A("wv", 0, W3), A("inv", 0, W3), on, O.subtract)
+        scan(A("ab", 0, 2 * W3), A("hbt", 0, 2 * W3), A("hft", 0, 2 * W3), O.max, O.min)
+        tc(A("lt", 64, 96), I(A("hbt", 2 * W3, 3 * W3), A("fin", 0, 2)))
+        tc(A("lt", 0, 64), I(A("ab", 0, 2 * W3), A("fin", 0, 4)))
+        turn(A("ltt", 0, 96), A("lt", 0, 96))
+        tc(A("li", 0, 64), A("ltt", 0, 64))
+        ts(A("lj", 0, 64), A("li", 0, 64), 511, O.bitwise_and)
+        tc(A("own%d" % t, 0, 64), A("lj", 0, 64))
+        send(T["came%d" % t][:, 0:32 + NC], A("own%d" % t, 0, 32 + NC), "arl%d" % t)
+        note("arl%d" % t, width, [], [("came%d" % t, 0, 64, 1)])
+        tt(A("bd0", 0, NC), A("lj", 32, 32 + NC), A("lj", 0, NC), O.subtract)
+        tt(A("ix", 0, W3), I(A("posc", 0, C), ou), A("wv", 0, W3), O.add)
+        tt(A("bd2", 0, NC), A("bd0", 0, NC), A("ltt", 64, 64 + NC), O.mult)
+        listed(A("iy", 0, W3), A("ix", 0, W3), W3)
+        tt(A("bt", 0, NC), A("bd2", 0, NC), A("lj", 0, NC), O.add)
+        ts(A("pu", 0, 6), A("iy", 15, W3, 16), kS24, O.mult)
+        tc(A("bu", 0, NC), A("bt", 0, NC))
+        ts(A("bh", 0, NC), A("bt", 0, NC), 496, O.bitwise_and)
+        parts = [(a, min(a + TG // 16, NC)) for a in range(0, NC, TG // 16)]
+        for a, e in parts:
+            act(A("val", 16 * a, 16 * e), I(A("mw", 0, 400), A("bu", a, e)), AF.Identity, bias=16.0 * a - UP * t)
+        turn(A("mrow", 0, W3), A("ab", 0, W3))
+        tt(A("bo", 0, NC), A("bh", 0, NC), A("tagq", 0, NC), O.add)
         if t == 0:
-            search_constants()
-        tc(A("pri", 0, SL), A("pr", 0, SL))
-        tt(A("k1", 0, 64), A("on", 0, 64), md(64), O.mult)
-        ts(A("xri", 0, SL), A("pri", 0, SL), 511, O.bitwise_and)
-        scan(A("kl", 0, 64), r16(64), A("k1", 0, 64), O.mult, O.add)
-        ts(A("xp", 0, SL), I(A("xri", 0, SL), A("pz", 20, 40)), -192.0, O.add)
-        for c in range(VROWS, 24):
-            act(A("d0e", EB * c + 2, EB * c + EB), A("xp", 0, SL), AF.Square, bias=A("nbias", c, c + 1), scale=32.0)
-        n64, pu = lambda k: A("n64", 64 * k, 64 * k + 64), A("pu", 0, 4)
-        between = [lambda: ts(A("po", 0, 4), A("kl", 15, 64, 16), 0.5, O.is_lt, 384.0, O.mult),
-                   lambda: tt(A("po", 4, 8), A("po", 0, 4), A("ol", 15, 64, 16), O.add),
-                   lambda: tc(pu, A("po", 4, 8)),
-                   lambda: ts(n64(0), A("kai", 0, 64), 0.0, O.is_gt)]
-        for c in range(VROWS):
-            ts(A("d0e", EB * c + 2, EB * c + EB), A("xp", 0, SL), A("nm", c, c + 1), O.not_equal, 1024.0, O.mult)
-            if c < len(between):
-                between[c]()
-        for k in range(4):
-            a, e = 6 * EB * k, 6 * EB * k + 6 * EB
-            scan(A("ste", a, e), A("d0e", a, e), A("one6", 0, 6 * EB), O.min, O.add)
-        ts(A("eu", 0, 24), A("ste", EB - 1, 24 * EB, EB), -1.0, O.add)
+            fill(A("one", 0, 12 * TG, TG), 4096.0)
+            quant(A("qv", 0, 128), A("sv", 0, 128), A("vt", 0, 512))
+        ts(A("ofu", 0, NC), A("bo", 0, NC), TG / 16.0, O.mult)
+        scatter(A("lrep", 0, 1800), A("pu", 0, 6), A("mrow", 0, W3))
+        dma("s", A("llr", 0, 48), row5)
+        tab = A("tab", 0, 25 * TG)
+        for a, e in parts:
+            val = A("val", 16 * a, 16 * e)
+            if a:
+                tt(A("tmp", 16 * a, 16 * e), I(tab, A("ofu", a, e)), val, O.min)
+                val = A("tmp", 16 * a, 16 * e)
+            scatter(tab, A("ofu", a, e), val)
+        for k in range(2):
+            a, e = 12 * TG * k, 12 * TG * (k + 1)
+            scan(A("ste", a, e), A("one", 0, 12 * TG), A("tab", a, e), O.add, O.min)
+        ts(A("eu", 0, 24), A("ste", TG - 1, 24 * TG, TG), UP * t, O.add, SL - 1.0, O.min)
         for b in range(4):
             z, win = A("za", SL * b, SL * b + SL), A("db%d" % b, 0, C + 16)
-            act(z, I(win, A("came%d" % t, 0, 20)))
-            tt(A("zt", b, 4 * SL, 4), I(win, A("came%d" % t, 20, 40)), z, O.add)
+            act(z, I(win, A("came%d" % t, 0, NC)))
+            tt(A("zt", b, 4 * SL, 4), I(win, A("came%d" % t, 32, 32 + NC)), z, O.add)
         quant(A("qz", 0, SL), A("sz", 0, SL), A("zt", 0, 4 * SL))
         for b in range(4):
             mm(A("pF%d" % b, 0, SL), A("qw", 128 * b, 128 * b + 128), A("sw", 128 * b, 128 * b + 128),
                A("qz", 0, SL), A("sz", 0, SL))
-        tc(n64(1), I(A("lrep", 0, 768), pu))
-        tt(n64(2), A("xri", 4 * M, 5 * M), n64(1), O.subtract)
-        tt(n64(3), n64(2), n64(0), O.mult)
-        tt(n64(4), n64(3), n64(1), O.add)
-        scatter(A("lrep", 0, 768), pu, n64(4))
         if last:
-            dma("s", ext(T.ol[:, :]), (T.lrep[0:128:16, :], [("lrep", 0, 768, 1)]))
+            ts(A("ll", 0, 48), A("llr", 0, 48), 511, O.bitwise_and)
+            fill(A("lo", 48, 64), 0.0)
+            tc(A("lo", 0, 48), A("ll", 0, 48))
+            turn(A("lot", 0, 64), A("lo", 0, 64))
+            for h in range(2):
+                dma("s", ext(T.ol[h:8:2, 0:512]), A("lot", 16 * h, 16 * h + 16))
+            for a in range(4):
+                for h in range(2):
+                    dma("s", ext(T.ol[2 * a + h:2 * a + h + 1, 512:768]),
+                        (T.lot[32 * a:32 * a + 16, 32 + 16 * h:48 + 16 * h], [("lot", 32, 64, 1)]))
         for b in range(4):
             act(A("hs%d" % b, 0, SL), A("pF%d" % b, 0, SL), scale=0.03125)
-            tt(A("x%d" % (t + 1), b, 4 * C, 4), I(A("hs%d" % b, 0, SL + 8), A("eu", 0, 24)), A("fb%d" % b, 0, C), O.add)
+            tt(A("x%d" % (t + 1), b, 4 * C, 4), I(A("hs%d" % b, 0, SL), A("eu", 0, 24)), A("fb%d" % b, 0, C), O.add)
 
     qx, sx = A("qx%d" % R, 0, C), A("sx%d" % R, 0, C)
     quant(qx, sx, A("x%d" % R, 0, 4 * C))

@@ -65,12 +65,12 @@ for _t in range(R + 1):
     _own("uint8", "sx%d:384" % _t)
 SCRATCH["gt"] = ("sbuf", [128, 48, 16], BF)
 _pool("poolf", F32, "col:32 s16:192 idr:384 posi:384 posc:384 b0:384 b1:384 b2:384 b3:384 w0:384 mk:384 d0f:384 "
-      "npos:24 tagq:24 cm:96 dl:24 fl:24 cn:24 cl:24 v0:384 v1:384 v2:384 v3:384 ssb:384 sp:768 ms:384 mi:384 ff:384 "
+      "npos:24 tagq:24 cm:96 f0:48 f1:48 f2:48 li2:24 li4:24 v0:384 v1:384 v2:384 v3:384 ssb:384 sp:768 ms:384 mi:384 ff:384 "
       "cnt:24 rk:24 rk2:24 rk3:24 cs:384 order:384 ol:96 sc:192 hf:192 hft:192 ab:192 lt:96 ltt:96 bd0:24 bd2:24 bo:24 "
       "ix:96 iy:96 mrow:96 lo:64")
 _pool("poolb", BF, "kt:384 r16b:384 mw:400 sgn:384 sk:384 gg:768 d1k:648 ne:648 st:648 z0:384 ex:384 kr:384 sg:1536 "
       "eqs:384 junk:1536 hb:288 hbt:288 inv:96 wv:96 val:384 tmp:384 tab:2400 one:1152")
-_pool("pooli", I32, "pi:2 li5:8 li2:24 li3:4 li4:24 ll:48 kai:96 jm:96 li:64 lj:64 bt:24 bh:24")
+_pool("pooli", I32, "pi:2 li5:8 li3:4 ll:48 kai:96 jm:96 li:64 lj:64 bt:24 bh:24")
 _pool("poolu", U16, "upl:8 irep:26 fin:4 lu:48 cu:24 rku:24 ou:6 pu:6 bu:24 ofu:24 eu:24")
 _pool("poolh", F16, "ste:2304")
 PSUM = ("pS", "pC", "pF0", "pF1", "pF2", "pF3")
@@ -249,22 +249,24 @@ def rank_program(g, core, T, topo):
     iota(A("idr", 0, C), [[1, C]], 0, 0, True)
     iota(A("li5", 0, 8), [[16, 8]], 0, 0)
     iota(A("s16", 32, 47), [[32, PER], [1, L]], 1, 0, True)
+    iota(A("li3", 0, 4), [[W3, 2], [16, 2]], 0, 0)
     ones, half, blocks = A("ones", 0, 512), A("bd1", 0, 512), A("bd", 0, 512)
     iota(ones, [[0, 512]], 1, 0, True)
-    for b in range(4):
-        choose(A("et", 512 * b, 512 * b + 512), ones, [[4, 128], [1, 4]], O.is_equal, -b, -4)
-    choose(half, ones, [[-16, 8], [0, 64]], O.is_ge, 0, 1)
-    choose(blocks, half, [[16, 8], [0, 64]], O.is_ge, 15, -1)
 
     def later_on_g():
-        iota(A("li2", 0, 24), [[16, 24]], 15, 0)
-        iota(A("li3", 0, 4), [[W3, 2], [16, 2]], 0, 0)
-        iota(A("li4", 0, 24), [[0, 4], [-16, 6]], TG - 1, 0)
+        choose(half, ones, [[-16, 8], [0, 64]], O.is_ge, 0, 1)
+        choose(blocks, half, [[16, 8], [0, 64]], O.is_ge, 15, -1)
+        iota(A("li2", 0, 24), [[16, 24]], 15, 0, True)
+        iota(A("li4", 0, 24), [[0, 4], [-16, 6]], TG - 1, 0, True)
+        for b in range(4):
+            choose(A("et", 512 * b, 512 * b + 512), ones, [[4, 128], [1, 4]], O.is_equal, -b, -4)
         iota(A("posi", 0, C), [[1, 24], [48, 16]], 24, 0, True)
         for b in range(4):
             iota(A("db%d" % b, C, C + 16), [[0, 16]], 0, 0, True)
         iota(A("tab", 0, 25 * TG), [[0, 25 * TG]], 512, 0, True)
-        iota(A("one", 0, 12 * TG), [[0, 12 * TG]], 1, 0, True)
+
+    def put(out, n, k):
+        act(out, A("idr", 0, n), AF.Identity, bias=k, scale=0.0)
 
     fill(s16(1), 0.0)
     for k in range(1, L):
@@ -292,7 +294,7 @@ def rank_program(g, core, T, topo):
     for k, bias in enumerate((kB0, kB1, kB2, kB3)):
         act(A("b%d" % k, 0, C), A("idr", 0, C), AF.Identity, bias=bias)
     ts(kS, kI, 0.0, O.is_equal, 1.0 / (KB * TINY), O.mult)
-    ts(kz, kI, 0.0, O.is_equal, TINY - 1.0, O.mult)
+    put(A("f0", 0, 48, 2), 24, 0.0)
     tc(A("upl", 0, 8), A("li5", 0, 8))
     ts(kS, kS, 1.0 / KB, O.max)
     ts(kOff, kType, UP, O.mult, -L * UP - 192.0, O.add)
@@ -312,42 +314,44 @@ def rank_program(g, core, T, topo):
         f[NB - 2] = -0.25
         f = [f[e] if f[e] is not None or e == NB - 1 else f[e + 1] for e in range(NB)]
         steps = [f[e] - f[e + 1] for e in range(NB - 2)] + [f[NB - 2], -100.0]
-        most = max(steps, key=steps.count)
-        fill(A("d1k", 0, 24 * NB), most)
-        fill(A("z0", 0, C), 0.0)
         for e in range(NB):
-            if steps[e] != most:
-                fill(A("d1k", e, 24 * NB, NB), steps[e])
+            if steps[e] != 7.0:
+                put(A("d1k", e, 24 * NB, NB), 24, steps[e])
 
     def count_constants():
         act(A("mk", 0, C), I(s16(4), A("irep", 0, 24)), AF.Identity, bias=-2e29, scale=5e29)
         act(A("d0f", 0, C), A("r16b", 0, C), AF.Identity, bias=-2e29, scale=5e29)
-        quant(A("qbd", 0, 128), A("sbd", 0, 128), A("bd", 0, 512))
-        fill(A("cnt", 0, 1), 0.0)
+        put(A("cnt", 0, 1), 1, 0.0)
         at = 0
         for rows, w in TILES:
-            fill(A("mt", at + 64 * min(rows), at + 4 * w), 0.0)
+            for a in range(at + 64 * min(rows), at + 4 * w, 256):
+                e = min(a + 256, at + 4 * w)
+                put(A("mt", a, e), e - a, 0.0)
             at += 4 * w
-        ts(kK, kI, 0.0, O.not_equal, TINY, O.max)
+
+    def rank_constants():
+        act(kSc, kI, AF.Sign)
+        act(kz, kI, scale=-1.0)
+        act(kK, kSc, AF.Identity, bias=KB * TINY, scale=KB)
+        act(A("npos", 0, 24), A("li2", 0, 24), AF.Identity, bias=kz)
 
     def slot_constants():
-        ts(A("npos", 0, 24), A("li2", 0, 24), kI, O.subtract)
-        ts(kK, kK, KB, O.mult)
-        tt(s16(11), s16(4), s16(2), O.mult)
-        ts(kBj, kI, 512.0, O.mult, 192.0, O.add)
-        total(kG, s16(11))
-        ts(kBi, kBj, float(C), O.max)
-        ts(kSc, kI, 0.5, O.is_gt)
-        ts(kP, kI, 8.0, O.mult, -7.0, O.add)
-        ts(kS24, kS, 24.0, O.mult)
-        ts(kIb, kI, -0.12, O.add)
-        fill(A("cm", 0, W3), 0.0)
-        ts(A("fin", 0, 4), A("li3", 0, 4), kG, O.add)
-        ts(A("tagq", 0, 24), A("li4", 0, 24), kIb, O.subtract, 16.0 / TG, O.mult)
+        act(kBj, kI, AF.Relu, bias=-192.0, scale=512.0)
+        act(kP, kI, AF.Identity, bias=-7.0, scale=8.0)
+        act(kS24, kS, scale=24.0)
+        act(kIb, kI, AF.Identity, bias=0.02, scale=-16.0 / TG)
+        put(A("cm", 0, W3), W3, 0.0)
+        act(kBi, kBj, AF.Identity, bias=float(C))
+        act(A("tagq", 0, 24), A("li4", 0, 24), AF.Identity, bias=kIb, scale=16.0 / TG)
         for u in range(PER):
-            fill(A("cm", 32 * u, 32 * u + (M - u + PER - 1) // PER), 1.0 / HUGE)
-        act(A("mw", 0, 400), I(s16(4), A("irep", 0, 25)), AF.Identity, bias=512.0, scale=-512.0)
+            n = (M - u + PER - 1) // PER
+            put(A("cm", 32 * u, 32 * u + n), n, 1.0 / HUGE)
         act(A("posc", 0, C), A("posi", 0, C), AF.Identity, bias=0.002, scale=1.0 / 24)
+
+    def search_constants():
+        for k in range(3):
+            put(A("one", C * k, C * k + C), C, 1.0)
+        put(A("one", 0, 12 * TG, TG), 12, 4096.0)
 
     trios = _trios()
     for t in range(R):
@@ -365,28 +369,36 @@ def rank_program(g, core, T, topo):
         act(A("sgn", 0, C), S, AF.Sign)
         ts(A("ll", 0, 48), A("llr", 0, 48), 511, O.bitwise_and)
         act(A("ssb", 0, C), S)
-        tt(A("dl", 0, 24), A("ll", 24, 48), A("ll", 0, 24), O.subtract)
+        tt(A("f0", 1, 48, 2), A("ll", 24, 48), A("ll", 0, 24), O.subtract)
+        tc(A("f1", 1, 48, 2), A("ll", 0, 24))
         tc(A("lu", 0, 48), A("ll", 0, 48))
+        if t == 0:
+            tt(s16(11), s16(4), s16(2), O.mult)
+            fill(A("d1k", 0, 24 * NB), 7.0)
+            total(kG, s16(11))
         listed(A("sk", 0, C), A("sgn", 0, C), C)
-        ts(A("fl", 0, 24), A("sk", 15, C, 16), kS, O.mult, 0.5, O.is_gt)
-        tt(A("cn", 0, 24), A("fl", 0, 24), A("dl", 0, 24), O.mult)
-        tt(A("cl", 0, 24), A("cn", 0, 24), A("ll", 0, 24), O.add)
-        tc(A("cu", 0, 24), A("cl", 0, 24))
-        act(A("sp", 0, 768), I(A("ssb", 0, C), A("lu", 0, 48)))
+        ts(A("f1", 0, 48, 2), A("sk", 15, C, 16), kS, O.mult, 0.5, O.is_gt)
+        scan(A("f2", 0, 48), A("f0", 0, 48), A("f1", 0, 48), O.mult, O.add)
+        tc(A("cu", 0, 24), A("f2", 1, 48, 2))
+        if t == 0:
+            meeting_constants()
+        else:
+            act(A("sp", 0, 768), I(A("ssb", 0, C), A("lu", 0, 48)))
         for k in range(4):
             tt(A("v%d" % k, 0, C), I(A("v%d" % (k - 1) if k else "w0", 0, C), A("cu", 0, 24)), A("b%d" % k, 0, C), O.max)
         if t:
             act(A("fb0", 0, C), A("pF0", 0, C))
+        else:
+            put(A("z0", 0, C), C, 0.0)
+            act(A("sp", 0, 768), I(A("ssb", 0, C), A("lu", 0, 48)))
         act(A("gg", 0, C), I(A("v3", 0, C), A("lu", 0, 24)), AF.Identity, bias=kOff)
         ts(A("gg", C, 2 * C), I(A("v3", 0, C), A("lu", 24, 48)), kOff, O.add)
         if t == 0:
-            quant(A("qe", 0, 512), A("se", 0, 512), A("et", 0, 2048))
-            planes(qx, sx)
-            meeting_constants()
             count_constants()
+            rank_constants()
         turn((T.gt[:, 24:48, :], [("gt", C, 2 * C, 1)]), A("gg", C, 2 * C))
         turn((T.gt[:, 0:24, :], [("gt", 0, C, 1)]), A("gg", 0, C))
-        for b in range(1 if t else 0, 4):
+        for b in range(1, 4 if t else 0):
             act(A("fb%d" % b, 0, C), A("pF%d" % b, 0, C))
         for x, ((r, s), (r2, s2)) in enumerate(trios):
             tt(A("ne", x, 24 * NB, NB // 3), (T.gt[:, 0:24, r:r + 2 * s + 1:s], [("gt", 0, C, 1)]),
@@ -398,6 +410,8 @@ def rank_program(g, core, T, topo):
         tt(A("ms", 0, C), S, A("kr", 0, C), O.min)
         tt(A("mi", 0, C), A("ms", 0, C), A("mk", 0, C), O.min)
         scan(A("ff", 0, C), A("d0f", 0, C), A("mi", 0, C), O.min, O.max)
+        if t == 0:
+            quant(A("qbd", 0, 128), A("sbd", 0, 128), A("bd", 0, 512))
         spot, at = {}, 0
         for rows, w in TILES:
             for i, c in enumerate(rows):
@@ -421,18 +435,23 @@ def rank_program(g, core, T, topo):
             quant(A("qm", a, a + w), A("sm", a, a + w), A("mt", at, at + 4 * w))
             mm(A("pC", 0, w), A("qbd", 0, 128), A("sbd", 0, 128), A("qm", a, a + w), A("sm", a, a + w), k == 0, k == 5)
             at += 4 * w
+            if k == 4:
+                tt(A("rk", 0, 24), A("npos", 0, 24), A("eqs", 15, C, 16), O.subtract)
         if t == 0:
+            quant(A("qe", 0, 512), A("se", 0, 512), A("et", 0, 2048))
+            planes(qx, sx)
             slot_constants()
-        planes(A("lc%d" % t, 0, C), A("ls%d" % t, 0, C))
-        tt(A("rk", 0, 24), A("npos", 0, 24), A("eqs", 15, C, 16), O.subtract)
-        listed(A("cs", 0, C), A("pC", 0, C), C)
+            for b in range(4):
+                act(A("fb%d" % b, 0, C), A("pF%d" % b, 0, C))
         tt(A("rk2", 0, 24), A("rk", 0, 24), A("cnt", 0, 24), O.subtract)
-        for b in range(4):
-            act(A("db%d" % b, 0, C), A("pF%d" % b, 0, C), scale=0.5)
+        listed(A("cs", 0, C), A("pC", 0, C), C)
         ts(A("rk3", 0, 24), A("rk2", 0, 24), kK, O.mult)
         tt(A("rk", 0, 24), A("rk3", 0, 24), A("cs", 15, C, 16), O.add)
         ts(A("rku", 0, 24), A("rk", 0, 24), kS, O.mult)
         scatter(A("order", 0, C), A("rku", 0, 24), A("idr", 0, C))
+        if t == 0:
+            ts(A("fin", 0, 4), A("li3", 0, 4), kG, O.add)
+        planes(A("lc%d" % t, 0, C), A("ls%d" % t, 0, C))
         for u in range(PER):
             listed(A("ol", 32 * u, 32 * u + 32), A("order", u, W3, PER), 32)
         ou = A("ou", 0, 6)
@@ -441,6 +460,10 @@ def rank_program(g, core, T, topo):
             act(A("sc", W3 * h, W3 * h + W3), I(A("sp", C * h, C * h + C), ou))
         for h in range(2):
             act(A("hf", W3 * h, W3 * h + W3), I(A("gg", C * h, C * h + C), ou), AF.Identity, bias=kBi, scale=kSc)
+        if t == 0:
+            act(A("mw", 0, 400), I(s16(4), A("irep", 0, 25)), AF.Identity, bias=512.0, scale=-512.0)
+        for b in range(2 if t == 0 else 4):
+            act(A("db%d" % b, 0, C), A("pF%d" % b, 0, C), scale=0.5)
         kai, on = A("kai", 0, W3), A("hb", 2 * W3, 3 * W3)
         tt(kai, I(A("kr", 0, C), ou), A("cm", 0, W3), O.mult)
         ts(A("jm", 0, W3), kai, 7, O.bitwise_and)
@@ -471,11 +494,11 @@ def rank_program(g, core, T, topo):
         parts = [(a, min(a + TG // 16, NC)) for a in range(0, NC, TG // 16)]
         for a, e in parts:
             act(A("val", 16 * a, 16 * e), I(A("mw", 0, 400), A("bu", a, e)), AF.Identity, bias=16.0 * a - UP * t)
-        turn(A("mrow", 0, W3), A("ab", 0, W3))
-        tt(A("bo", 0, NC), A("bh", 0, NC), A("tagq", 0, NC), O.add)
         if t == 0:
-            fill(A("one", 0, 12 * TG, TG), 4096.0)
-            quant(A("qv", 0, 128), A("sv", 0, 128), A("vt", 0, 512))
+            for b in range(2, 4):
+                act(A("db%d" % b, 0, C), A("pF%d" % b, 0, C), scale=0.5)
+        tt(A("bo", 0, NC), A("bh", 0, NC), A("tagq", 0, NC), O.add)
+        turn(A("mrow", 0, W3), A("ab", 0, W3))
         ts(A("ofu", 0, NC), A("bo", 0, NC), TG / 16.0, O.mult)
         scatter(A("lrep", 0, 1800), A("pu", 0, 6), A("mrow", 0, W3))
         dma("s", A("llr", 0, 48), row5)
@@ -486,18 +509,22 @@ def rank_program(g, core, T, topo):
                 tt(A("tmp", 16 * a, 16 * e), I(tab, A("ofu", a, e)), val, O.min)
                 val = A("tmp", 16 * a, 16 * e)
             scatter(tab, A("ofu", a, e), val)
-        for k in range(2):
-            a, e = 12 * TG * k, 12 * TG * (k + 1)
-            scan(A("ste", a, e), A("one", 0, 12 * TG), A("tab", a, e), O.add, O.min)
-        ts(A("eu", 0, 24), A("ste", TG - 1, 24 * TG, TG), UP * t, O.add, SL - 1.0, O.min)
         for b in range(4):
             z, win = A("za", SL * b, SL * b + SL), A("db%d" % b, 0, C + 16)
             act(z, I(win, A("came%d" % t, 0, NC)))
             tt(A("zt", b, 4 * SL, 4), I(win, A("came%d" % t, 32, 32 + NC)), z, O.add)
+        if t == 0:
+            search_constants()
         quant(A("qz", 0, SL), A("sz", 0, SL), A("zt", 0, 4 * SL))
         for b in range(4):
             mm(A("pF%d" % b, 0, SL), A("qw", 128 * b, 128 * b + 128), A("sw", 128 * b, 128 * b + 128),
                A("qz", 0, SL), A("sz", 0, SL))
+        for k in range(2):
+            a, e = 12 * TG * k, 12 * TG * (k + 1)
+            scan(A("ste", a, e), A("one", 0, 12 * TG), A("tab", a, e), O.add, O.min)
+        if t == 0:
+            quant(A("qv", 0, 128), A("sv", 0, 128), A("vt", 0, 512))
+        ts(A("eu", 0, 24), A("ste", TG - 1, 24 * TG, TG), UP * t, O.add, SL - 1.0, O.min)
         if last:
             ts(A("ll", 0, 48), A("llr", 0, 48), 511, O.bitwise_and)
             fill(A("lo", 48, 64), 0.0)
@@ -511,16 +538,20 @@ def rank_program(g, core, T, topo):
                         (T.lot[32 * a:32 * a + 16, 32 + 16 * h:48 + 16 * h], [("lot", 32, 64, 1)]))
         for b in range(4):
             act(A("hs%d" % b, 0, SL), A("pF%d" % b, 0, SL), scale=0.03125)
-            tt(A("x%d" % (t + 1), b, 4 * C, 4), I(A("hs%d" % b, 0, SL), A("eu", 0, 24)), A("fb%d" % b, 0, C), O.add)
+        for a, e in ((0, 256), (256, C)) if last else ((0, C),):
+            for b in range(4):
+                tt(A("x%d" % (t + 1), 4 * a + b, 4 * e, 4), I(A("hs%d" % b, 0, SL), A("eu", a // 16, e // 16)),
+                   A("fb%d" % b, a, e), O.add)
+            if last:
+                qx, sx, bank = A("qx%d" % R, a, e), A("sx%d" % R, a, e), A("pC" if a else "pS", 0, e - a)
+                quant(qx, sx, A("x%d" % R, 4 * a, 4 * e))
+                mm(bank, A("qv", 0, 128), A("sv", 0, 128), qx, sx)
+                dma("s", ext(T.oc[:, 4 * a:4 * e]), U8("qx%d" % R, a, e))
+                act(A("ys", a, e), bank)
+                dma("a", ext(T.y[:, a:e]), A("ys", a, e))
 
-    qx, sx = A("qx%d" % R, 0, C), A("sx%d" % R, 0, C)
-    quant(qx, sx, A("x%d" % R, 0, 4 * C))
-    mm(S, A("qv", 0, 128), A("sv", 0, 128), qx, sx)
-    dma("s", ext(T.oc[:, :]), U8("qx%d" % R, 0, C))
     for k in range(4):
-        dma("as"[k % 2], ext(T.osc[4 * k:4 * k + 4, :]), (T["sx%d" % R][32 * k:32 * k + 4, 0:C], sx[1]))
-    act(A("ys", 0, C), S)
-    dma("a", ext(T.y[:, :]), A("ys", 0, C))
+        dma("s", ext(T.osc[4 * k:4 * k + 4, :]), (T["sx%d" % R][32 * k:32 * k + 4, 0:C], [("sx%d" % R, 0, C, 1)]))
     for src in sorted(count):
         need("p", src, count[src])
     g.wait_ge(T.sem.lsent, R * 3 * width)

@@ -13,6 +13,7 @@ TG = 96
 UP = 1024.0
 KB, TINY = 2.0 ** 17, 2.0 ** -40
 HUGE = 2.0 ** 80
+WAKE, SLACK, AHEAD = 110.0, 0.0, 40
 AROWS = (20, 19, 18)
 TILES = [(rows, max(128, 16 * min(max(rows), 24))) for rows in ([24, 23, 22, 21], [20, 19, 18, 17], [16, 15, 14, 13],
                                                               [12, 11, 10, 9], [8, 7, 6, 5], [4, 3, 2, 1])]
@@ -50,10 +51,10 @@ def _pool(pool, dtype, spec):
 
 
 _own(BF, "x0:1536 x1:1536 x2:1536 x3:1536 ut:512 vt:512 et:2048 ones:512 za:1408 zt:1408")
-_own(BF, "fb0:384 fb1:384 fb2:384 fb3:384 db0:400 db1:400 db2:400 db3:400 bd:512 bd1:512 mt:5632")
-_own(F32, "hs0:352 hs1:352 hs2:352 hs3:352 ys:384 lot:64")
+_own(BF, "fb0:384 fb1:384 db0:400 db1:400 db2:400 db3:400 bd:1024 bd1:512 mt:5632")
+_own(F32, "hs0:352 hs1:352 hs2:352 hs3:352 ga2:384 ga3:384 ys:384 lot:64")
 _own(I32, "llr:48 lrep:1824")
-for _n, _k in (("w", 512), ("v", 128), ("u0", 128), ("u", 128), ("e", 512), ("z", SL), ("bd", 128), ("m", 1408)):
+for _n, _k in (("w", 512), ("v", 128), ("u0", 128), ("u", 128), ("e", 512), ("z", SL), ("bd", 256), ("m", 1408)):
     _own(COD, "q%s:%d" % (_n, _k))
     _own("uint8", "s%s:%d" % (_n, _k))
 for _t in range(R):
@@ -64,16 +65,18 @@ for _t in range(R + 1):
     _own(COD, "qx%d:384" % _t)
     _own("uint8", "sx%d:384" % _t)
 SCRATCH["gt"] = ("sbuf", [128, 48, 16], BF)
-_pool("poolf", F32, "col:32 s16:192 idr:384 posi:384 posc:384 b0:384 b1:384 b2:384 b3:384 w0:384 mk:384 d0f:384 "
-      "npos:24 tagq:24 cm:96 f0:48 f1:48 f2:48 li2:24 li4:24 v0:384 v1:384 v2:384 v3:384 ssb:384 sp:768 ms:384 mi:384 ff:384 "
+_pool("poolf", F32, "col:32 s16:192 idr:384 posi:384 posc:384 b0:384 b1:384 b2:384 b3:384 w0:384 smd:384 sn:384 t1:24 slm:24 pre:24 "
+      "npos:24 tagq:24 cm:96 f0:48 f1:48 f2:48 li2:24 li4:24 v0:384 v1:384 v2:384 v3:384 ssb:384 sp:768 ms:384 "
       "cnt:24 rk:24 rk2:24 rk3:24 cs:384 order:384 ol:96 sc:192 hf:192 hft:192 ab:192 lt:96 ltt:96 bd0:24 bd2:24 bo:24 "
       "ix:96 iy:96 mrow:96 lo:64")
-_pool("poolb", BF, "kt:384 r16b:384 mw:400 sgn:384 sk:384 gg:768 d1k:648 ne:648 st:648 z0:384 ex:384 kr:384 sg:1536 "
+_pool("poolb", BF, "kt:384 r16b:384 md:384 kp:384 sk:384 gg:768 d1k:324 ne:648 st:648 z0:384 ex:384 kr:384 sg:1536 "
       "eqs:384 junk:1536 hb:288 hbt:288 inv:96 wv:96 val:384 tmp:384 tab:2400 one:1152")
-_pool("pooli", I32, "pi:2 li5:8 li3:4 ll:48 kai:96 jm:96 li:64 lj:64 bt:24 bh:24")
-_pool("poolu", U16, "upl:8 irep:26 fin:4 lu:48 cu:24 rku:24 ou:6 pu:6 bu:24 ofu:24 eu:24")
+_pool("pooli", I32, "pi:2 li5:8 li3:4 ll:48 kai:96 jm:96 li:64 lj:64 bt:24 bh:24 bl:24")
+_pool("poolu", U16, "upl:8 irep:26 blk:24 fin:4 lu:48 cu:24 rku:24 ou:6 pu:6 bu:24 ofu:24 eu:24")
 _pool("poolh", F16, "ste:2304")
-PSUM = ("pS", "pC", "pF0", "pF1", "pF2", "pF3")
+PSUM = ("pS", "pC", "pF0", "pF1", "pF2", "pF3", "pG2", "pG3")
+OWN = ("pF0", "pF1", "pG2", "pG3")
+HALVES = ((0, 192), (192, C))
 for _n in PSUM:
     SCRATCH[_n] = ("psum", [128, 512], F32)
 NDMA = 40
@@ -92,7 +95,7 @@ def rank_program(g, core, T, topo):
     eng = {"v": g.vector, "a": g.scalar, "t": g.tensor, "p": g, "s": g.sync}
     semof = {"v": "qv_", "a": "qa_", "t": "qt_", "p": "qp_"}
     count, known = {}, {q: {} for q in eng}
-    clocks, hist = {}, {}
+    clocks, hist, ops = {}, {}, []
     ndma = [0]
 
     def need(q, src, val):
@@ -109,45 +112,96 @@ def rank_program(g, core, T, topo):
     def covers(x, y):
         return x[0] <= y[0] and y[1] <= x[1] and (x[2] == 1 or x[2] == y[2] and (x[0] - y[0]) % x[2] == 0)
 
-    def order(q, reads, writes):
-        todo = {}
-        mine = semof.get(q)
+    def record(q, kind, fn, reads, writes, hold, more=0.0, after=()):
+        deps = {i: True for i in after}
         for r, w in [(r, False) for r in reads] + [(r, True) for r in writes]:
-            for piece, src, val, wrote in hist.get(r[0], ()):
-                if meet(r[1:], piece) and (w or wrote or (r[0] in PSUM and src != mine)):
-                    todo[src] = max(todo.get(src, 0), val)
-        for src in sorted(todo, key=lambda s: s != mine):
-            need(q, src, todo[src])
-
-    def note(src, val, reads, writes):
+            for piece, i, wrote in hist.get(r[0], ()):
+                if (meet(r[1:], piece) and (w or wrote)) or (r[0] in PSUM and ops[i]["q"] != q):
+                    deps[i] = True
+        if kind == "sum":
+            deps = {i: ops[i]["q"] != q for i in deps}
+        me = len(ops)
+        ops.append({"q": q, "kind": kind, "fn": fn, "deps": deps, "hold": hold, "more": more})
         for r in writes:
-            h = [x for x in hist.get(r[0], ()) if not covers(r[1:], x[0])]
-            hist[r[0]] = h + [(r[1:], src, val, True)]
+            hist[r[0]] = [x for x in hist.get(r[0], ()) if not covers(r[1:], x[0])] + [(r[1:], me, True)]
         for r in reads:
             if r not in writes:
-                h = [x for x in hist.get(r[0], ()) if not (x[0] == r[1:] and x[1] == src and not x[3])]
-                hist[r[0]] = h + [(r[1:], src, val, False)]
+                hist[r[0]] = hist.get(r[0], []) + [(r[1:], me, False)]
+        return me
 
-    def emit(q, fn, reads, writes):
-        order(q, reads, writes)
-        src = semof[q]
-        count[src] = count.get(src, 0) + 1
-        fn().then_inc(T.sem[src], 1)
-        clocks[(src, count[src])] = {**known[q], src: count[src]}
-        note(src, count[src], reads, writes)
+    def arrange():
+        n = len(ops)
+        users = [[] for _ in range(n)]
+        for j, o in enumerate(ops):
+            for i in o["deps"]:
+                users[i].append(j)
+        left = [len(o["deps"]) for o in ops]
+        earliest, out = [0.0] * n, []
+        line = {q: [i for i in range(n) if ops[i]["q"] == q] for q in "vatpsr"}
+        free = {q: 0.0 for q in line}
+        while len(out) < n:
+            due, q = min((max(earliest[l[0]], free[q]), q) for q, l in line.items() if l and not left[l[0]])
+            fits = [j for j in line[q][1:AHEAD] if not left[j] and ops[j]["kind"] == "call"
+                    and max(earliest[j], free[q]) < due and max(earliest[j], free[q]) + ops[j]["hold"] <= due + SLACK]
+            i = fits[0] if fits else line[q][0]
+            line[q].remove(i)
+            out.append(i)
+            free[q] = max(earliest[i], free[q]) + ops[i]["hold"]
+            for j in users[i]:
+                earliest[j] = max(earliest[j], free[q] + ops[i]["more"] + (WAKE if ops[j]["deps"][i] else 0.0))
+                left[j] -= 1
+        return out
 
-    def dma(q, out, in_):
-        order(q, in_[1], out[1])
-        src = "d%d" % ndma[0]
-        ndma[0] += 1
-        eng[q].dma_start(out[0], in_[0]).then_inc(T.sem[src], 16)
-        count[src] = 16
-        clocks[(src, 16)] = {**known[q], src: 16}
-        note(src, 16, in_[1], out[1])
+    def issue():
+        mark = {}
+        for i in arrange():
+            o = ops[i]
+            q, todo = o["q"], {}
+            if o["kind"] == "landing":
+                mark[i] = o["fn"]
+                continue
+            for j, wait in o["deps"].items():
+                if wait and j in mark:
+                    todo[mark[j][0]] = max(todo.get(mark[j][0], 0), mark[j][1])
+            for src in sorted(todo, key=lambda s: s != semof.get(q)):
+                need(q, src, todo[src])
+            if o["kind"] == "send":
+                o["fn"]()
+                continue
+            src, step = semof.get(q), 1
+            if o["kind"] == "dma":
+                src, step = "d%d" % ndma[0], 16
+                ndma[0] += 1
+            count[src] = count.get(src, 0) + step
+            o["fn"]().then_inc(T.sem[src], step)
+            clocks[(src, count[src])] = {**known[q], src: count[src]}
+            mark[i] = (src, count[src])
+
+    def size(piece):
+        return len(range(*piece[1:]))
+
+    def wide(piece):
+        return SCRATCH[PLACE.get(piece[0], piece)[0]][2] not in (BF, F16, U16)
+
+    def emit(q, fn, reads, writes, rate=1.0, n=None):
+        n = size(writes[0]) if n is None else n
+        if any(isinstance(r, list) for r in reads + writes):
+            hold = 60.0 + n * (3.8 if isinstance(writes[0], list) else 1.56)
+        elif q == "v":
+            both = all(r[0] not in PSUM for r in reads)
+            hold = max(64.0, n * (rate if both else 1.0) * (1.0 if any(wide(r) for r in reads + writes if size(r) > 1) else 0.5))
+        else:
+            hold = max(64.0, n * rate)
+        record(q, "call", fn, [tuple(r) for r in reads], [tuple(r) for r in writes], hold)
+
+    def dma(q, out, in_, more=2500.0):
+        record(q, "dma", lambda: eng[q].dma_start(out[0], in_[0]), in_[1], out[1], 50.0, more)
 
     def send(out, in_, sem):
-        order("p", in_[1], [])
-        g.remote_dma(out, in_[0], T.sem[sem], T.sem.lsent, pid, rid, mask)
+        return record("p", "send", lambda: g.remote_dma(out, in_[0], T.sem[sem], T.sem.lsent, pid, rid, mask), in_[1], [], 1000.0)
+
+    def landing(sem, val, pieces, after, more):
+        record("r", "landing", (sem, val), [], pieces, 0.0, more, after)
 
     def A(n, a, b, s=1):
         buf, o = PLACE.get(n, (n, 0))
@@ -160,7 +214,7 @@ def rank_program(g, core, T, topo):
         return (T[n][:, a:b].bitcast(dt.uint32), [(n, a, b, 1)])
 
     def I(win, off):
-        return (win[0].indirect(off[0]), win[1] + off[1])
+        return (win[0].indirect(off[0]), [list(win[1][0])] + off[1])
 
     def ext(v):
         return (v, [])
@@ -177,10 +231,10 @@ def rank_program(g, core, T, topo):
         emit("v", lambda: V.tensor_copy(out[0], in_[0]), rd(in_), out[1])
 
     def scatter(win, off, in_):
-        emit("v", lambda: V.tensor_copy(win[0].indirect(off[0]), in_[0]), rd(off, in_), win[1])
+        emit("v", lambda: V.tensor_copy(win[0].indirect(off[0]), in_[0]), rd(off, in_), [list(win[1][0])], 1.0, size(in_[1][0]))
 
     def tt(out, a, b, op):
-        emit("v", lambda: V.tensor_tensor(out[0], a[0], b[0], op), rd(a, b), out[1])
+        emit("v", lambda: V.tensor_tensor(out[0], a[0], b[0], op), rd(a, b), out[1], 2.0)
 
     def ts(out, a, s1, op0, s2=None, op1=None):
         if op1 is None:
@@ -204,7 +258,7 @@ def rank_program(g, core, T, topo):
         emit("v", lambda: V.memset(out[0], k), [], out[1])
 
     def quant(q, s, x):
-        emit("v", lambda: V.quantize_mx(q[0], s[0], x[0]), rd(x), q[1] + s[1])
+        record("v", "call", lambda: V.quantize_mx(q[0], s[0], x[0]), rd(x), q[1] + s[1], 15.0 + 0.27 * size(x[1][0]))
 
     def act(out, in_, func=AF.Copy, bias=None, scale=None, accum=None):
         kw = {}
@@ -218,17 +272,16 @@ def rank_program(g, core, T, topo):
              out[1] + (accum[1] if accum is not None else []))
 
     def mm(out, w, ws, x, xs, start=True, stop=True):
-        emit("t", lambda: g.tensor.matmul_mx(out[0], w[0], ws[0], x[0], xs[0], start, stop), rd(w, ws, x, xs),
-             out[1] if start else [])
-        if not start:
-            note(semof["t"], count[semof["t"]], [], [("pC", 0, C, 1)])
+        record("t", "call" if start else "sum", lambda: g.tensor.matmul_mx(out[0], w[0], ws[0], x[0], xs[0], start, stop),
+               rd(w, ws, x, xs), out[1], 16.0 + size(out[1][0]))
 
     def iota(out, pattern, base, cm, flag=False):
         kw = {"allow_small_or_imprecise_dtypes": True} if flag else {}
-        emit("p", lambda: g.iota(out[0], pattern, base, cm, **kw), [], out[1])
+        record("p", "call", lambda: g.iota(out[0], pattern, base, cm, **kw), [], out[1], 130.0 + 2 * size(out[1][0]))
 
     def choose(out, in_, pattern, cmp, base, cm):
-        emit("p", lambda: g.affine_select(out[0], in_[0], pattern, cmp, 0.0, base, cm), in_[1], out[1])
+        record("p", "call", lambda: g.affine_select(out[0], in_[0], pattern, cmp, 0.0, base, cm), in_[1], out[1],
+               170.0 + 2 * size(out[1][0]))
 
     (kI, kType, kG, kB0, kB1, kB2, kB3, kOff, kSc, kBi, kBj, kP, kS, kS24, kK, kIb, kz) = [
         A("col", k, k + 1) for k in range(17)]
@@ -252,11 +305,12 @@ def rank_program(g, core, T, topo):
     iota(A("li3", 0, 4), [[W3, 2], [16, 2]], 0, 0)
     ones, half, blocks = A("ones", 0, 512), A("bd1", 0, 512), A("bd", 0, 512)
     iota(ones, [[0, 512]], 1, 0, True)
+    choose(half, ones, [[-16, 8], [0, 64]], O.is_ge, 0, 1)
+    choose(blocks, half, [[16, 8], [0, 64]], O.is_ge, 15, -1)
+    choose(A("bd", 512, 1024), blocks, [[-1, 128], [1000, 4]], O.is_ge, -1, 1)
 
     def later_on_g():
-        choose(half, ones, [[-16, 8], [0, 64]], O.is_ge, 0, 1)
-        choose(blocks, half, [[16, 8], [0, 64]], O.is_ge, 15, -1)
-        iota(A("li2", 0, 24), [[16, 24]], 15, 0, True)
+        iota(A("li2", 0, 24), [[16, 24]], 0, 0, True)
         iota(A("li4", 0, 24), [[0, 4], [-16, 6]], TG - 1, 0, True)
         for b in range(4):
             choose(A("et", 512 * b, 512 * b + 512), ones, [[4, 128], [1, 4]], O.is_equal, -b, -4)
@@ -290,7 +344,7 @@ def rank_program(g, core, T, topo):
     for k, bias in enumerate((kB0, kB1, kB2, kB3)):
         ts(bias, kType, L - 1.5 - k, O.is_lt, UP * (k + 2), O.mult)
     act(A("w0", 0, C), A("idr", 0, C), AF.Identity, bias=UP)
-    act(A("kt", 0, C), I(s16(10), A("irep", 0, 24)))
+    act(A("md", 0, C), I(s16(4), A("irep", 0, 24)))
     for k, bias in enumerate((kB0, kB1, kB2, kB3)):
         act(A("b%d" % k, 0, C), A("idr", 0, C), AF.Identity, bias=bias)
     ts(kS, kI, 0.0, O.is_equal, 1.0 / (KB * TINY), O.mult)
@@ -299,15 +353,16 @@ def rank_program(g, core, T, topo):
     ts(kS, kS, 1.0 / KB, O.max)
     ts(kOff, kType, UP, O.mult, -L * UP - 192.0, O.add)
     fill(A("r16b", 0, C, 16), 0.0)
+    tc(A("blk", 0, 24), A("idr", 0, 24))
     quant(A("qu0", 0, 128), A("su0", 0, 128), A("ut", 0, 512))
     tc(U32("qu", 0, 128), I(U32("qu0", 0, 128), A("upl", 0, 8)))
     tc(A("su", 0, 128), I(A("su0", 0, 128), A("upl", 0, 8)))
 
     S = A("pS", 0, C)
 
-    def planes(codes, plane):
+    def planes(codes, plane, banks=PSUM[2:6]):
         for b in range(4):
-            mm(A("pF%d" % b, 0, C), A("qe", 128 * b, 128 * b + 128), A("se", 128 * b, 128 * b + 128), codes, plane)
+            mm(A(banks[b], 0, C), A("qe", 128 * b, 128 * b + 128), A("se", 128 * b, 128 * b + 128), codes, plane)
 
     def meeting_constants():
         f = [8 * m[0] + m[1] + 1.25 if m else None for m in MEET]
@@ -316,11 +371,13 @@ def rank_program(g, core, T, topo):
         steps = [f[e] - f[e + 1] for e in range(NB - 2)] + [f[NB - 2], -100.0]
         for e in range(NB):
             if steps[e] != 7.0:
-                put(A("d1k", e, 24 * NB, NB), 24, steps[e])
+                put(A("d1k", e, 12 * NB, NB), 12, steps[e])
 
     def count_constants():
-        act(A("mk", 0, C), I(s16(4), A("irep", 0, 24)), AF.Identity, bias=-2e29, scale=5e29)
-        act(A("d0f", 0, C), A("r16b", 0, C), AF.Identity, bias=-2e29, scale=5e29)
+        act(A("kt", 0, C), I(s16(10), A("irep", 0, 24)))
+        act(s16(5), s16(4), AF.Identity, bias=1.0, scale=UP - 1.0)
+        put(A("s16", 80, 81), 1, 0.0)
+        act(A("kp", 0, C), I(s16(5), A("irep", 0, 24)))
         put(A("cnt", 0, 1), 1, 0.0)
         at = 0
         for rows, w in TILES:
@@ -331,7 +388,7 @@ def rank_program(g, core, T, topo):
 
     def rank_constants():
         act(kSc, kI, AF.Sign)
-        act(kz, kI, scale=-1.0)
+        act(kz, kI, AF.Identity, bias=0.2)
         act(kK, kSc, AF.Identity, bias=KB * TINY, scale=KB)
         act(A("npos", 0, 24), A("li2", 0, 24), AF.Identity, bias=kz)
 
@@ -359,25 +416,27 @@ def rank_program(g, core, T, topo):
         qx, sx = A("qx%d" % t, 0, C), A("sx%d" % t, 0, C)
         quant(qx, sx, A("x%d" % t, 0, 4 * C))
         mm(S, A("qu", 0, 128), A("su", 0, 128), qx, sx)
-        send(T["lc%d" % t][:, 0:C].bitcast(dt.uint8), U8("qx%d" % t, 0, C), "arx%d" % t)
-        send(T["ls%d" % t][:, 0:C], sx, "arx%d" % t)
-        note("arx%d" % t, 2 * width, [], [("lc%d" % t, 0, C, 1), ("ls%d" % t, 0, C, 1)])
+        sent = [send(T["lc%d" % t][:, 0:C].bitcast(dt.uint8), U8("qx%d" % t, 0, C), "arx%d" % t),
+                send(T["ls%d" % t][:, 0:C], sx, "arx%d" % t)]
+        landing("arx%d" % t, 2 * width, [("lc%d" % t, 0, C, 1), ("ls%d" % t, 0, C, 1)], sent, 14000.0)
         if t == 0:
             later_on_g()
         else:
-            planes(qx, sx)
-        act(A("sgn", 0, C), S, AF.Sign)
+            planes(qx, sx, OWN)
         ts(A("ll", 0, 48), A("llr", 0, 48), 511, O.bitwise_and)
-        act(A("ssb", 0, C), S)
+        if t == 0:
+            tt(s16(11), s16(4), s16(2), O.mult)
+            fill(A("d1k", 0, 12 * NB), 7.0)
+            total(kG, s16(11))
         tt(A("f0", 1, 48, 2), A("ll", 24, 48), A("ll", 0, 24), O.subtract)
         tc(A("f1", 1, 48, 2), A("ll", 0, 24))
         tc(A("lu", 0, 48), A("ll", 0, 48))
-        if t == 0:
-            tt(s16(11), s16(4), s16(2), O.mult)
-            fill(A("d1k", 0, 24 * NB), 7.0)
-            total(kG, s16(11))
-        listed(A("sk", 0, C), A("sgn", 0, C), C)
-        ts(A("f1", 0, 48, 2), A("sk", 15, C, 16), kS, O.mult, 0.5, O.is_gt)
+        for a, e in HALVES:
+            tt(A("smd", a, e), A("pS", a, e), A("md", a, e), O.mult)
+        for a, e in HALVES:
+            scan(A("sn", a, e), A("r16b", a, e), A("smd", a, e), O.mult, O.add)
+        act(A("ssb", 0, C), S)
+        ts(A("f1", 0, 48, 2), A("sn", 15, C, 16), 0.0, O.is_gt)
         scan(A("f2", 0, 48), A("f0", 0, 48), A("f1", 0, 48), O.mult, O.add)
         tc(A("cu", 0, 24), A("f2", 1, 48, 2))
         if t == 0:
@@ -398,54 +457,70 @@ def rank_program(g, core, T, topo):
             rank_constants()
         turn((T.gt[:, 24:48, :], [("gt", C, 2 * C, 1)]), A("gg", C, 2 * C))
         turn((T.gt[:, 0:24, :], [("gt", 0, C, 1)]), A("gg", 0, C))
-        for b in range(1, 4 if t else 0):
-            act(A("fb%d" % b, 0, C), A("pF%d" % b, 0, C))
+        if t:
+            act(A("fb1", 0, C), A("pF1", 0, C))
         for x, ((r, s), (r2, s2)) in enumerate(trios):
             tt(A("ne", x, 24 * NB, NB // 3), (T.gt[:, 0:24, r:r + 2 * s + 1:s], [("gt", 0, C, 1)]),
                (T.gt[:, 24:48, r2:r2 + 2 * s2 + 1:s2], [("gt", C, 2 * C, 1)]), O.not_equal)
-        scan(A("st", 0, 24 * NB), A("ne", 0, 24 * NB), A("d1k", 0, 24 * NB), O.mult, O.add, -100.0)
-        ts(A("z0", 0, C, 16), A("st", NB - 2, 24 * NB, NB), -0.25, O.max, HUGE, O.mult)
-        scan(A("ex", 0, C), A("r16b", 0, C), A("z0", 0, C), O.mult, O.add)
-        turn(A("kr", 0, C), A("ex", 0, C))
-        tt(A("ms", 0, C), S, A("kr", 0, C), O.min)
-        tt(A("mi", 0, C), A("ms", 0, C), A("mk", 0, C), O.min)
-        scan(A("ff", 0, C), A("d0f", 0, C), A("mi", 0, C), O.min, O.max)
+        for a, e in HALVES:
+            a, e = a // 16 * NB, e // 16 * NB
+            scan(A("st", a, e), A("ne", a, e), A("d1k", 0, e - a), O.mult, O.add, -100.0)
+        for a, e in HALVES:
+            ts(A("z0", a, e, 16), A("st", a // 16 * NB + NB - 2, e // 16 * NB, NB), -0.25, O.max, HUGE, O.mult)
+        for a, e in HALVES:
+            scan(A("ex", a, e), A("r16b", a, e), A("z0", a, e), O.mult, O.add)
+        for a, e in HALVES:
+            turn(A("kr", a, e), A("ex", a, e))
+        for a, e in HALVES:
+            listed(A("sk", a, e), A("kr", a, e), e - a)
+        tt(A("ms", 0, 192), A("pS", 0, 192), A("kr", 0, 192), O.min)
+        ts(A("t1", 0, 24), A("sk", 15, C, 16), kS, O.mult, -HUGE / 8, O.max)
+        tt(A("ms", 192, C), A("pS", 192, C), A("kr", 192, C), O.min)
+        tt(A("slm", 0, 24), A("t1", 0, 24), A("sn", 15, C, 16), O.min)
         if t == 0:
-            quant(A("qbd", 0, 128), A("sbd", 0, 128), A("bd", 0, 512))
+            quant(A("qbd", 0, 256), A("sbd", 0, 256), A("bd", 0, 1024))
         spot, at = {}, 0
         for rows, w in TILES:
             for i, c in enumerate(rows):
                 spot[c] = A("mt", at + i, at + 64 * min(c, 24), 4)
             at += 4 * w
-        score = lambda c: A("ff", 16 * c + 15, 16 * c + 16)
+        score = lambda c: A("slm", c, c + 1)
+        sg = lambda c: A("sg", C * (c % 4), C * (c % 4) + 16 * c)
         for c in AROWS:
-            sg = A("sg", C * (c % 4), C * (c % 4) + 16 * c)
-            act(sg, A("ms", 0, 16 * c), AF.Sign, bias=score(c), scale=-1.0)
-            act(spot[c], sg, AF.Relu, accum=A("cnt", c, c + 1))
-        at = 0
+            act(sg(c), A("ms", 0, 16 * c), AF.Sign, bias=score(c), scale=-1.0)
+        for c in AROWS:
+            act(spot[c], sg(c), AF.Relu, accum=A("cnt", c, c + 1))
+        at, sums = 0, []
+
+        def column_sums(k, at, w):
+            a, s = at // 4, 128 if k == 0 else 0
+            quant(A("qm", a, a + w), A("sm", a, a + w), A("mt", at, at + 4 * w))
+            mm(A("pC", 0, w), A("qbd", s, s + 128), A("sbd", s, s + 128), A("qm", a, a + w), A("sm", a, a + w), k == 0, k == 5)
+
         for k, (rows, w) in enumerate(TILES):
-            for c in rows:
+            for c in sorted(rows, key=lambda c: c == 24):
                 if c == 24:
-                    tt(spot[c], A("ms", 0, C), A("ff", 0, C), O.is_le)
-                    scan(A("eqs", 0, C), A("r16b", 0, C), spot[c], O.mult, O.add)
+                    tt(spot[c], I(A("slm", 0, 24), A("blk", 0, 24)), A("ms", 0, C), O.is_gt)
                 elif c not in AROWS:
                     ts(spot[c], A("ms", 0, 16 * c), score(c), O.is_lt)
                     act(A("junk", C * (c % 4), C * (c % 4) + 16 * c), spot[c], accum=A("cnt", c, c + 1))
-            a = at // 4
-            quant(A("qm", a, a + w), A("sm", a, a + w), A("mt", at, at + 4 * w))
-            mm(A("pC", 0, w), A("qbd", 0, 128), A("sbd", 0, 128), A("qm", a, a + w), A("sm", a, a + w), k == 0, k == 5)
+                if sums and c not in AROWS:
+                    column_sums(*sums.pop())
+            sums.append((k, at, w))
             at += 4 * w
-            if k == 4:
-                tt(A("rk", 0, 24), A("npos", 0, 24), A("eqs", 15, C, 16), O.subtract)
+        scan(A("eqs", 0, C), A("kp", 0, C), spot[24], O.mult, O.add)
+        column_sums(*sums.pop())
+        ts(A("pre", 0, 24), A("eqs", 15, C, 16), -1.0 / UP, O.mult)
         if t == 0:
             quant(A("qe", 0, 512), A("se", 0, 512), A("et", 0, 2048))
-            planes(qx, sx)
+            planes(qx, sx, OWN)
             slot_constants()
-            for b in range(4):
+            for b in range(2):
                 act(A("fb%d" % b, 0, C), A("pF%d" % b, 0, C))
-        tt(A("rk2", 0, 24), A("rk", 0, 24), A("cnt", 0, 24), O.subtract)
+        tt(A("rk2", 0, 24), A("npos", 0, 24), A("cnt", 0, 24), O.subtract)
+        tt(A("rk", 0, 24), A("rk2", 0, 24), A("pre", 0, 24), O.add)
+        ts(A("rk3", 0, 24), A("rk", 0, 24), kK, O.mult)
         listed(A("cs", 0, C), A("pC", 0, C), C)
-        ts(A("rk3", 0, 24), A("rk2", 0, 24), kK, O.mult)
         tt(A("rk", 0, 24), A("rk3", 0, 24), A("cs", 15, C, 16), O.add)
         ts(A("rku", 0, 24), A("rk", 0, 24), kS, O.mult)
         scatter(A("order", 0, C), A("rku", 0, 24), A("idr", 0, C))
@@ -461,53 +536,57 @@ def rank_program(g, core, T, topo):
         for h in range(2):
             act(A("hf", W3 * h, W3 * h + W3), I(A("gg", C * h, C * h + C), ou), AF.Identity, bias=kBi, scale=kSc)
         if t == 0:
-            act(A("mw", 0, 400), I(s16(4), A("irep", 0, 25)), AF.Identity, bias=512.0, scale=-512.0)
+            act(s16(9), s16(4), AF.Identity, bias=512.0, scale=-512.0)
         for b in range(2 if t == 0 else 4):
             act(A("db%d" % b, 0, C), A("pF%d" % b, 0, C), scale=0.5)
         kai, on = A("kai", 0, W3), A("hb", 2 * W3, 3 * W3)
         tt(kai, I(A("kr", 0, C), ou), A("cm", 0, W3), O.mult)
         ts(A("jm", 0, W3), kai, 7, O.bitwise_and)
         ts(A("hb", 0, W3), kai, kP, O.is_ge, 8192.0, O.mult)
-        ts(A("inv", 0, W3), kai, 0.0, O.is_equal, 43.0, O.mult)
         ts(A("hb", W3, 2 * W3), A("jm", 0, W3), kI, O.is_ge, 8192.0, O.mult)
         tt(on, A("sc", W3, 2 * W3), A("sc", 0, W3), O.is_gt)
-        turn(A("hbt", 0, 3 * W3), A("hb", 0, 3 * W3))
+        turn(A("hbt", 0, 2 * W3), A("hb", 0, 2 * W3))
+        turn(A("hbt", 2 * W3, 3 * W3), on)
         turn(A("hft", 0, 2 * W3), A("hf", 0, 2 * W3))
-        tt(A("wv", 0, W3), A("inv", 0, W3), on, O.subtract)
+        ts(A("lt", 64, 96), I(A("hbt", 2 * W3, 3 * W3), A("fin", 0, 2)), 8192.0, O.mult, -4096.0, O.add)
         scan(A("ab", 0, 2 * W3), A("hbt", 0, 2 * W3), A("hft", 0, 2 * W3), O.max, O.min)
-        tc(A("lt", 64, 96), I(A("hbt", 2 * W3, 3 * W3), A("fin", 0, 2)))
+        turn(A("ltt", 64, 96), A("lt", 64, 96))
         tc(A("lt", 0, 64), I(A("ab", 0, 2 * W3), A("fin", 0, 4)))
-        turn(A("ltt", 0, 96), A("lt", 0, 96))
+        turn(A("ltt", 0, 64), A("lt", 0, 64))
         tc(A("li", 0, 64), A("ltt", 0, 64))
+        tt(A("bd0", 0, NC), A("ltt", 32, 32 + NC), A("ltt", 64, 64 + NC), O.add)
         ts(A("lj", 0, 64), A("li", 0, 64), 511, O.bitwise_and)
+        tt(A("bt", 0, NC), A("bd0", 0, NC), A("ltt", 0, NC), O.max)
         tc(A("own%d" % t, 0, 64), A("lj", 0, 64))
-        send(T["came%d" % t][:, 0:32 + NC], A("own%d" % t, 0, 32 + NC), "arl%d" % t)
-        note("arl%d" % t, width, [], [("came%d" % t, 0, 64, 1)])
-        tt(A("bd0", 0, NC), A("lj", 32, 32 + NC), A("lj", 0, NC), O.subtract)
-        tt(A("ix", 0, W3), I(A("posc", 0, C), ou), A("wv", 0, W3), O.add)
-        tt(A("bd2", 0, NC), A("bd0", 0, NC), A("ltt", 64, 64 + NC), O.mult)
-        listed(A("iy", 0, W3), A("ix", 0, W3), W3)
-        tt(A("bt", 0, NC), A("bd2", 0, NC), A("lj", 0, NC), O.add)
-        ts(A("pu", 0, 6), A("iy", 15, W3, 16), kS24, O.mult)
-        tc(A("bu", 0, NC), A("bt", 0, NC))
+        ts(A("bl", 0, NC), A("bt", 0, NC), 15, O.bitwise_and)
         ts(A("bh", 0, NC), A("bt", 0, NC), 496, O.bitwise_and)
+        tc(A("bu", 0, NC), A("bl", 0, NC))
+        tt(A("bo", 0, NC), A("bh", 0, NC), A("tagq", 0, NC), O.add)
+        sent = [send(T["came%d" % t][:, 0:32 + NC], A("own%d" % t, 0, 32 + NC), "arl%d" % t)]
+        landing("arl%d" % t, width, [("came%d" % t, 0, 64, 1)], sent, 2500.0)
         parts = [(a, min(a + TG // 16, NC)) for a in range(0, NC, TG // 16)]
         for a, e in parts:
-            act(A("val", 16 * a, 16 * e), I(A("mw", 0, 400), A("bu", a, e)), AF.Identity, bias=16.0 * a - UP * t)
+            act(A("val", 16 * a, 16 * e), I(s16(9), A("bu", a, e)), AF.Identity, bias=16.0 * a - UP * t)
         if t == 0:
             for b in range(2, 4):
                 act(A("db%d" % b, 0, C), A("pF%d" % b, 0, C), scale=0.5)
-        tt(A("bo", 0, NC), A("bh", 0, NC), A("tagq", 0, NC), O.add)
-        turn(A("mrow", 0, W3), A("ab", 0, W3))
+        between = [lambda: tt(A("wv", 0, W3), A("inv", 0, W3), on, O.subtract),
+                   lambda: tt(A("ix", 0, W3), I(A("posc", 0, C), ou), A("wv", 0, W3), O.add),
+                   lambda: listed(A("iy", 0, W3), A("ix", 0, W3), W3),
+                   lambda: ts(A("pu", 0, 6), A("iy", 15, W3, 16), kS24, O.mult),
+                   lambda: turn(A("mrow", 0, W3), A("ab", 0, W3)),
+                   lambda: scatter(A("lrep", 0, 1800), A("pu", 0, 6), A("mrow", 0, W3)),
+                   lambda: dma("s", A("llr", 0, 48), row5)]
+        ts(A("inv", 0, W3), kai, 0.0, O.is_equal, 43.0, O.mult)
         ts(A("ofu", 0, NC), A("bo", 0, NC), TG / 16.0, O.mult)
-        scatter(A("lrep", 0, 1800), A("pu", 0, 6), A("mrow", 0, W3))
-        dma("s", A("llr", 0, 48), row5)
         tab = A("tab", 0, 25 * TG)
         for a, e in parts:
             val = A("val", 16 * a, 16 * e)
             if a:
+                between.pop(0)()
                 tt(A("tmp", 16 * a, 16 * e), I(tab, A("ofu", a, e)), val, O.min)
                 val = A("tmp", 16 * a, 16 * e)
+            between.pop(0)()
             scatter(tab, A("ofu", a, e), val)
         for b in range(4):
             z, win = A("za", SL * b, SL * b + SL), A("db%d" % b, 0, C + 16)
@@ -540,8 +619,12 @@ def rank_program(g, core, T, topo):
             act(A("hs%d" % b, 0, SL), A("pF%d" % b, 0, SL), scale=0.03125)
         for a, e in ((0, 256), (256, C)) if last else ((0, C),):
             for b in range(4):
-                tt(A("x%d" % (t + 1), 4 * a + b, 4 * e, 4), I(A("hs%d" % b, 0, SL), A("eu", a // 16, e // 16)),
-                   A("fb%d" % b, a, e), O.add)
+                x, h = A("x%d" % (t + 1), 4 * a + b, 4 * e, 4), I(A("hs%d" % b, 0, SL), A("eu", a // 16, e // 16))
+                if b < 2:
+                    tt(x, h, A("fb%d" % b, a, e), O.add)
+                else:
+                    act(A("ga%d" % b, a, e), h)
+                    tt(x, A(OWN[b], a, e), A("ga%d" % b, a, e), O.add)
             if last:
                 qx, sx, bank = A("qx%d" % R, a, e), A("sx%d" % R, a, e), A("pC" if a else "pS", 0, e - a)
                 quant(qx, sx, A("x%d" % R, 4 * a, 4 * e))
@@ -552,6 +635,7 @@ def rank_program(g, core, T, topo):
 
     for k in range(4):
         dma("s", ext(T.osc[4 * k:4 * k + 4, :]), (T["sx%d" % R][32 * k:32 * k + 4, 0:C], [("sx%d" % R, 0, C, 1)]))
+    issue()
     for src in sorted(count):
         need("p", src, count[src])
     g.wait_ge(T.sem.lsent, R * 3 * width)

@@ -11,10 +11,11 @@ MEET = MEET[:18] + [None] + MEET[18:] + [None]
 NB = len(MEET)
 TG = 96
 UP = 1024.0
-KB, TINY = 2.0 ** 17, 2.0 ** -40
+KB = 2.0 ** 17
+ZA = 1
 HUGE = 2.0 ** 80
 WAKE, SLACK, AHEAD = 110.0, 0.0, 40
-AROWS = (20, 19, 18)
+AROWS = (19, 18, 17, 16)
 TILES = [(rows, max(128, 16 * min(max(rows), 24))) for rows in ([24, 23, 22, 21], [20, 19, 18, 17], [16, 15, 14, 13],
                                                               [12, 11, 10, 9], [8, 7, 6, 5], [4, 3, 2, 1])]
 
@@ -50,7 +51,7 @@ def _pool(pool, dtype, spec):
     SCRATCH[pool] = ("sbuf", [128, at], dtype)
 
 
-_own(BF, "x0:1536 x1:1536 x2:1536 x3:1536 ut:512 vt:512 et:2048 ones:512 za:1408 zt:1408")
+_own(BF, "x0:1536 x1:1536 x2:1536 x3:1536 ut:512 vt:512 et:516 ones:516 za:1408 zb:704 zt:1408")
 _own(BF, "fb0:384 fb1:384 db0:400 db1:400 db2:400 db3:400 bd:1024 bd1:512 mt:5632")
 _own(F32, "hs0:352 hs1:352 hs2:352 hs3:352 ga2:384 ga3:384 ys:384 lot:64")
 _own(I32, "llr:48 lrep:1824")
@@ -67,11 +68,11 @@ for _t in range(R + 1):
 SCRATCH["gt"] = ("sbuf", [128, 48, 16], BF)
 _pool("poolf", F32, "col:32 s16:192 idr:384 posi:384 posc:384 b0:384 b1:384 b2:384 b3:384 w0:384 smd:384 sn:384 t1:24 slm:24 pre:24 "
       "npos:24 tagq:24 cm:96 f0:48 f1:48 f2:48 li2:24 li4:24 v0:384 v1:384 v2:384 v3:384 ssb:384 sp:768 ms:384 "
-      "cnt:24 rk:24 rk2:24 rk3:24 cs:384 order:384 ol:96 sc:192 hf:192 hft:192 ab:192 lt:96 ltt:96 bd0:24 bd2:24 bo:24 "
+      "cnt:24 cna:24 rk:24 rk2:24 rk3:24 cs:384 order:384 ol:96 sc:192 hf:192 hft:192 ab:192 lt:96 ltt:96 bd0:24 bd2:24 bo:24 "
       "ix:96 iy:96 mrow:96 lo:64")
-_pool("poolb", BF, "kt:384 r16b:384 md:384 kp:384 sk:384 gg:768 d1k:324 ne:648 st:648 z0:384 ex:384 kr:384 sg:1536 "
-      "eqs:384 junk:1536 hb:288 hbt:288 inv:96 wv:96 val:384 tmp:384 tab:2400 one:1152")
-_pool("pooli", I32, "pi:2 li5:8 li3:4 ll:48 kai:96 jm:96 li:64 lj:64 bt:24 bh:24 bl:24")
+_pool("poolb", BF, "kt:384 r16b:384 md:384 sgn:384 kp:384 sk:384 gg:768 d1k:324 ne:648 st:648 z0:384 ex:384 kr:384 sg:1536 "
+      "eqs:384 junk:1536 hb:288 hbt:288 inv:96 wv:96 val:384 tmp:384 tab:2400 one:2304")
+_pool("pooli", I32, "pi:2 li5:8 li3:4 ll:48 kai:96 jm:96 lh:64 li:64 lj:64 bt:24 bh:24 bl:24")
 _pool("poolu", U16, "upl:8 irep:26 blk:24 fin:4 lu:48 cu:24 rku:24 ou:6 pu:6 bu:24 ofu:24 eu:24")
 _pool("poolh", F16, "ste:2304")
 PSUM = ("pS", "pC", "pF0", "pF1", "pF2", "pF3", "pG2", "pG3")
@@ -141,7 +142,7 @@ def rank_program(g, core, T, topo):
         free = {q: 0.0 for q in line}
         while len(out) < n:
             due, q = min((max(earliest[l[0]], free[q]), q) for q, l in line.items() if l and not left[l[0]])
-            fits = [j for j in line[q][1:AHEAD] if not left[j] and ops[j]["kind"] == "call"
+            fits = [j for j in line[q][1:AHEAD] if not left[j] and ops[j]["kind"] == "call" and (q != "v" or ops[j]["hold"] < 250)
                     and max(earliest[j], free[q]) < due and max(earliest[j], free[q]) + ops[j]["hold"] <= due + SLACK]
             i = fits[0] if fits else line[q][0]
             line[q].remove(i)
@@ -186,19 +187,19 @@ def rank_program(g, core, T, topo):
     def emit(q, fn, reads, writes, rate=1.0, n=None):
         n = size(writes[0]) if n is None else n
         if any(isinstance(r, list) for r in reads + writes):
-            hold = 60.0 + n * (3.8 if isinstance(writes[0], list) else 1.56)
+            hold = (60.0 if q == "v" else 80.0) + n * (3.8 if isinstance(writes[0], list) else 1.56)
         elif q == "v":
             both = all(r[0] not in PSUM for r in reads)
             hold = max(64.0, n * (rate if both else 1.0) * (1.0 if any(wide(r) for r in reads + writes if size(r) > 1) else 0.5))
         else:
-            hold = max(64.0, n * rate)
+            hold = max(64.0, n * rate) + 20.0 * (len(writes) - 1)
         record(q, "call", fn, [tuple(r) for r in reads], [tuple(r) for r in writes], hold)
 
-    def dma(q, out, in_, more=2500.0):
+    def dma(q, out, in_, more=3600.0):
         record(q, "dma", lambda: eng[q].dma_start(out[0], in_[0]), in_[1], out[1], 50.0, more)
 
     def send(out, in_, sem):
-        return record("p", "send", lambda: g.remote_dma(out, in_[0], T.sem[sem], T.sem.lsent, pid, rid, mask), in_[1], [], 1000.0)
+        return record("p", "send", lambda: g.remote_dma(out, in_[0], T.sem[sem], T.sem.lsent, pid, rid, mask), in_[1], [], 3000.0 if sem == "arx0" else 1000.0)
 
     def landing(sem, val, pieces, after, more):
         record("r", "landing", (sem, val), [], pieces, 0.0, more, after)
@@ -246,7 +247,7 @@ def rank_program(g, core, T, topo):
         emit("v", lambda: V.tensor_tensor_scan(out[0], d0[0], d1[0], first, op0, op1), rd(d0, d1), out[1])
 
     def listed(out, rep, n):
-        scan(out, rep, A("kt", 0, n), O.add, O.mult)
+        scan(out, A("kt", 0, n), rep, O.mult, O.add)
 
     def total(out, in_):
         emit("v", lambda: V.tensor_reduce(out[0], in_[0], AX.X, O.add), rd(in_), out[1])
@@ -273,7 +274,7 @@ def rank_program(g, core, T, topo):
 
     def mm(out, w, ws, x, xs, start=True, stop=True):
         record("t", "call" if start else "sum", lambda: g.tensor.matmul_mx(out[0], w[0], ws[0], x[0], xs[0], start, stop),
-               rd(w, ws, x, xs), out[1], 16.0 + size(out[1][0]))
+               rd(w, ws, x, xs), out[1], 14.0 + 0.85 * size(out[1][0]))
 
     def iota(out, pattern, base, cm, flag=False):
         kw = {"allow_small_or_imprecise_dtypes": True} if flag else {}
@@ -283,8 +284,8 @@ def rank_program(g, core, T, topo):
         record("p", "call", lambda: g.affine_select(out[0], in_[0], pattern, cmp, 0.0, base, cm), in_[1], out[1],
                170.0 + 2 * size(out[1][0]))
 
-    (kI, kType, kG, kB0, kB1, kB2, kB3, kOff, kSc, kBi, kBj, kP, kS, kS24, kK, kIb, kz) = [
-        A("col", k, k + 1) for k in range(17)]
+    (kI, kType, kG, kB0, kB1, kB2, kB3, kOff, kSc, kBi, kBj, kP, kS, kS24, kK, kIb, kz, kKm, kN) = [
+        A("col", k, k + 1) for k in range(19)]
     s16 = lambda k: A("s16", 16 * k, 16 * k + 16)
     row5 = (T.lrep[L:128:16, 0:2 * C], [("lrep", 0, 2 * C, 1)])
 
@@ -293,72 +294,79 @@ def rank_program(g, core, T, topo):
     dma("s", A("x0", 768, 1536), ext(T.x[:, 768:1536]))
     dma("a", A("llr", 0, 48), ext(T.nb[:, :]))
     dma("s", row5, ext(T.nb[:, :]))
-    dma("s", U8("qw", 0, 512), ext(T.wc[:, :]))
+    dma("s", U8("qw", 0, 512), (T.wc[:, :], [("x0", 0, 4 * C, 1)]))
     dma("s", A("sw", 0, 512), ext(T.ws[:, :]))
-    dma("s", A("vt", 0, 512), ext(T.v[:, :]))
+    dma("s", A("vt", 0, 512), ext(T.v[:, :]), 6000.0)
 
     iota(A("pi", 0, 1), [[1, 1]], 0, 1)
     iota(s16(0), [[1, 16]], 0, 0, True)
-    iota(A("idr", 0, C), [[1, C]], 0, 0, True)
     iota(A("li5", 0, 8), [[16, 8]], 0, 0)
+    ones, half, blocks = A("ones", 0, 512), A("bd1", 0, 512), A("bd", 0, 512)
+    fill(A("ones", 0, 516), 1.0)
+    choose(A("et", 0, 516), A("ones", 0, 516), [[1, 516]], O.is_equal, -3, -4)
+    iota(A("idr", 0, C), [[1, C]], 0, 0, True)
     iota(A("s16", 32, 47), [[32, PER], [1, L]], 1, 0, True)
     iota(A("li3", 0, 4), [[W3, 2], [16, 2]], 0, 0)
-    ones, half, blocks = A("ones", 0, 512), A("bd1", 0, 512), A("bd", 0, 512)
-    iota(ones, [[0, 512]], 1, 0, True)
     choose(half, ones, [[-16, 8], [0, 64]], O.is_ge, 0, 1)
     choose(blocks, half, [[16, 8], [0, 64]], O.is_ge, 15, -1)
     choose(A("bd", 512, 1024), blocks, [[-1, 128], [1000, 4]], O.is_ge, -1, 1)
+    iota(A("li2", 0, 24), [[16, 24]], 0, 0, True)
+    iota(A("li4", 0, 24), [[0, 4], [-16, 6]], TG - 1, 0, True)
 
     def later_on_g():
-        iota(A("li2", 0, 24), [[16, 24]], 0, 0, True)
-        iota(A("li4", 0, 24), [[0, 4], [-16, 6]], TG - 1, 0, True)
-        for b in range(4):
-            choose(A("et", 512 * b, 512 * b + 512), ones, [[4, 128], [1, 4]], O.is_equal, -b, -4)
         iota(A("posi", 0, C), [[1, 24], [48, 16]], 24, 0, True)
         for b in range(4):
             iota(A("db%d" % b, C, C + 16), [[0, 16]], 0, 0, True)
         iota(A("tab", 0, 25 * TG), [[0, 25 * TG]], 512, 0, True)
+        iota(A("one", 0, 24 * TG), [[0, 24 * TG]], 1, 0, True)
+        iota(A("one", 0, 24 * TG, TG), [[0, 24]], 4096, 0, True)
 
     def put(out, n, k):
         act(out, A("idr", 0, n), AF.Identity, bias=k, scale=0.0)
 
-    fill(s16(1), 0.0)
-    for k in range(1, L):
+    for k in range(L):
         rows = [r for r in range(16) if TYPES[r] == k]
         for a, b in zip(rows[0::2], rows[1::2] + [None]):
-            fill(A("s16", 16 + a, 16 + (b or a) + 1, b - a if b else 1), float(k))
+            act(A("s16", 16 + a, 16 + (b or a) + 1, b - a if b else 1), A("s16", 0, 2 if b else 1), AF.Identity,
+                bias=float(k), scale=0.0)
     ts(A("pi", 1, 2), A("pi", 0, 1), 15, O.bitwise_and)
     fill(A("s16", 47, 48), 0.0)
     tc(kI, A("pi", 1, 2))
     fill(A("r16b", 0, C), 1.0)
     ts(s16(3), s16(0), kI, O.subtract)
-    ts(A("irep", 0, 26), A("idr", 0, 26), 0.0, O.mult, kI, O.add)
+    ts(A("irep", 0, 24), A("ones", 0, 24), 0.0, O.mult, kI, O.add)
     ts(s16(4), s16(3), 0.0, O.is_equal)
-    ts(s16(5), s16(3), -1.0, O.not_equal)
-    ts(s16(6), s16(3), 15.0, O.not_equal, TINY, O.max)
-    ts(s16(7), s16(3), 0.0, O.is_equal, KB, O.mult)
+    ts(s16(6), s16(3), 0.0, O.not_equal)
+    ts(s16(7), s16(3), 1.0, O.is_equal, KB, O.mult)
     tt(s16(8), s16(4), s16(1), O.mult)
-    tt(s16(9), s16(5), s16(6), O.min)
+    tt(s16(10), s16(6), s16(7), O.max)
     total(kType, s16(8))
-    tt(s16(10), s16(9), s16(7), O.max)
+    ts(kKm, kI, 14.5, O.is_lt, KB - 1.0, O.mult)
     for k, bias in enumerate((kB0, kB1, kB2, kB3)):
         ts(bias, kType, L - 1.5 - k, O.is_lt, UP * (k + 2), O.mult)
-    act(A("w0", 0, C), A("idr", 0, C), AF.Identity, bias=UP)
     act(A("md", 0, C), I(s16(4), A("irep", 0, 24)))
+    act(A("kt", 0, C), I(s16(10), A("irep", 0, 24)))
+    act(A("w0", 0, C), A("idr", 0, C), AF.Identity, bias=UP)
     for k, bias in enumerate((kB0, kB1, kB2, kB3)):
         act(A("b%d" % k, 0, C), A("idr", 0, C), AF.Identity, bias=bias)
-    ts(kS, kI, 0.0, O.is_equal, 1.0 / (KB * TINY), O.mult)
+    ts(kS, kI, 14.5, O.is_gt, 1.0 / KB, O.max)
     put(A("f0", 0, 48, 2), 24, 0.0)
     tc(A("upl", 0, 8), A("li5", 0, 8))
-    ts(kS, kS, 1.0 / KB, O.max)
     ts(kOff, kType, UP, O.mult, -L * UP - 192.0, O.add)
     fill(A("r16b", 0, C, 16), 0.0)
     tc(A("blk", 0, 24), A("idr", 0, 24))
+    for b in range(4):
+        quant(A("qe", 128 * b, 128 * b + 128), A("se", 128 * b, 128 * b + 128), A("et", 3 - b, 515 - b))
     quant(A("qu0", 0, 128), A("su0", 0, 128), A("ut", 0, 512))
     tc(U32("qu", 0, 128), I(U32("qu0", 0, 128), A("upl", 0, 8)))
-    tc(A("su", 0, 128), I(A("su0", 0, 128), A("upl", 0, 8)))
+    act(A("su", 0, 128), I(A("su0", 0, 128), A("upl", 0, 8)))
 
-    S = A("pS", 0, C)
+    S = lambda a, e: A("pC" if a else "pS", 0, e - a)
+
+    def scores(t, a, e):
+        qx, sx, w = A("qx%d" % t, a, e), A("sx%d" % t, a, e), "v" if t == R else "u"
+        quant(qx, sx, A("x%d" % t, 4 * a, 4 * e))
+        mm(S(a, e), A("q" + w, 0, 128), A("s" + w, 0, 128), qx, sx)
 
     def planes(codes, plane, banks=PSUM[2:6]):
         for b in range(4):
@@ -374,8 +382,7 @@ def rank_program(g, core, T, topo):
                 put(A("d1k", e, 12 * NB, NB), 12, steps[e])
 
     def count_constants():
-        act(A("kt", 0, C), I(s16(10), A("irep", 0, 24)))
-        act(s16(5), s16(4), AF.Identity, bias=1.0, scale=UP - 1.0)
+        act(s16(5), s16(4), AF.Identity, bias=1.0, scale=kKm)
         put(A("s16", 80, 81), 1, 0.0)
         act(A("kp", 0, C), I(s16(5), A("irep", 0, 24)))
         put(A("cnt", 0, 1), 1, 0.0)
@@ -389,8 +396,9 @@ def rank_program(g, core, T, topo):
     def rank_constants():
         act(kSc, kI, AF.Sign)
         act(kz, kI, AF.Identity, bias=0.2)
-        act(kK, kSc, AF.Identity, bias=KB * TINY, scale=KB)
-        act(A("npos", 0, 24), A("li2", 0, 24), AF.Identity, bias=kz)
+        act(kK, kKm, AF.Identity, bias=1.0)
+        act(kN, kKm, AF.Identity, bias=-1.0, scale=-1.0)
+        act(A("npos", 0, 24), A("li2", 0, 24), AF.Identity, scale=kK)
 
     def slot_constants():
         act(kBj, kI, AF.Relu, bias=-192.0, scale=512.0)
@@ -405,24 +413,19 @@ def rank_program(g, core, T, topo):
             put(A("cm", 32 * u, 32 * u + n), n, 1.0 / HUGE)
         act(A("posc", 0, C), A("posi", 0, C), AF.Identity, bias=0.002, scale=1.0 / 24)
 
-    def search_constants():
-        for k in range(3):
-            put(A("one", C * k, C * k + C), C, 1.0)
-        put(A("one", 0, 12 * TG, TG), 12, 4096.0)
-
     trios = _trios()
     for t in range(R):
         last = t == R - 1
         qx, sx = A("qx%d" % t, 0, C), A("sx%d" % t, 0, C)
-        quant(qx, sx, A("x%d" % t, 0, 4 * C))
-        mm(S, A("qu", 0, 128), A("su", 0, 128), qx, sx)
+        if t == 0:
+            for a, e in HALVES:
+                scores(0, a, e)
         sent = [send(T["lc%d" % t][:, 0:C].bitcast(dt.uint8), U8("qx%d" % t, 0, C), "arx%d" % t),
                 send(T["ls%d" % t][:, 0:C], sx, "arx%d" % t)]
-        landing("arx%d" % t, 2 * width, [("lc%d" % t, 0, C, 1), ("ls%d" % t, 0, C, 1)], sent, 14000.0)
+        landing("arx%d" % t, 2 * width, [("lc%d" % t, 0, C, 1), ("ls%d" % t, 0, C, 1)], sent, 11000.0 if t == 0 else 16000.0)
         if t == 0:
             later_on_g()
-        else:
-            planes(qx, sx, OWN)
+        planes(qx, sx, OWN)
         ts(A("ll", 0, 48), A("llr", 0, 48), 511, O.bitwise_and)
         if t == 0:
             tt(s16(11), s16(4), s16(2), O.mult)
@@ -431,11 +434,13 @@ def rank_program(g, core, T, topo):
         tt(A("f0", 1, 48, 2), A("ll", 24, 48), A("ll", 0, 24), O.subtract)
         tc(A("f1", 1, 48, 2), A("ll", 0, 24))
         tc(A("lu", 0, 48), A("ll", 0, 48))
+        pick = lambda a, e: tt(A("smd", a, e), A("pC" if a >= 192 else "pS", a % 192, a % 192 + e - a), A("md", a, e), O.mult)
+        hold = lambda a, e: scan(A("sn", a, e), A("r16b", a, e), A("smd", a, e), O.mult, O.add)
         for a, e in HALVES:
-            tt(A("smd", a, e), A("pS", a, e), A("md", a, e), O.mult)
+            pick(a, e)
+            act(A("ssb", a, e), S(a, e))
         for a, e in HALVES:
-            scan(A("sn", a, e), A("r16b", a, e), A("smd", a, e), O.mult, O.add)
-        act(A("ssb", 0, C), S)
+            hold(a, e)
         ts(A("f1", 0, 48, 2), A("sn", 15, C, 16), 0.0, O.is_gt)
         scan(A("f2", 0, 48), A("f0", 0, 48), A("f1", 0, 48), O.mult, O.add)
         tc(A("cu", 0, 24), A("f2", 1, 48, 2))
@@ -445,23 +450,29 @@ def rank_program(g, core, T, topo):
             act(A("sp", 0, 768), I(A("ssb", 0, C), A("lu", 0, 48)))
         for k in range(4):
             tt(A("v%d" % k, 0, C), I(A("v%d" % (k - 1) if k else "w0", 0, C), A("cu", 0, 24)), A("b%d" % k, 0, C), O.max)
+            if t == 0 and k in (1, 2):
+                a = 128 * (k - 1)
+                quant(A("qbd", a, a + 128), A("sbd", a, a + 128), A("bd", 4 * a, 4 * a + 512))
         if t:
             act(A("fb0", 0, C), A("pF0", 0, C))
         else:
             put(A("z0", 0, C), C, 0.0)
             act(A("sp", 0, 768), I(A("ssb", 0, C), A("lu", 0, 48)))
         act(A("gg", 0, C), I(A("v3", 0, C), A("lu", 0, 24)), AF.Identity, bias=kOff)
-        ts(A("gg", C, 2 * C), I(A("v3", 0, C), A("lu", 24, 48)), kOff, O.add)
+        for a, e in ((0, 256), (256, C)):
+            ts(A("gg", C + a, C + e), I(A("v3", 0, C), A("lu", 24 + a // 16, 24 + e // 16)), kOff, O.add)
         if t == 0:
             count_constants()
             rank_constants()
-        turn((T.gt[:, 24:48, :], [("gt", C, 2 * C, 1)]), A("gg", C, 2 * C))
-        turn((T.gt[:, 0:24, :], [("gt", 0, C, 1)]), A("gg", 0, C))
+        for a, e in ((C, C + 256), (0, C), (C + 256, 2 * C)):
+            turn((T.gt[:, a // 16:e // 16, :], [("gt", a, e, 1)]), A("gg", a, e))
         if t:
             act(A("fb1", 0, C), A("pF1", 0, C))
         for x, ((r, s), (r2, s2)) in enumerate(trios):
             tt(A("ne", x, 24 * NB, NB // 3), (T.gt[:, 0:24, r:r + 2 * s + 1:s], [("gt", 0, C, 1)]),
                (T.gt[:, 24:48, r2:r2 + 2 * s2 + 1:s2], [("gt", C, 2 * C, 1)]), O.not_equal)
+        if t == 0:
+            quant(A("qv", 0, 128), A("sv", 0, 128), A("vt", 0, 512))
         for a, e in HALVES:
             a, e = a // 16 * NB, e // 16 * NB
             scan(A("st", a, e), A("ne", a, e), A("d1k", 0, e - a), O.mult, O.add, -100.0)
@@ -473,12 +484,9 @@ def rank_program(g, core, T, topo):
             turn(A("kr", a, e), A("ex", a, e))
         for a, e in HALVES:
             listed(A("sk", a, e), A("kr", a, e), e - a)
-        tt(A("ms", 0, 192), A("pS", 0, 192), A("kr", 0, 192), O.min)
-        ts(A("t1", 0, 24), A("sk", 15, C, 16), kS, O.mult, -HUGE / 8, O.max)
-        tt(A("ms", 192, C), A("pS", 192, C), A("kr", 192, C), O.min)
-        tt(A("slm", 0, 24), A("t1", 0, 24), A("sn", 15, C, 16), O.min)
-        if t == 0:
-            quant(A("qbd", 0, 256), A("sbd", 0, 256), A("bd", 0, 1024))
+        tt(A("ms", 0, 192), S(0, 192), A("kr", 0, 192), O.min)
+        tt(A("slm", 0, 24), A("sk", 15, C, 16), A("sn", 15, C, 16), O.min)
+        tt(A("ms", 192, C), S(192, C), A("kr", 192, C), O.min)
         spot, at = {}, 0
         for rows, w in TILES:
             for i, c in enumerate(rows):
@@ -489,7 +497,7 @@ def rank_program(g, core, T, topo):
         for c in AROWS:
             act(sg(c), A("ms", 0, 16 * c), AF.Sign, bias=score(c), scale=-1.0)
         for c in AROWS:
-            act(spot[c], sg(c), AF.Relu, accum=A("cnt", c, c + 1))
+            act(spot[c], sg(c), AF.Relu, accum=A("cna", c, c + 1))
         at, sums = 0, []
 
         def column_sums(k, at, w):
@@ -503,26 +511,23 @@ def rank_program(g, core, T, topo):
                     tt(spot[c], I(A("slm", 0, 24), A("blk", 0, 24)), A("ms", 0, C), O.is_gt)
                 elif c not in AROWS:
                     ts(spot[c], A("ms", 0, 16 * c), score(c), O.is_lt)
-                    act(A("junk", C * (c % 4), C * (c % 4) + 16 * c), spot[c], accum=A("cnt", c, c + 1))
+                    act(A("junk", C * (c % 4), C * (c % 4) + 16 * c), spot[c], AF.Identity, scale=kN, bias=kK, accum=A("cnt", c, c + 1))
                 if sums and c not in AROWS:
-                    column_sums(*sums.pop())
+                    column_sums(*sums.pop(0))
+            for c in AROWS if k == 2 else ():
+                act(A("cnt", c, c + 1), A("cna", c, c + 1), AF.Identity, scale=kN, bias=A("npos", c, c + 1))
             sums.append((k, at, w))
             at += 4 * w
-        scan(A("eqs", 0, C), A("kp", 0, C), spot[24], O.mult, O.add)
         column_sums(*sums.pop())
-        ts(A("pre", 0, 24), A("eqs", 15, C, 16), -1.0 / UP, O.mult)
+        scan(A("eqs", 0, C), A("kp", 0, C), spot[24], O.mult, O.add)
         if t == 0:
-            quant(A("qe", 0, 512), A("se", 0, 512), A("et", 0, 2048))
-            planes(qx, sx, OWN)
             slot_constants()
             for b in range(2):
                 act(A("fb%d" % b, 0, C), A("pF%d" % b, 0, C))
-        tt(A("rk2", 0, 24), A("npos", 0, 24), A("cnt", 0, 24), O.subtract)
-        tt(A("rk", 0, 24), A("rk2", 0, 24), A("pre", 0, 24), O.add)
-        ts(A("rk3", 0, 24), A("rk", 0, 24), kK, O.mult)
         listed(A("cs", 0, C), A("pC", 0, C), C)
+        tt(A("rk3", 0, 24), A("cnt", 0, 24), A("eqs", 15, C, 16), O.subtract)
         tt(A("rk", 0, 24), A("rk3", 0, 24), A("cs", 15, C, 16), O.add)
-        ts(A("rku", 0, 24), A("rk", 0, 24), kS, O.mult)
+        ts(A("rku", 0, 24), A("rk", 0, 24), kS, O.mult, kz, O.add)
         scatter(A("order", 0, C), A("rku", 0, 24), A("idr", 0, C))
         if t == 0:
             ts(A("fin", 0, 4), A("li3", 0, 4), kG, O.add)
@@ -537,8 +542,6 @@ def rank_program(g, core, T, topo):
             act(A("hf", W3 * h, W3 * h + W3), I(A("gg", C * h, C * h + C), ou), AF.Identity, bias=kBi, scale=kSc)
         if t == 0:
             act(s16(9), s16(4), AF.Identity, bias=512.0, scale=-512.0)
-        for b in range(2 if t == 0 else 4):
-            act(A("db%d" % b, 0, C), A("pF%d" % b, 0, C), scale=0.5)
         kai, on = A("kai", 0, W3), A("hb", 2 * W3, 3 * W3)
         tt(kai, I(A("kr", 0, C), ou), A("cm", 0, W3), O.mult)
         ts(A("jm", 0, W3), kai, 7, O.bitwise_and)
@@ -548,36 +551,37 @@ def rank_program(g, core, T, topo):
         turn(A("hbt", 0, 2 * W3), A("hb", 0, 2 * W3))
         turn(A("hbt", 2 * W3, 3 * W3), on)
         turn(A("hft", 0, 2 * W3), A("hf", 0, 2 * W3))
-        ts(A("lt", 64, 96), I(A("hbt", 2 * W3, 3 * W3), A("fin", 0, 2)), 8192.0, O.mult, -4096.0, O.add)
+        act(A("lt", 64, 96), I(A("hbt", 2 * W3, 3 * W3), A("fin", 0, 2)), AF.Identity, bias=-4096.0, scale=8192.0)
+        for b in range(3 if t else 2):
+            act(A("db%d" % b, 0, C), A("pF%d" % b, 0, C), scale=0.5)
         scan(A("ab", 0, 2 * W3), A("hbt", 0, 2 * W3), A("hft", 0, 2 * W3), O.max, O.min)
+        ts(A("inv", 0, W3), kai, 0.0, O.is_equal, 43.0, O.mult)
+        tc(A("lh", 0, 64), I(A("ab", 0, 2 * W3), A("fin", 0, 4)))
+        tt(A("wv", 0, W3), A("inv", 0, W3), on, O.subtract)
+        turn(A("li", 0, 64), A("lh", 0, 64))
         turn(A("ltt", 64, 96), A("lt", 64, 96))
-        tc(A("lt", 0, 64), I(A("ab", 0, 2 * W3), A("fin", 0, 4)))
-        turn(A("ltt", 0, 64), A("lt", 0, 64))
-        tc(A("li", 0, 64), A("ltt", 0, 64))
-        tt(A("bd0", 0, NC), A("ltt", 32, 32 + NC), A("ltt", 64, 64 + NC), O.add)
+        tt(A("bd0", 0, NC), A("li", 32, 32 + NC), A("ltt", 64, 64 + NC), O.add)
         ts(A("lj", 0, 64), A("li", 0, 64), 511, O.bitwise_and)
-        tt(A("bt", 0, NC), A("bd0", 0, NC), A("ltt", 0, NC), O.max)
+        tt(A("bt", 0, NC), A("bd0", 0, NC), A("li", 0, NC), O.max)
         tc(A("own%d" % t, 0, 64), A("lj", 0, 64))
         ts(A("bl", 0, NC), A("bt", 0, NC), 15, O.bitwise_and)
         ts(A("bh", 0, NC), A("bt", 0, NC), 496, O.bitwise_and)
         tc(A("bu", 0, NC), A("bl", 0, NC))
         tt(A("bo", 0, NC), A("bh", 0, NC), A("tagq", 0, NC), O.add)
         sent = [send(T["came%d" % t][:, 0:32 + NC], A("own%d" % t, 0, 32 + NC), "arl%d" % t)]
-        landing("arl%d" % t, width, [("came%d" % t, 0, 64, 1)], sent, 2500.0)
+        landing("arl%d" % t, width, [("came%d" % t, 0, 64, 1)], sent, 1400.0)
         parts = [(a, min(a + TG // 16, NC)) for a in range(0, NC, TG // 16)]
         for a, e in parts:
             act(A("val", 16 * a, 16 * e), I(s16(9), A("bu", a, e)), AF.Identity, bias=16.0 * a - UP * t)
-        if t == 0:
-            for b in range(2, 4):
-                act(A("db%d" % b, 0, C), A("pF%d" % b, 0, C), scale=0.5)
-        between = [lambda: tt(A("wv", 0, W3), A("inv", 0, W3), on, O.subtract),
-                   lambda: tt(A("ix", 0, W3), I(A("posc", 0, C), ou), A("wv", 0, W3), O.add),
+        for b in range(3 if t else 2, 4):
+            act(A("db%d" % b, 0, C), A("pF%d" % b, 0, C), scale=0.5)
+        between = [lambda: tt(A("ix", 0, W3), I(A("posc", 0, C), ou), A("wv", 0, W3), O.add),
                    lambda: listed(A("iy", 0, W3), A("ix", 0, W3), W3),
                    lambda: ts(A("pu", 0, 6), A("iy", 15, W3, 16), kS24, O.mult),
                    lambda: turn(A("mrow", 0, W3), A("ab", 0, W3)),
                    lambda: scatter(A("lrep", 0, 1800), A("pu", 0, 6), A("mrow", 0, W3)),
-                   lambda: dma("s", A("llr", 0, 48), row5)]
-        ts(A("inv", 0, W3), kai, 0.0, O.is_equal, 43.0, O.mult)
+                   lambda: dma("s", A("llr", 0, 48), row5, 2600.0),
+                   lambda: None]
         ts(A("ofu", 0, NC), A("bo", 0, NC), TG / 16.0, O.mult)
         tab = A("tab", 0, 25 * TG)
         for a, e in parts:
@@ -587,22 +591,23 @@ def rank_program(g, core, T, topo):
                 tt(A("tmp", 16 * a, 16 * e), I(tab, A("ofu", a, e)), val, O.min)
                 val = A("tmp", 16 * a, 16 * e)
             between.pop(0)()
-            scatter(tab, A("ofu", a, e), val)
+            if e < NC:
+                scatter(tab, A("ofu", a, e), val)
         for b in range(4):
             z, win = A("za", SL * b, SL * b + SL), A("db%d" % b, 0, C + 16)
             act(z, I(win, A("came%d" % t, 0, NC)))
-            tt(A("zt", b, 4 * SL, 4), I(win, A("came%d" % t, 32, 32 + NC)), z, O.add)
-        if t == 0:
-            search_constants()
+            if b == 1:
+                scatter(tab, A("ofu", a, e), val)
+            if b < 4 - ZA:
+                tt(A("zt", b, 4 * SL, 4), I(win, A("came%d" % t, 32, 32 + NC)), z, O.add)
+            else:
+                act(A("zb", SL * (3 - b), SL * (4 - b)), I(win, A("came%d" % t, 32, 32 + NC)))
+                tt(A("zt", b, 4 * SL, 4), A("zb", SL * (3 - b), SL * (4 - b)), z, O.add)
         quant(A("qz", 0, SL), A("sz", 0, SL), A("zt", 0, 4 * SL))
         for b in range(4):
             mm(A("pF%d" % b, 0, SL), A("qw", 128 * b, 128 * b + 128), A("sw", 128 * b, 128 * b + 128),
                A("qz", 0, SL), A("sz", 0, SL))
-        for k in range(2):
-            a, e = 12 * TG * k, 12 * TG * (k + 1)
-            scan(A("ste", a, e), A("one", 0, 12 * TG), A("tab", a, e), O.add, O.min)
-        if t == 0:
-            quant(A("qv", 0, 128), A("sv", 0, 128), A("vt", 0, 512))
+        scan(A("ste", 0, 24 * TG), A("one", 0, 24 * TG), A("tab", 0, 24 * TG), O.add, O.min)
         ts(A("eu", 0, 24), A("ste", TG - 1, 24 * TG, TG), UP * t, O.add, SL - 1.0, O.min)
         if last:
             ts(A("ll", 0, 48), A("llr", 0, 48), 511, O.bitwise_and)
@@ -617,21 +622,24 @@ def rank_program(g, core, T, topo):
                         (T.lot[32 * a:32 * a + 16, 32 + 16 * h:48 + 16 * h], [("lot", 32, 64, 1)]))
         for b in range(4):
             act(A("hs%d" % b, 0, SL), A("pF%d" % b, 0, SL), scale=0.03125)
-        for a, e in ((0, 256), (256, C)) if last else ((0, C),):
-            for b in range(4):
-                x, h = A("x%d" % (t + 1), 4 * a + b, 4 * e, 4), I(A("hs%d" % b, 0, SL), A("eu", a // 16, e // 16))
-                if b < 2:
-                    tt(x, h, A("fb%d" % b, a, e), O.add)
-                else:
-                    act(A("ga%d" % b, a, e), h)
-                    tt(x, A(OWN[b], a, e), A("ga%d" % b, a, e), O.add)
-            if last:
-                qx, sx, bank = A("qx%d" % R, a, e), A("sx%d" % R, a, e), A("pC" if a else "pS", 0, e - a)
-                quant(qx, sx, A("x%d" % R, 4 * a, 4 * e))
-                mm(bank, A("qv", 0, 128), A("sv", 0, 128), qx, sx)
-                dma("s", ext(T.oc[:, 4 * a:4 * e]), U8("qx%d" % R, a, e))
-                act(A("ys", a, e), bank)
-                dma("a", ext(T.y[:, a:e]), A("ys", a, e))
+        pieces = ((0, 256), (256, C)) if last else HALVES
+        x = lambda b, a, e: A("x%d" % (t + 1), 4 * a + b, 4 * e, 4)
+        h = lambda b, a, e: I(A("hs%d" % b, 0, SL), A("eu", a // 16, e // 16))
+        for a, e in pieces:
+            for b in range(2):
+                act(A("ga%d" % (b + 2), a, e), h(b + 2, a, e))
+        for b, k in ((0, 0), (1, 0), (0, 1), (1, 1), (2, 0), (3, 0), (2, 1), (4, 0), (3, 1), (4, 1)):
+            a, e = pieces[k]
+            if b < 2:
+                tt(x(b, a, e), h(b, a, e), A("fb%d" % b, a, e), O.add)
+            elif b < 4:
+                tt(x(b, a, e), A(OWN[b], a, e), A("ga%d" % b, a, e), O.add)
+            else:
+                scores(t + 1, a, e)
+        for a, e in pieces if last else ():
+            dma("s", ext(T.oc[:, 4 * a:4 * e]), U8("qx%d" % R, a, e))
+            act(A("ys", a, e), S(a, e))
+            dma("a", ext(T.y[:, a:e]), A("ys", a, e))
 
     for k in range(4):
         dma("s", ext(T.osc[4 * k:4 * k + 4, :]), (T["sx%d" % R][32 * k:32 * k + 4, 0:C], [("sx%d" % R, 0, C, 1)]))

@@ -52,8 +52,8 @@ def _pool(pool, dtype, spec):
 
 
 _own(BF, "x0:1536 x1:1536 x2:1536 x3:1536 ut:512 vt:512 et:516 ones:516 za:1408 zb:704 zt:1408")
-_own(BF, "fb0:384 fb1:384 db0:400 db1:400 db2:400 db3:400 bd:1024 bd1:512 mt:5632")
-_own(F32, "hs0:352 hs1:352 hs2:352 hs3:352 ga2:384 ga3:384 ys:384 lot:64")
+_own(BF, "fb0:384 fb1:384 fb2:384 fb3:384 db0:400 db1:400 db2:400 db3:400 bd:1024 bd1:512 mt:5632")
+_own(F32, "hs0:352 hs1:352 hs2:352 hs3:352 ga1:384 ga2:384 ga3:384 ys:384 lot:64")
 _own(I32, "llr:48 lrep:1824")
 for _n, _k in (("w", 512), ("v", 128), ("u0", 128), ("u", 128), ("e", 512), ("z", SL), ("bd", 256), ("m", 1408)):
     _own(COD, "q%s:%d" % (_n, _k))
@@ -70,17 +70,30 @@ _pool("poolf", F32, "col:32 s16:192 idr:384 posi:384 posc:384 b0:384 b1:384 b2:3
       "npos:24 tagq:24 cm:96 f0:48 f1:48 f2:48 li2:24 li4:24 v0:384 v1:384 v2:384 v3:384 ssb:384 sp:768 ms:384 "
       "cnt:24 cna:24 rk:24 rk2:24 rk3:24 cs:384 order:384 ol:96 sc:192 hf:192 hft:192 ab:192 lt:96 ltt:96 bd0:24 bd2:24 bo:24 "
       "ix:96 iy:96 mrow:96 lo:64")
-_pool("poolb", BF, "kt:384 r16b:384 md:384 sgn:384 kp:384 sk:384 gg:768 d1k:324 ne:648 st:648 z0:384 ex:384 kr:384 sg:1536 "
-      "eqs:384 junk:1536 hb:288 hbt:288 inv:96 wv:96 val:384 tmp:384 tab:2400 one:2304")
+_pool("poolb", BF, "kt:384 r16b:384 md:384 sgn:384 kp:384 sk:384 gg:768 d1k:324 ne:648 st:648 z0:384 ex:384 kr:384 sg:2304 "
+      "eqs:384 junk:1536 hb:288 hbt:288 inv:96 wv:96 val:384 tmp:384")
+_own(BF, "tab:3200 one:3072")
 _pool("pooli", I32, "pi:2 li5:8 li3:4 ll:48 kai:96 jm:96 lh:64 li:64 lj:64 bt:24 bh:24 bl:24")
-_pool("poolu", U16, "upl:8 irep:26 blk:24 fin:4 lu:48 cu:24 rku:24 ou:6 pu:6 bu:24 ofu:24 eu:24")
-_pool("poolh", F16, "ste:2304")
+_pool("poolu", U16, "upl:8 irep:26 blk:24 fin:4 lu:48 cu:24 c2u:24 rku:24 ou:6 pu:6 bu:24 ofu:24 eu:24")
+_pool("poolh", F16, "ste:3072")
 PSUM = ("pS", "pC", "pF0", "pF1", "pF2", "pF3", "pG2", "pG3")
 OWN = ("pF0", "pF1", "pG2", "pG3")
 HALVES = ((0, 192), (192, C))
+PIECES = ((0, 256), (256, C))
+LATE = (200.0, 0.0)
+VV = 0
+SLOTS = "s0 s1 p q kai jm keepp keepq on hbt ont hft inv lt db ab wv lh ltt li lj bd0 own bt bl bh bu bo"
+SEARCH = "ofu ix s0 iy mrow l1 pu s1 links back l2 s2 z0 l3 z1 s3 z2 z3"
+PE = 1.0
+LASTP = ((0, 256), (256, C))
+DB = 2
+CUT = 384
+CROSS = 110.0
+GA = ((2, 0), (3, 0), (2, 1))
+STATE = ((0, 2), (1, 2), (2, 0), (3, 0), (3, 1), (4, 0), (2, 1), (4, 1))
 for _n in PSUM:
     SCRATCH[_n] = ("psum", [128, 512], F32)
-NDMA = 40
+NDMA = 44
 SEMAPHORES = (["qv_", "qa_", "qt_", "qp_", "lsent"] + ["arx%d" % t for t in range(R)] + ["arl%d" % t for t in range(R)]
               + ["d%d" % k for k in range(NDMA)])
 
@@ -97,7 +110,7 @@ def rank_program(g, core, T, topo):
     semof = {"v": "qv_", "a": "qa_", "t": "qt_", "p": "qp_"}
     count, known = {}, {q: {} for q in eng}
     clocks, hist, ops = {}, {}, []
-    ndma = [0]
+    ndma, stay, late = [0], [False], [False]
 
     def need(q, src, val):
         if known[q].get(src, 0) >= val:
@@ -108,7 +121,9 @@ def rank_program(g, core, T, topo):
                 known[q][s] = n
 
     def meet(x, y):
-        return x[0] < y[1] and y[0] < x[1] and not (x[2] == y[2] and (x[0] - y[0]) % x[2])
+        if x[0] >= y[1] or y[0] >= x[1] or x[2] == y[2] and (x[0] - y[0]) % x[2]:
+            return False
+        return min(x[2], y[2]) == 1 and max(x[1] - x[0], y[1] - y[0]) > 32 or bool(set(range(*x)) & set(range(*y)))
 
     def covers(x, y):
         return x[0] <= y[0] and y[1] <= x[1] and (x[2] == 1 or x[2] == y[2] and (x[0] - y[0]) % x[2] == 0)
@@ -149,7 +164,7 @@ def rank_program(g, core, T, topo):
             out.append(i)
             free[q] = max(earliest[i], free[q]) + ops[i]["hold"]
             for j in users[i]:
-                earliest[j] = max(earliest[j], free[q] + ops[i]["more"] + (WAKE if ops[j]["deps"][i] else 0.0))
+                earliest[j] = max(earliest[j], free[q] + ops[i]["more"] + ((WAKE if ops[j]["q"] == q else CROSS) if ops[j]["deps"][i] else 0.0))
                 left[j] -= 1
         return out
 
@@ -193,7 +208,8 @@ def rank_program(g, core, T, topo):
             hold = max(64.0, n * (rate if both else 1.0) * (1.0 if any(wide(r) for r in reads + writes if size(r) > 1) else 0.5))
         else:
             hold = max(64.0, n * rate) + 20.0 * (len(writes) - 1)
-        record(q, "call", fn, [tuple(r) for r in reads], [tuple(r) for r in writes], hold)
+        more = LATE[0] if isinstance(writes[0], list) else LATE[1] if any(isinstance(r, list) for r in reads) else 0.0
+        record(q, "kept" if stay[0] and q == "v" or late[0] else "call", fn, [tuple(r) for r in reads], [tuple(r) for r in writes], hold, more)
 
     def dma(q, out, in_, more=3600.0):
         record(q, "dma", lambda: eng[q].dma_start(out[0], in_[0]), in_[1], out[1], 50.0, more)
@@ -274,11 +290,11 @@ def rank_program(g, core, T, topo):
 
     def mm(out, w, ws, x, xs, start=True, stop=True):
         record("t", "call" if start else "sum", lambda: g.tensor.matmul_mx(out[0], w[0], ws[0], x[0], xs[0], start, stop),
-               rd(w, ws, x, xs), out[1], 14.0 + 0.85 * size(out[1][0]))
+               rd(w, ws, x, xs), out[1], PE * (16 + size(out[1][0])))
 
     def iota(out, pattern, base, cm, flag=False):
         kw = {"allow_small_or_imprecise_dtypes": True} if flag else {}
-        record("p", "call", lambda: g.iota(out[0], pattern, base, cm, **kw), [], out[1], 130.0 + 2 * size(out[1][0]))
+        record("p", "kept" if stay[0] else "call", lambda: g.iota(out[0], pattern, base, cm, **kw), [], out[1], 130.0 + 2 * size(out[1][0]))
 
     def choose(out, in_, pattern, cmp, base, cm):
         record("p", "call", lambda: g.affine_select(out[0], in_[0], pattern, cmp, 0.0, base, cm), in_[1], out[1],
@@ -289,10 +305,10 @@ def rank_program(g, core, T, topo):
     s16 = lambda k: A("s16", 16 * k, 16 * k + 16)
     row5 = (T.lrep[L:128:16, 0:2 * C], [("lrep", 0, 2 * C, 1)])
 
-    dma("s", A("ut", 0, 512), ext(T.u[:, :]))
-    dma("a", A("x0", 0, 768), ext(T.x[:, 0:768]))
-    dma("s", A("x0", 768, 1536), ext(T.x[:, 768:1536]))
-    dma("a", A("llr", 0, 48), ext(T.nb[:, :]))
+    dma("s", A("ut", 0, 512), ext(T.u[:, :]), 1500.0)
+    for q, (a, e) in zip("as", PIECES):
+        dma(q, A("x0", 4 * a, 4 * e), ext(T.x[:, 4 * a:4 * e]), 2000.0)
+    dma("a", A("llr", 0, 48), ext(T.nb[:, :]), 2400.0)
     dma("s", row5, ext(T.nb[:, :]))
     dma("s", U8("qw", 0, 512), (T.wc[:, :], [("x0", 0, 4 * C, 1)]))
     dma("s", A("sw", 0, 512), ext(T.ws[:, :]))
@@ -302,24 +318,24 @@ def rank_program(g, core, T, topo):
     iota(s16(0), [[1, 16]], 0, 0, True)
     iota(A("li5", 0, 8), [[16, 8]], 0, 0)
     ones, half, blocks = A("ones", 0, 512), A("bd1", 0, 512), A("bd", 0, 512)
-    fill(A("ones", 0, 516), 1.0)
-    choose(A("et", 0, 516), A("ones", 0, 516), [[1, 516]], O.is_equal, -3, -4)
     iota(A("idr", 0, C), [[1, C]], 0, 0, True)
+    iota(A("ones", 0, 516), [[0, 516]], 1, 0, True)
+    choose(A("et", 0, 516), A("ones", 0, 516), [[1, 516]], O.is_equal, -3, -4)
     iota(A("s16", 32, 47), [[32, PER], [1, L]], 1, 0, True)
     iota(A("li3", 0, 4), [[W3, 2], [16, 2]], 0, 0)
     choose(half, ones, [[-16, 8], [0, 64]], O.is_ge, 0, 1)
     choose(blocks, half, [[16, 8], [0, 64]], O.is_ge, 15, -1)
     choose(A("bd", 512, 1024), blocks, [[-1, 128], [1000, 4]], O.is_ge, -1, 1)
     iota(A("li2", 0, 24), [[16, 24]], 0, 0, True)
-    iota(A("li4", 0, 24), [[0, 4], [-16, 6]], TG - 1, 0, True)
+    iota(A("li4", 0, 24), [[0, 384 // TG], [-16, TG // 16]], TG - 1, 0, True)
 
     def later_on_g():
         iota(A("posi", 0, C), [[1, 24], [48, 16]], 24, 0, True)
         for b in range(4):
             iota(A("db%d" % b, C, C + 16), [[0, 16]], 0, 0, True)
         iota(A("tab", 0, 25 * TG), [[0, 25 * TG]], 512, 0, True)
-        iota(A("one", 0, 24 * TG), [[0, 24 * TG]], 1, 0, True)
-        iota(A("one", 0, 24 * TG, TG), [[0, 24]], 4096, 0, True)
+        iota(A("one", 0, 12 * TG), [[0, 12 * TG]], 1, 0, True)
+        iota(A("one", 0, 12 * TG, TG), [[0, 12]], 4096, 0, True)
 
     def put(out, n, k):
         act(out, A("idr", 0, n), AF.Identity, bias=k, scale=0.0)
@@ -329,37 +345,44 @@ def rank_program(g, core, T, topo):
         for a, b in zip(rows[0::2], rows[1::2] + [None]):
             act(A("s16", 16 + a, 16 + (b or a) + 1, b - a if b else 1), A("s16", 0, 2 if b else 1), AF.Identity,
                 bias=float(k), scale=0.0)
-    ts(A("pi", 1, 2), A("pi", 0, 1), 15, O.bitwise_and)
-    fill(A("s16", 47, 48), 0.0)
-    tc(kI, A("pi", 1, 2))
     fill(A("r16b", 0, C), 1.0)
+    ts(A("pi", 1, 2), A("pi", 0, 1), 15, O.bitwise_and)
+    tc(kI, A("pi", 1, 2))
+    tc(A("upl", 0, 8), A("li5", 0, 8))
+    ts(s16(4), s16(0), kI, O.is_equal)
+    ts(A("irep", 0, 24), A("r16b", 0, 24), 0.0, O.mult, kI, O.add)
     ts(s16(3), s16(0), kI, O.subtract)
-    ts(A("irep", 0, 24), A("ones", 0, 24), 0.0, O.mult, kI, O.add)
-    ts(s16(4), s16(3), 0.0, O.is_equal)
-    ts(s16(6), s16(3), 0.0, O.not_equal)
-    ts(s16(7), s16(3), 1.0, O.is_equal, KB, O.mult)
-    tt(s16(8), s16(4), s16(1), O.mult)
-    tt(s16(10), s16(6), s16(7), O.max)
-    total(kType, s16(8))
-    ts(kKm, kI, 14.5, O.is_lt, KB - 1.0, O.mult)
-    for k, bias in enumerate((kB0, kB1, kB2, kB3)):
-        ts(bias, kType, L - 1.5 - k, O.is_lt, UP * (k + 2), O.mult)
     act(A("md", 0, C), I(s16(4), A("irep", 0, 24)))
-    act(A("kt", 0, C), I(s16(10), A("irep", 0, 24)))
+    fill(A("r16b", 0, C, 16), 0.0)
+    tt(s16(8), s16(4), s16(1), O.mult)
+    fill(A("d1k", 0, 12 * NB), 7.0)
+    total(kType, s16(8))
     act(A("w0", 0, C), A("idr", 0, C), AF.Identity, bias=UP)
     for k, bias in enumerate((kB0, kB1, kB2, kB3)):
-        act(A("b%d" % k, 0, C), A("idr", 0, C), AF.Identity, bias=bias)
-    ts(kS, kI, 14.5, O.is_gt, 1.0 / KB, O.max)
-    put(A("f0", 0, 48, 2), 24, 0.0)
-    tc(A("upl", 0, 8), A("li5", 0, 8))
-    ts(kOff, kType, UP, O.mult, -L * UP - 192.0, O.add)
-    fill(A("r16b", 0, C, 16), 0.0)
-    tc(A("blk", 0, 24), A("idr", 0, 24))
-    for b in range(4):
-        quant(A("qe", 128 * b, 128 * b + 128), A("se", 128 * b, 128 * b + 128), A("et", 3 - b, 515 - b))
+        ts(bias, kType, L - 1.5 - k, O.is_lt, UP * (k + 2), O.mult)
+
+    def step_constants():
+        put(A("f0", 0, 48, 2), 24, 0.0)
+        for k, bias in enumerate((kB0, kB1, kB2, kB3)):
+            act(A("b%d" % k, 0, C), A("idr", 0, C), AF.Identity, bias=bias)
+
+    def small_constants():
+        ts(s16(6), s16(3), 0.0, O.not_equal)
+        ts(s16(7), s16(3), 1.0, O.is_equal, KB, O.mult)
+        ts(kKm, kI, 14.5, O.is_lt, KB - 1.0, O.mult)
+        tt(s16(10), s16(6), s16(7), O.max)
+        ts(kOff, kType, UP, O.mult, -L * UP - 192.0, O.add)
+        ts(kS, kI, 14.5, O.is_gt, 1.0 / KB, O.max)
+
+    def late_constants():
+        fill(A("s16", 47, 48), 0.0)
+        tt(s16(11), s16(4), s16(2), O.mult)
+        total(kG, s16(11))
+
     quant(A("qu0", 0, 128), A("su0", 0, 128), A("ut", 0, 512))
     tc(U32("qu", 0, 128), I(U32("qu0", 0, 128), A("upl", 0, 8)))
     act(A("su", 0, 128), I(A("su0", 0, 128), A("upl", 0, 8)))
+    unpacking = lambda b: quant(A("qe", 128 * b, 128 * b + 128), A("se", 128 * b, 128 * b + 128), A("et", 3 - b, 515 - b))
 
     S = lambda a, e: A("pC" if a else "pS", 0, e - a)
 
@@ -382,6 +405,7 @@ def rank_program(g, core, T, topo):
                 put(A("d1k", e, 12 * NB, NB), 12, steps[e])
 
     def count_constants():
+        act(A("kt", 0, C), I(s16(10), A("irep", 0, 24)))
         act(s16(5), s16(4), AF.Identity, bias=1.0, scale=kKm)
         put(A("s16", 80, 81), 1, 0.0)
         act(A("kp", 0, C), I(s16(5), A("irep", 0, 24)))
@@ -418,61 +442,62 @@ def rank_program(g, core, T, topo):
         last = t == R - 1
         qx, sx = A("qx%d" % t, 0, C), A("sx%d" % t, 0, C)
         if t == 0:
-            for a, e in HALVES:
+            for a, e in PIECES:
                 scores(0, a, e)
+            step_constants()
         sent = [send(T["lc%d" % t][:, 0:C].bitcast(dt.uint8), U8("qx%d" % t, 0, C), "arx%d" % t),
                 send(T["ls%d" % t][:, 0:C], sx, "arx%d" % t)]
-        landing("arx%d" % t, 2 * width, [("lc%d" % t, 0, C, 1), ("ls%d" % t, 0, C, 1)], sent, 11000.0 if t == 0 else 16000.0)
+        landing("arx%d" % t, 2 * width, [("lc%d" % t, 0, C, 1), ("ls%d" % t, 0, C, 1)], sent, 11000.0 if t else 8500.0)
         if t == 0:
             later_on_g()
-        planes(qx, sx, OWN)
+        else:
+            planes(qx, sx, OWN)
         ts(A("ll", 0, 48), A("llr", 0, 48), 511, O.bitwise_and)
-        if t == 0:
-            tt(s16(11), s16(4), s16(2), O.mult)
-            fill(A("d1k", 0, 12 * NB), 7.0)
-            total(kG, s16(11))
         tt(A("f0", 1, 48, 2), A("ll", 24, 48), A("ll", 0, 24), O.subtract)
         tc(A("f1", 1, 48, 2), A("ll", 0, 24))
         tc(A("lu", 0, 48), A("ll", 0, 48))
-        pick = lambda a, e: tt(A("smd", a, e), A("pC" if a >= 192 else "pS", a % 192, a % 192 + e - a), A("md", a, e), O.mult)
-        hold = lambda a, e: scan(A("sn", a, e), A("r16b", a, e), A("smd", a, e), O.mult, O.add)
-        for a, e in HALVES:
-            pick(a, e)
+        for a, e in PIECES:
+            tt(A("smd", a, e), S(a, e), A("md", a, e), O.mult)
             act(A("ssb", a, e), S(a, e))
-        for a, e in HALVES:
-            hold(a, e)
+        for a, e in PIECES:
+            scan(A("sn", a, e), A("r16b", a, e), A("smd", a, e), O.mult, O.add)
         ts(A("f1", 0, 48, 2), A("sn", 15, C, 16), 0.0, O.is_gt)
         scan(A("f2", 0, 48), A("f0", 0, 48), A("f1", 0, 48), O.mult, O.add)
         tc(A("cu", 0, 24), A("f2", 1, 48, 2))
         if t == 0:
             meeting_constants()
+            put(A("z0", 0, C), C, 0.0)
         else:
             act(A("sp", 0, 768), I(A("ssb", 0, C), A("lu", 0, 48)))
         for k in range(4):
             tt(A("v%d" % k, 0, C), I(A("v%d" % (k - 1) if k else "w0", 0, C), A("cu", 0, 24)), A("b%d" % k, 0, C), O.max)
-            if t == 0 and k in (1, 2):
-                a = 128 * (k - 1)
-                quant(A("qbd", a, a + 128), A("sbd", a, a + 128), A("bd", 4 * a, 4 * a + 512))
+            if t == 0:
+                unpacking(k)
+        if t == 0:
+            planes(qx, sx, OWN)
+            small_constants()
         if t:
             act(A("fb0", 0, C), A("pF0", 0, C))
-        else:
-            put(A("z0", 0, C), C, 0.0)
-            act(A("sp", 0, 768), I(A("ssb", 0, C), A("lu", 0, 48)))
-        act(A("gg", 0, C), I(A("v3", 0, C), A("lu", 0, 24)), AF.Identity, bias=kOff)
-        for a, e in ((0, 256), (256, C)):
-            ts(A("gg", C + a, C + e), I(A("v3", 0, C), A("lu", 24 + a // 16, 24 + e // 16)), kOff, O.add)
+        act(A("gg", 0, CUT), I(A("v3", 0, C), A("lu", 0, CUT // 16)), AF.Identity, bias=kOff)
+        for a, e in ((CUT, C + 256), (C + 256, 2 * C)):
+            ts(A("gg", a, e), I(A("v3", 0, C), A("lu", a // 16, e // 16)), kOff, O.add)
         if t == 0:
             count_constants()
             rank_constants()
-        for a, e in ((C, C + 256), (0, C), (C + 256, 2 * C)):
+        for a, e in ((CUT, C + 256), (C + 256, 2 * C), (0, CUT)):
             turn((T.gt[:, a // 16:e // 16, :], [("gt", a, e, 1)]), A("gg", a, e))
         if t:
             act(A("fb1", 0, C), A("pF1", 0, C))
+        for b in (2, 3) if t else ():
+            if (b, 0) not in GA or (b, 1) not in GA:
+                act(A("fb%d" % b, 0, C), A(OWN[b], 0, C))
+        if t == 0:
+            quant(A("qbd", 0, 128), A("sbd", 0, 128), A("bd", 0, 512))
         for x, ((r, s), (r2, s2)) in enumerate(trios):
             tt(A("ne", x, 24 * NB, NB // 3), (T.gt[:, 0:24, r:r + 2 * s + 1:s], [("gt", 0, C, 1)]),
                (T.gt[:, 24:48, r2:r2 + 2 * s2 + 1:s2], [("gt", C, 2 * C, 1)]), O.not_equal)
         if t == 0:
-            quant(A("qv", 0, 128), A("sv", 0, 128), A("vt", 0, 512))
+            quant(A("qbd", 128, 256), A("sbd", 128, 256), A("bd", 512, 1024))
         for a, e in HALVES:
             a, e = a // 16 * NB, e // 16 * NB
             scan(A("st", a, e), A("ne", a, e), A("d1k", 0, e - a), O.mult, O.add, -100.0)
@@ -482,18 +507,21 @@ def rank_program(g, core, T, topo):
             scan(A("ex", a, e), A("r16b", a, e), A("z0", a, e), O.mult, O.add)
         for a, e in HALVES:
             turn(A("kr", a, e), A("ex", a, e))
+        if t == 0:
+            tc(A("blk", 0, 24), A("idr", 0, 24))
         for a, e in HALVES:
             listed(A("sk", a, e), A("kr", a, e), e - a)
-        tt(A("ms", 0, 192), S(0, 192), A("kr", 0, 192), O.min)
+        tt(A("ms", *PIECES[0]), S(*PIECES[0]), A("kr", *PIECES[0]), O.min)
         tt(A("slm", 0, 24), A("sk", 15, C, 16), A("sn", 15, C, 16), O.min)
-        tt(A("ms", 192, C), S(192, C), A("kr", 192, C), O.min)
+        for a, e in PIECES[1:]:
+            tt(A("ms", a, e), S(a, e), A("kr", a, e), O.min)
         spot, at = {}, 0
         for rows, w in TILES:
             for i, c in enumerate(rows):
                 spot[c] = A("mt", at + i, at + 64 * min(c, 24), 4)
             at += 4 * w
         score = lambda c: A("slm", c, c + 1)
-        sg = lambda c: A("sg", C * (c % 4), C * (c % 4) + 16 * c)
+        sg = lambda c: A("sg", C * (c % 6), C * (c % 6) + 16 * c)
         for c in AROWS:
             act(sg(c), A("ms", 0, 16 * c), AF.Sign, bias=score(c), scale=-1.0)
         for c in AROWS:
@@ -521,93 +549,119 @@ def rank_program(g, core, T, topo):
         column_sums(*sums.pop())
         scan(A("eqs", 0, C), A("kp", 0, C), spot[24], O.mult, O.add)
         if t == 0:
+            quant(A("qv", 0, 128), A("sv", 0, 128), A("vt", 0, 512))
+            late[0] = True
+            act(A("sp", 0, 768), I(A("ssb", 0, C), A("lu", 0, 48)))
+            late[0] = False
             slot_constants()
-            for b in range(2):
-                act(A("fb%d" % b, 0, C), A("pF%d" % b, 0, C))
+            for b in range(4):
+                if (b, 0) not in GA or (b, 1) not in GA:
+                    act(A("fb%d" % b, 0, C), A(OWN[b], 0, C))
         listed(A("cs", 0, C), A("pC", 0, C), C)
         tt(A("rk3", 0, 24), A("cnt", 0, 24), A("eqs", 15, C, 16), O.subtract)
         tt(A("rk", 0, 24), A("rk3", 0, 24), A("cs", 15, C, 16), O.add)
         ts(A("rku", 0, 24), A("rk", 0, 24), kS, O.mult, kz, O.add)
         scatter(A("order", 0, C), A("rku", 0, 24), A("idr", 0, C))
         if t == 0:
+            late_constants()
             ts(A("fin", 0, 4), A("li3", 0, 4), kG, O.add)
         planes(A("lc%d" % t, 0, C), A("ls%d" % t, 0, C))
+        for b in range(DB if t else 0):
+            act(A("db%d" % b, 0, C), A("pF%d" % b, 0, C), scale=0.5)
+        pieces = LASTP if last else PIECES
         for u in range(PER):
             listed(A("ol", 32 * u, 32 * u + 32), A("order", u, W3, PER), 32)
         ou = A("ou", 0, 6)
         ts(ou, A("ol", 15, W3, 16), kS, O.mult)
-        for h in range(2):
-            act(A("sc", W3 * h, W3 * h + W3), I(A("sp", C * h, C * h + C), ou))
-        for h in range(2):
-            act(A("hf", W3 * h, W3 * h + W3), I(A("gg", C * h, C * h + C), ou), AF.Identity, bias=kBi, scale=kSc)
         if t == 0:
             act(s16(9), s16(4), AF.Identity, bias=512.0, scale=-512.0)
         kai, on = A("kai", 0, W3), A("hb", 2 * W3, 3 * W3)
-        tt(kai, I(A("kr", 0, C), ou), A("cm", 0, W3), O.mult)
-        ts(A("jm", 0, W3), kai, 7, O.bitwise_and)
-        ts(A("hb", 0, W3), kai, kP, O.is_ge, 8192.0, O.mult)
-        ts(A("hb", W3, 2 * W3), A("jm", 0, W3), kI, O.is_ge, 8192.0, O.mult)
-        tt(on, A("sc", W3, 2 * W3), A("sc", 0, W3), O.is_gt)
-        turn(A("hbt", 0, 2 * W3), A("hb", 0, 2 * W3))
-        turn(A("hbt", 2 * W3, 3 * W3), on)
-        turn(A("hft", 0, 2 * W3), A("hf", 0, 2 * W3))
-        act(A("lt", 64, 96), I(A("hbt", 2 * W3, 3 * W3), A("fin", 0, 2)), AF.Identity, bias=-4096.0, scale=8192.0)
-        for b in range(3 if t else 2):
-            act(A("db%d" % b, 0, C), A("pF%d" % b, 0, C), scale=0.5)
-        scan(A("ab", 0, 2 * W3), A("hbt", 0, 2 * W3), A("hft", 0, 2 * W3), O.max, O.min)
-        ts(A("inv", 0, W3), kai, 0.0, O.is_equal, 43.0, O.mult)
-        tc(A("lh", 0, 64), I(A("ab", 0, 2 * W3), A("fin", 0, 4)))
-        tt(A("wv", 0, W3), A("inv", 0, W3), on, O.subtract)
-        turn(A("li", 0, 64), A("lh", 0, 64))
-        turn(A("ltt", 64, 96), A("lt", 64, 96))
-        tt(A("bd0", 0, NC), A("li", 32, 32 + NC), A("ltt", 64, 64 + NC), O.add)
-        ts(A("lj", 0, 64), A("li", 0, 64), 511, O.bitwise_and)
-        tt(A("bt", 0, NC), A("bd0", 0, NC), A("li", 0, NC), O.max)
-        tc(A("own%d" % t, 0, 64), A("lj", 0, 64))
-        ts(A("bl", 0, NC), A("bt", 0, NC), 15, O.bitwise_and)
-        ts(A("bh", 0, NC), A("bt", 0, NC), 496, O.bitwise_and)
-        tc(A("bu", 0, NC), A("bl", 0, NC))
-        tt(A("bo", 0, NC), A("bh", 0, NC), A("tagq", 0, NC), O.add)
+        calls = {
+            "s0": lambda: act(A("sc", 0, W3), I(A("sp", 0, C), ou)),
+            "s1": lambda: act(A("sc", W3, 2 * W3), I(A("sp", C, 2 * C), ou)),
+            "p": lambda: act(A("hf", 0, W3), I(A("gg", 0, C), ou), AF.Identity, bias=kBi, scale=kSc),
+            "q": lambda: act(A("hf", W3, 2 * W3), I(A("gg", C, 2 * C), ou), AF.Identity, bias=kBi, scale=kSc),
+            "kai": lambda: tt(kai, I(A("kr", 0, C), ou), A("cm", 0, W3), O.mult),
+            "jm": lambda: ts(A("jm", 0, W3), kai, 7, O.bitwise_and),
+            "keepp": lambda: ts(A("hb", 0, W3), kai, kP, O.is_ge, 8192.0, O.mult),
+            "keepq": lambda: ts(A("hb", W3, 2 * W3), A("jm", 0, W3), kI, O.is_ge, 8192.0, O.mult),
+            "on": lambda: tt(on, A("sc", W3, 2 * W3), A("sc", 0, W3), O.is_gt),
+            "hbt": lambda: turn(A("hbt", 0, 2 * W3), A("hb", 0, 2 * W3)),
+            "ont": lambda: turn(A("hbt", 2 * W3, 3 * W3), on),
+            "hft": lambda: turn(A("hft", 0, 2 * W3), A("hf", 0, 2 * W3)),
+            "inv": lambda: ts(A("inv", 0, W3), kai, 0.0, O.is_equal, 43.0, O.mult),
+            "lt": lambda: act(A("lt", 64, 96), I(A("hbt", 2 * W3, 3 * W3), A("fin", 0, 2)), AF.Identity, bias=-4096.0, scale=8192.0),
+            "db": lambda: [act(A("db%d" % b, 0, C), A("pF%d" % b, 0, C), scale=0.5)
+                           for b in range(DB if t else 0, min(DB + 2, 4) if t else 2)],
+            "ab": lambda: scan(A("ab", 0, 2 * W3), A("hbt", 0, 2 * W3), A("hft", 0, 2 * W3), O.max, O.min),
+            "lh": lambda: tc(A("lh", 0, 64), I(A("ab", 0, 2 * W3), A("fin", 0, 4))),
+            "wv": lambda: tt(A("wv", 0, W3), A("inv", 0, W3), on, O.subtract),
+            "li": lambda: turn(A("li", 0, 64), A("lh", 0, 64)),
+            "ltt": lambda: turn(A("ltt", 64, 96), A("lt", 64, 96)),
+            "lj": lambda: ts(A("lj", 0, 64), A("li", 0, 64), 511, O.bitwise_and),
+            "bd0": lambda: tt(A("bd0", 0, NC), A("li", 32, 32 + NC), A("ltt", 64, 64 + NC), O.add),
+            "own": lambda: tc(A("own%d" % t, 0, 64), A("lj", 0, 64)),
+            "bt": lambda: tt(A("bt", 0, NC), A("bd0", 0, NC), A("li", 0, NC), O.max),
+            "bl": lambda: ts(A("bl", 0, NC), A("bt", 0, NC), 15, O.bitwise_and),
+            "bh": lambda: ts(A("bh", 0, NC), A("bt", 0, NC), 496, O.bitwise_and),
+            "bu": lambda: tc(A("bu", 0, NC), A("bl", 0, NC)),
+            "bo": lambda: tt(A("bo", 0, NC), A("bh", 0, NC), A("tagq", 0, NC), O.add),
+            "mrow": lambda: turn(A("mrow", 0, W3), A("ab", 0, W3)),
+            "ix": lambda: tt(A("ix", 0, W3), I(A("posc", 0, C), ou), A("wv", 0, W3), O.add)}
+        stay[0] = True
+        for name in SLOTS.split():
+            calls[name]()
+        stay[0] = False
         sent = [send(T["came%d" % t][:, 0:32 + NC], A("own%d" % t, 0, 32 + NC), "arl%d" % t)]
         landing("arl%d" % t, width, [("came%d" % t, 0, 64, 1)], sent, 1400.0)
         parts = [(a, min(a + TG // 16, NC)) for a in range(0, NC, TG // 16)]
-        for a, e in parts:
+        for a, e in parts[VV:]:
             act(A("val", 16 * a, 16 * e), I(s16(9), A("bu", a, e)), AF.Identity, bias=16.0 * a - UP * t)
-        for b in range(3 if t else 2, 4):
+        for b in range(min(DB + 2, 4) if t else 2, 4):
             act(A("db%d" % b, 0, C), A("pF%d" % b, 0, C), scale=0.5)
-        between = [lambda: tt(A("ix", 0, W3), I(A("posc", 0, C), ou), A("wv", 0, W3), O.add),
-                   lambda: listed(A("iy", 0, W3), A("ix", 0, W3), W3),
-                   lambda: ts(A("pu", 0, 6), A("iy", 15, W3, 16), kS24, O.mult),
-                   lambda: turn(A("mrow", 0, W3), A("ab", 0, W3)),
-                   lambda: scatter(A("lrep", 0, 1800), A("pu", 0, 6), A("mrow", 0, W3)),
-                   lambda: dma("s", A("llr", 0, 48), row5, 2600.0),
-                   lambda: None]
-        ts(A("ofu", 0, NC), A("bo", 0, NC), TG / 16.0, O.mult)
         tab = A("tab", 0, 25 * TG)
-        for a, e in parts:
-            val = A("val", 16 * a, 16 * e)
-            if a:
-                between.pop(0)()
-                tt(A("tmp", 16 * a, 16 * e), I(tab, A("ofu", a, e)), val, O.min)
-                val = A("tmp", 16 * a, 16 * e)
-            between.pop(0)()
-            if e < NC:
-                scatter(tab, A("ofu", a, e), val)
-        for b in range(4):
+
+        def lower(k):
+            a, e = parts[k]
+            tt(A("tmp", 16 * a, 16 * e), I(tab, A("ofu", a, e)), A("val", 16 * a, 16 * e), O.min)
+
+        def store(k):
+            a, e = parts[k]
+            scatter(tab, A("ofu", a, e), A("tmp" if k else "val", 16 * a, 16 * e))
+
+        def z_plane(b):
             z, win = A("za", SL * b, SL * b + SL), A("db%d" % b, 0, C + 16)
             act(z, I(win, A("came%d" % t, 0, NC)))
-            if b == 1:
-                scatter(tab, A("ofu", a, e), val)
+            other, out = I(win, A("came%d" % t, 32, 32 + NC)), A("zt", b, 4 * SL, 4)
             if b < 4 - ZA:
-                tt(A("zt", b, 4 * SL, 4), I(win, A("came%d" % t, 32, 32 + NC)), z, O.add)
+                tt(out, other, z, O.add)
             else:
-                act(A("zb", SL * (3 - b), SL * (4 - b)), I(win, A("came%d" % t, 32, 32 + NC)))
-                tt(A("zt", b, 4 * SL, 4), A("zb", SL * (3 - b), SL * (4 - b)), z, O.add)
+                act(A("zb", SL * (3 - b), SL * (4 - b)), other)
+                tt(out, A("zb", SL * (3 - b), SL * (4 - b)), z, O.add)
+
+        calls = {"ix": lambda: tt(A("ix", 0, W3), I(A("posc", 0, C), ou), A("wv", 0, W3), O.add),
+                 "val": lambda: ts(A("val", 0, TG), I(s16(9), A("bu", 0, TG // 16)), -UP * t, O.add),
+                 "iy": lambda: listed(A("iy", 0, W3), A("ix", 0, W3), W3),
+                 "pu": lambda: ts(A("pu", 0, 6), A("iy", 15, W3, 16), kS24, O.mult),
+                 "mrow": lambda: turn(A("mrow", 0, W3), A("ab", 0, W3)),
+                 "links": lambda: scatter(A("lrep", 0, 1800), A("pu", 0, 6), A("mrow", 0, W3)),
+                 "back": lambda: dma("s", A("llr", 0, 48), row5, 2600.0),
+                 "ofu": lambda: ts(A("ofu", 0, NC), A("bo", 0, NC), TG / 16.0, O.mult)}
+        stay[0] = True
+        for name in SEARCH.split():
+            if name in calls:
+                calls[name]()
+            else:
+                {"l": lower, "s": store, "z": z_plane}[name[0]](int(name[1]))
+        stay[0] = False
         quant(A("qz", 0, SL), A("sz", 0, SL), A("zt", 0, 4 * SL))
         for b in range(4):
             mm(A("pF%d" % b, 0, SL), A("qw", 128 * b, 128 * b + 128), A("sw", 128 * b, 128 * b + 128),
                A("qz", 0, SL), A("sz", 0, SL))
-        scan(A("ste", 0, 24 * TG), A("one", 0, 24 * TG), A("tab", 0, 24 * TG), O.add, O.min)
+        for b in range(4):
+            act(A("hs%d" % b, 0, SL), A("pF%d" % b, 0, SL), scale=0.03125)
+        for a in (0, 12 * TG):
+            scan(A("ste", a, a + 12 * TG), A("one", 0, 12 * TG), A("tab", a, a + 12 * TG), O.add, O.min)
         ts(A("eu", 0, 24), A("ste", TG - 1, 24 * TG, TG), UP * t, O.add, SL - 1.0, O.min)
         if last:
             ts(A("ll", 0, 48), A("llr", 0, 48), 511, O.bitwise_and)
@@ -620,22 +674,20 @@ def rank_program(g, core, T, topo):
                 for h in range(2):
                     dma("s", ext(T.ol[2 * a + h:2 * a + h + 1, 512:768]),
                         (T.lot[32 * a:32 * a + 16, 32 + 16 * h:48 + 16 * h], [("lot", 32, 64, 1)]))
-        for b in range(4):
-            act(A("hs%d" % b, 0, SL), A("pF%d" % b, 0, SL), scale=0.03125)
-        pieces = ((0, 256), (256, C)) if last else HALVES
         x = lambda b, a, e: A("x%d" % (t + 1), 4 * a + b, 4 * e, 4)
         h = lambda b, a, e: I(A("hs%d" % b, 0, SL), A("eu", a // 16, e // 16))
-        for a, e in pieces:
-            for b in range(2):
-                act(A("ga%d" % (b + 2), a, e), h(b + 2, a, e))
-        for b, k in ((0, 0), (1, 0), (0, 1), (1, 1), (2, 0), (3, 0), (2, 1), (4, 0), (3, 1), (4, 1)):
-            a, e = pieces[k]
-            if b < 2:
-                tt(x(b, a, e), h(b, a, e), A("fb%d" % b, a, e), O.add)
-            elif b < 4:
-                tt(x(b, a, e), A(OWN[b], a, e), A("ga%d" % b, a, e), O.add)
-            else:
-                scores(t + 1, a, e)
+        for b, k in GA:
+            if k < len(pieces):
+                act(A("ga%d" % b, *pieces[k]), h(b, *pieces[k]))
+        for b, k in STATE:
+            if k < len(pieces) or k == 2:
+                a, e = (pieces + ((0, C),))[k]
+                if b == 4:
+                    scores(t + 1, a, e)
+                elif (b, k) in GA:
+                    tt(x(b, a, e), A(OWN[b], a, e), A("ga%d" % b, a, e), O.add)
+                else:
+                    tt(x(b, a, e), h(b, a, e), A("fb%d" % b, a, e), O.add)
         for a, e in pieces if last else ():
             dma("s", ext(T.oc[:, 4 * a:4 * e]), U8("qx%d" % R, a, e))
             act(A("ys", a, e), S(a, e))
@@ -644,9 +696,10 @@ def rank_program(g, core, T, topo):
     for k in range(4):
         dma("s", ext(T.osc[4 * k:4 * k + 4, :]), (T["sx%d" % R][32 * k:32 * k + 4, 0:C], [("sx%d" % R, 0, C, 1)]))
     issue()
-    for src in sorted(count):
-        need("p", src, count[src])
     g.wait_ge(T.sem.lsent, R * 3 * width)
     for t in range(R):
         need("p", "arx%d" % t, 2 * width)
         need("p", "arl%d" % t, width)
+    stores = ["d%d" % k for k in range(ndma[0])]
+    for src in stores[:-2] + list(semof.values()) + stores[-2:]:
+        need("p", src, count[src])

@@ -9,13 +9,18 @@ TYPES = (4, 0, 1, 2, 3, 4, 2, 1, 0, 1, 0, 3, 3, 2, 0, 1)
 MEET = [(i, j) for _, i, j in sorted(((i + j, i, j) for i in range(L) for j in range(L)), reverse=True)]
 MEET = MEET[:18] + [None] + MEET[18:] + [None]
 NB = len(MEET)
+Z0 = 16 * (NB - 2)
 TG = 96
 UP = 1024.0
+CL = 3 * C + 32
 KB = 2.0 ** 17
 ZA = 1
 HUGE = 2.0 ** 80
-WAKE, SLACK, AHEAD = 110.0, 0.0, 40
-AROWS = (19, 18, 17, 16)
+WAKE, SLACK, AHEAD = 200.0, 0.0, 40
+XROWS = (23, 22)
+ZROWS = (21, 20, 19, 18, 17)
+APART = 4
+ZN = (0, 0, 0, 1, 1, 0, 1)
 TILES = [(rows, max(128, 16 * min(max(rows), 24))) for rows in ([24, 23, 22, 21], [20, 19, 18, 17], [16, 15, 14, 13],
                                                               [12, 11, 10, 9], [8, 7, 6, 5], [4, 3, 2, 1])]
 
@@ -53,8 +58,9 @@ def _pool(pool, dtype, spec):
 
 _own(BF, "x0:1536 x1:1536 x2:1536 x3:1536 ut:512 vt:512 et:516 ones:516 za:1408 zb:704 zt:1408")
 _own(BF, "fb0:384 fb1:384 fb2:384 fb3:384 db0:400 db1:400 db2:400 db3:400 bd:1024 bd1:512 mt:5632")
-_own(F32, "hs0:352 hs1:352 hs2:352 hs3:352 ga1:384 ga2:384 ga3:384 ys:384 lot:64")
-_own(I32, "llr:48 lrep:1824")
+_own(F32, "hs0:352 hs1:352 hs2:352 hs3:352 ga0:384 ga1:384 ga2:384 ga3:384 ys:384 lot:64")
+_own(I32, "llr:48")
+_own(F32, "al:384 g32:768 k32:384 sp:768 ssp:384 sn:24 met:384")
 for _n, _k in (("w", 512), ("v", 128), ("u0", 128), ("u", 128), ("e", 512), ("z", SL), ("bd", 256), ("m", 1408)):
     _own(COD, "q%s:%d" % (_n, _k))
     _own("uint8", "s%s:%d" % (_n, _k))
@@ -66,34 +72,34 @@ for _t in range(R + 1):
     _own(COD, "qx%d:384" % _t)
     _own("uint8", "sx%d:384" % _t)
 SCRATCH["gt"] = ("sbuf", [128, 48, 16], BF)
-_pool("poolf", F32, "col:32 s16:192 idr:384 posi:384 posc:384 b0:384 b1:384 b2:384 b3:384 w0:384 smd:384 sn:384 t1:24 slm:24 pre:24 "
-      "npos:24 tagq:24 cm:96 f0:48 f1:48 f2:48 li2:24 li4:24 v0:384 v1:384 v2:384 v3:384 ssb:384 sp:768 ms:384 "
-      "cnt:24 cna:24 rk:24 rk2:24 rk3:24 cs:384 order:384 ol:96 sc:192 hf:192 hft:192 ab:192 lt:96 ltt:96 bd0:24 bd2:24 bo:24 "
-      "ix:96 iy:96 mrow:96 lo:64")
-_pool("poolb", BF, "kt:384 r16b:384 md:384 sgn:384 kp:384 sk:384 gg:768 d1k:324 ne:648 st:648 z0:384 ex:384 kr:384 sg:2304 "
-      "eqs:384 junk:1536 hb:288 hbt:288 inv:96 wv:96 val:384 tmp:384")
-_own(BF, "tab:3200 one:3072")
-_pool("pooli", I32, "pi:2 li5:8 li3:4 ll:48 kai:96 jm:96 lh:64 li:64 lj:64 bt:24 bh:24 bl:24")
-_pool("poolu", U16, "upl:8 irep:26 blk:24 fin:4 lu:48 cu:24 c2u:24 rku:24 ou:6 pu:6 bu:24 ofu:24 eu:24")
-_pool("poolh", F16, "ste:3072")
+_pool("poolf", F32, "col:32 s16:176 kd:72 cm:72 idr:384 b0:384 b1:384 b2:384 b3:384 w0:384 slm:24 pre:24 "
+      "npos:24 tagq:24 li2:24 li4:24 v0:384 v1:384 v2:384 v3:384 ssb:384 ms:384 "
+      "cnt:24 cna:24 rk:24 rk3:24 cs:384 order:384 xt:96 hd:96 ab:128 lt:96 ltt:96 bd0:24 bo:24 "
+      "side:6 wt:96 wx:96 wn:384 wl:384 lo:64")
+_pool("poolb", BF, "kt:384 kr:384 fl:384 cl:1184 r8b:384 kp:384 sk:384 gg:768 d1k:648 ne:648 ex:384 sg:3072 "
+      "eqs:384 junk:768 hb:96 on:128 dn:96 val:384 tmp:384")
+_own(BF, "tab:3200 one:3072 z0:384 zs:10768 ends:6144")
+_pool("pooli", I32, "pi:4 li5:8 li3:4 ll:48 an:48 lh:64 li:64 lj:64 bt:24 bh:24")
+_pool("poolu", U16, "upl:8 irep:26 blk:24 fin:4 fon:2 lu:48 cu:24 rku:24 prm:24 bu:24 ofu:24 eu:24")
+_pool("poolh", F16, "ste:3072 rs:2688")
 PSUM = ("pS", "pC", "pF0", "pF1", "pF2", "pF3", "pG2", "pG3")
 OWN = ("pF0", "pF1", "pG2", "pG3")
 HALVES = ((0, 192), (192, C))
 PIECES = ((0, 256), (256, C))
 LATE = (200.0, 0.0)
-VV = 0
-SLOTS = "s0 s1 p q kai jm keepp keepq on hbt ont hft inv lt db ab wv lh ltt li lj bd0 own bt bl bh bu bo"
-SEARCH = "ofu ix s0 iy mrow l1 pu s1 links back l2 s2 z0 l3 z1 s3 z2 z3"
+SLOTS = "t0 t1 t2 down on keep lt side ab lh ltt db li wt lj bd0 own bt bh bu bo"
+SEARCH = "ofu wx db s0 u0 u1 l1 u2 wn s1 l2 s2 l3 s3 z0 z1 z2 z3"
+WLP = 96
 PE = 1.0
 LASTP = ((0, 256), (256, C))
 DB = 2
 CUT = 384
-CROSS = 110.0
-GA = ((2, 0), (3, 0), (2, 1))
-STATE = ((0, 2), (1, 2), (2, 0), (3, 0), (3, 1), (4, 0), (2, 1), (4, 1))
+CROSS = 200.0
+GA = ((3, 0), (2, 1), (3, 1))
+STATE = ((0, 2), (1, 2), (2, 0), (3, 0), (4, 0), (2, 1), (3, 1), (4, 1))
 for _n in PSUM:
     SCRATCH[_n] = ("psum", [128, 512], F32)
-NDMA = 44
+NDMA = 69
 SEMAPHORES = (["qv_", "qa_", "qt_", "qp_", "lsent"] + ["arx%d" % t for t in range(R)] + ["arl%d" % t for t in range(R)]
               + ["d%d" % k for k in range(NDMA)])
 
@@ -109,8 +115,8 @@ def rank_program(g, core, T, topo):
     eng = {"v": g.vector, "a": g.scalar, "t": g.tensor, "p": g, "s": g.sync}
     semof = {"v": "qv_", "a": "qa_", "t": "qt_", "p": "qp_"}
     count, known = {}, {q: {} for q in eng}
-    clocks, hist, ops = {}, {}, []
-    ndma, stay, late = [0], [False], [False]
+    clocks, hist, met, ops = {}, {}, {}, []
+    ndma, stay = [0], [False]
 
     def need(q, src, val):
         if known[q].get(src, 0) >= val:
@@ -123,7 +129,9 @@ def rank_program(g, core, T, topo):
     def meet(x, y):
         if x[0] >= y[1] or y[0] >= x[1] or x[2] == y[2] and (x[0] - y[0]) % x[2]:
             return False
-        return min(x[2], y[2]) == 1 and max(x[1] - x[0], y[1] - y[0]) > 32 or bool(set(range(*x)) & set(range(*y)))
+        if (x, y) not in met:
+            met[(x, y)] = min(x[2], y[2]) == 1 and max(x[1] - x[0], y[1] - y[0]) > 32 or bool(set(range(*x)) & set(range(*y)))
+        return met[(x, y)]
 
     def covers(x, y):
         return x[0] <= y[0] and y[1] <= x[1] and (x[2] == 1 or x[2] == y[2] and (x[0] - y[0]) % x[2] == 0)
@@ -209,13 +217,13 @@ def rank_program(g, core, T, topo):
         else:
             hold = max(64.0, n * rate) + 20.0 * (len(writes) - 1)
         more = LATE[0] if isinstance(writes[0], list) else LATE[1] if any(isinstance(r, list) for r in reads) else 0.0
-        record(q, "kept" if stay[0] and q == "v" or late[0] else "call", fn, [tuple(r) for r in reads], [tuple(r) for r in writes], hold, more)
+        record(q, "kept" if stay[0] in (q, True) and q in ("v", stay[0]) else "call", fn, [tuple(r) for r in reads], [tuple(r) for r in writes], hold, more)
 
     def dma(q, out, in_, more=3600.0):
-        record(q, "dma", lambda: eng[q].dma_start(out[0], in_[0]), in_[1], out[1], 50.0, more)
+        record(q, "dma", lambda: eng[q].dma_start(out[0], in_[0]), in_[1], out[1], 1000.0 if q == "p" else 50.0, more)
 
     def send(out, in_, sem):
-        return record("p", "send", lambda: g.remote_dma(out, in_[0], T.sem[sem], T.sem.lsent, pid, rid, mask), in_[1], [], 3000.0 if sem == "arx0" else 1000.0)
+        return record("p", "send", lambda: g.remote_dma(out, in_[0], T.sem[sem], T.sem.lsent, pid, rid, mask), in_[1], [], 1800.0 if sem == "arx0" else 1000.0)
 
     def landing(sem, val, pieces, after, more):
         record("r", "landing", (sem, val), [], pieces, 0.0, more, after)
@@ -294,90 +302,114 @@ def rank_program(g, core, T, topo):
 
     def iota(out, pattern, base, cm, flag=False):
         kw = {"allow_small_or_imprecise_dtypes": True} if flag else {}
-        record("p", "kept" if stay[0] else "call", lambda: g.iota(out[0], pattern, base, cm, **kw), [], out[1], 130.0 + 2 * size(out[1][0]))
+        record("p", "kept", lambda: g.iota(out[0], pattern, base, cm, **kw), [], out[1], 130.0 + 2 * size(out[1][0]))
 
     def choose(out, in_, pattern, cmp, base, cm):
-        record("p", "call", lambda: g.affine_select(out[0], in_[0], pattern, cmp, 0.0, base, cm), in_[1], out[1],
+        record("p", "kept", lambda: g.affine_select(out[0], in_[0], pattern, cmp, 0.0, base, cm), in_[1], out[1],
                170.0 + 2 * size(out[1][0]))
 
-    (kI, kType, kG, kB0, kB1, kB2, kB3, kOff, kSc, kBi, kBj, kP, kS, kS24, kK, kIb, kz, kKm, kN) = [
-        A("col", k, k + 1) for k in range(19)]
+    (kI, kType, kG, kB0, kB1, kB2, kB3, kOff, kL, kU, kS, kSn, kK, kIb, kz, kKm, kN, kC, kT0, kT1, kE0, kE1) = [
+        A("col", k, k + 1) for k in range(22)]
     s16 = lambda k: A("s16", 16 * k, 16 * k + 16)
-    row5 = (T.lrep[L:128:16, 0:2 * C], [("lrep", 0, 2 * C, 1)])
+    every = lambda n, r, s, w: (T[n][r:128:s, 0:w], [(n, 0, w, 1)])
+    carried = lambda r: (T.al[r:128:8, 0:C], [("al", r, C, 8)])
 
     dma("s", A("ut", 0, 512), ext(T.u[:, :]), 1500.0)
     for q, (a, e) in zip("as", PIECES):
         dma(q, A("x0", 4 * a, 4 * e), ext(T.x[:, 4 * a:4 * e]), 2000.0)
     dma("a", A("llr", 0, 48), ext(T.nb[:, :]), 2400.0)
-    dma("s", row5, ext(T.nb[:, :]))
-    dma("s", U8("qw", 0, 512), (T.wc[:, :], [("x0", 0, 4 * C, 1)]))
-    dma("s", A("sw", 0, 512), ext(T.ws[:, :]))
-    dma("s", A("vt", 0, 512), ext(T.v[:, :]), 6000.0)
 
+    def late_loads():
+        dma("s", U8("qw", 0, 512), ext(T.wc[:, :]))
+        dma("s", A("sw", 0, 512), ext(T.ws[:, :]))
+        dma("s", A("vt", 0, 512), ext(T.v[:, :]), 6000.0)
+
+    ones, half, blocks = A("ones", 0, 512), A("bd1", 0, 512), A("bd", 0, 512)
     iota(A("pi", 0, 1), [[1, 1]], 0, 1)
     iota(s16(0), [[1, 16]], 0, 0, True)
     iota(A("li5", 0, 8), [[16, 8]], 0, 0)
-    ones, half, blocks = A("ones", 0, 512), A("bd1", 0, 512), A("bd", 0, 512)
     iota(A("idr", 0, C), [[1, C]], 0, 0, True)
-    iota(A("ones", 0, 516), [[0, 516]], 1, 0, True)
+    fill(A("ones", 0, 516), 1.0)
+    iota(A("wn", 0, C), [[1, 16], [16, 24]], 0, 0, True)
     choose(A("et", 0, 516), A("ones", 0, 516), [[1, 516]], O.is_equal, -3, -4)
-    iota(A("s16", 32, 47), [[32, PER], [1, L]], 1, 0, True)
-    iota(A("li3", 0, 4), [[W3, 2], [16, 2]], 0, 0)
+
+    choose(A("r8b", 0, C), A("ones", 0, C), [[0, C // 8], [1, 8]], O.not_equal, 0, 0)
     choose(half, ones, [[-16, 8], [0, 64]], O.is_ge, 0, 1)
     choose(blocks, half, [[16, 8], [0, 64]], O.is_ge, 15, -1)
     choose(A("bd", 512, 1024), blocks, [[-1, 128], [1000, 4]], O.is_ge, -1, 1)
     iota(A("li2", 0, 24), [[16, 24]], 0, 0, True)
-    iota(A("li4", 0, 24), [[0, 384 // TG], [-16, TG // 16]], TG - 1, 0, True)
 
     def later_on_g():
-        iota(A("posi", 0, C), [[1, 24], [48, 16]], 24, 0, True)
+        iota(A("li3", 0, 4), [[8, 2], [16, 2]], 1, 0)
+        iota(A("li4", 0, 24), [[0, 384 // TG], [-16, TG // 16]], TG - 1, 0, True)
         for b in range(4):
             iota(A("db%d" % b, C, C + 16), [[0, 16]], 0, 0, True)
         iota(A("tab", 0, 25 * TG), [[0, 25 * TG]], 512, 0, True)
+
+    def scan_constants():
         iota(A("one", 0, 12 * TG), [[0, 12 * TG]], 1, 0, True)
         iota(A("one", 0, 12 * TG, TG), [[0, 12]], 4096, 0, True)
 
     def put(out, n, k):
-        act(out, A("idr", 0, n), AF.Identity, bias=k, scale=0.0)
+        act(out, A("ones", 0, n), AF.Identity, bias=k, scale=0.0)
 
     for k in range(L):
         rows = [r for r in range(16) if TYPES[r] == k]
         for a, b in zip(rows[0::2], rows[1::2] + [None]):
             act(A("s16", 16 + a, 16 + (b or a) + 1, b - a if b else 1), A("s16", 0, 2 if b else 1), AF.Identity,
                 bias=float(k), scale=0.0)
-    fill(A("r16b", 0, C), 1.0)
     ts(A("pi", 1, 2), A("pi", 0, 1), 15, O.bitwise_and)
     tc(kI, A("pi", 1, 2))
     tc(A("upl", 0, 8), A("li5", 0, 8))
     ts(s16(4), s16(0), kI, O.is_equal)
-    ts(A("irep", 0, 24), A("r16b", 0, 24), 0.0, O.mult, kI, O.add)
     ts(s16(3), s16(0), kI, O.subtract)
-    act(A("md", 0, C), I(s16(4), A("irep", 0, 24)))
-    fill(A("r16b", 0, C, 16), 0.0)
+    ts(A("irep", 0, 24), A("ones", 0, 24), 0.0, O.mult, kI, O.add)
+    ts(s16(6), s16(3), 0.0, O.not_equal)
+    ts(s16(7), s16(3), 1.0, O.is_equal, KB, O.mult)
     tt(s16(8), s16(4), s16(1), O.mult)
-    fill(A("d1k", 0, 12 * NB), 7.0)
+    tt(s16(10), s16(6), s16(7), O.max)
     total(kType, s16(8))
+    put(A("z0", 0, C), C, 0.0)
+    at = 0
+    for rows, w in TILES:
+        for a in range(at + 64 * min(rows), at + 4 * w, C):
+            e = min(a + C, at + 4 * w)
+            zeros = A("z0", 0, e - a)
+            dma("s", A("mt", a, e), (zeros[0], zeros[1] + [("x0", 0, 4 * C, 1)]), 2400.0)
+        at += 4 * w
     act(A("w0", 0, C), A("idr", 0, C), AF.Identity, bias=UP)
+    put(A("met", 0, C), C, 0.0)
+    dma("s", carried(7), every("met", 7, 8, C), 2200.0)
+    ts(kS, kI, 14.5, O.is_gt, 1.0 / KB, O.max)
+    for side in range(2):
+        fill(A("d1k", 12 * NB * side, 12 * NB * (side + 1)), (1 - 2 * side) * HUGE)
     for k, bias in enumerate((kB0, kB1, kB2, kB3)):
         ts(bias, kType, L - 1.5 - k, O.is_lt, UP * (k + 2), O.mult)
+    tc(A("kt", 0, C), I(s16(10), A("irep", 0, 24)))
+    fill(A("kd", 0, 72, 3), 0.0)
+    fill(A("cl", 61, CL, 48), 0.0)
+    listed(A("cs", 0, C), A("wn", 0, C), C)
+    ts(A("kd", 1, 72, 3), A("ones", 0, 24), kS, O.mult)
+
+    def small_constants():
+        ts(A("prm", 0, 24), A("cs", 15, C, 16), kS, O.mult)
+        ts(kKm, kI, 14.5, O.is_lt, KB - 1.0, O.mult)
+        ts(kOff, kType, UP, O.mult, -L * UP - 192.0, O.add)
 
     def step_constants():
-        put(A("f0", 0, 48, 2), 24, 0.0)
         for k, bias in enumerate((kB0, kB1, kB2, kB3)):
             act(A("b%d" % k, 0, C), A("idr", 0, C), AF.Identity, bias=bias)
 
-    def small_constants():
-        ts(s16(6), s16(3), 0.0, O.not_equal)
-        ts(s16(7), s16(3), 1.0, O.is_equal, KB, O.mult)
-        ts(kKm, kI, 14.5, O.is_lt, KB - 1.0, O.mult)
-        tt(s16(10), s16(6), s16(7), O.max)
-        ts(kOff, kType, UP, O.mult, -L * UP - 192.0, O.add)
-        ts(kS, kI, 14.5, O.is_gt, 1.0 / KB, O.max)
-
     def late_constants():
-        fill(A("s16", 47, 48), 0.0)
-        tt(s16(11), s16(4), s16(2), O.mult)
-        total(kG, s16(11))
+        ts(A("pi", 2, 3), A("pi", 0, 1), 31, O.bitwise_and)
+        ts(A("pi", 3, 4), kI, 1.0 / L, O.mult, -0.4, O.add)
+        tc(kC, A("pi", 2, 3))
+        ts(kG, A("pi", 3, 4), 32.0 - L, O.mult, kI, O.add)
+        ts(kU, A("pi", 3, 4), 32.0, O.mult, 6.0, O.add)
+
+    def last_constants():
+        ts(A("fon", 0, 2), A("li3", 0, 2), kU, O.add)
+        ts(A("fin", 0, 4), A("li3", 0, 4), kG, O.add)
 
     quant(A("qu0", 0, 128), A("su0", 0, 128), A("ut", 0, 512))
     tc(U32("qu", 0, 128), I(U32("qu0", 0, 128), A("upl", 0, 8)))
@@ -396,46 +428,56 @@ def rank_program(g, core, T, topo):
             mm(A(banks[b], 0, C), A("qe", 128 * b, 128 * b + 128), A("se", 128 * b, 128 * b + 128), codes, plane)
 
     def meeting_constants():
-        f = [8 * m[0] + m[1] + 1.25 if m else None for m in MEET]
-        f[NB - 2] = -0.25
-        f = [f[e] if f[e] is not None or e == NB - 1 else f[e + 1] for e in range(NB)]
-        steps = [f[e] - f[e + 1] for e in range(NB - 2)] + [f[NB - 2], -100.0]
-        for e in range(NB):
-            if steps[e] != 7.0:
-                put(A("d1k", e, 12 * NB, NB), 12, steps[e])
+        put(A("zs", Z0, Z0 + NB * C, NB), C, 0.0)
+        put(A("ne", NB - 1, 24 * NB, NB), 24, 0.0)
+        for side in range(2):
+            f = [m[side] + 1.0 if m else None for m in MEET]
+            f[NB - 2] = -1.0
+            f = [f[e] if f[e] is not None or e == NB - 1 else f[e + 1] for e in range(NB)]
+            steps = [f[e] - f[e + 1] for e in range(NB - 2)] + [f[NB - 2], -1.0 - f[0]]
+            for e in range(NB):
+                if steps[e] != 1 - 2 * side:
+                    put(A("d1k", 12 * NB * side + e, 12 * NB * (side + 1), NB), 12, steps[e] * HUGE)
 
     def count_constants():
-        act(A("kt", 0, C), I(s16(10), A("irep", 0, 24)))
         act(s16(5), s16(4), AF.Identity, bias=1.0, scale=kKm)
+        act(kL, kI, AF.Identity, bias=192.0, scale=512.0)
         put(A("s16", 80, 81), 1, 0.0)
+        put(A("cna", 0, 1), 1, 0.0)
         act(A("kp", 0, C), I(s16(5), A("irep", 0, 24)))
-        put(A("cnt", 0, 1), 1, 0.0)
-        at = 0
-        for rows, w in TILES:
-            for a in range(at + 64 * min(rows), at + 4 * w, 256):
-                e = min(a + 256, at + 4 * w)
-                put(A("mt", a, e), e - a, 0.0)
-            at += 4 * w
+        act(A("ends", 0, C), I(s16(4), A("irep", 0, 24)), AF.Identity, bias=512.0, scale=-512.0)
+        for a in range(1, 4):
+            dma("s", A("ends", a * C, (a + 1) * C), A("ends", 0, C), 2400.0)
 
     def rank_constants():
-        act(kSc, kI, AF.Sign)
         act(kz, kI, AF.Identity, bias=0.2)
         act(kK, kKm, AF.Identity, bias=1.0)
         act(kN, kKm, AF.Identity, bias=-1.0, scale=-1.0)
         act(A("npos", 0, 24), A("li2", 0, 24), AF.Identity, scale=kK)
 
     def slot_constants():
-        act(kBj, kI, AF.Relu, bias=-192.0, scale=512.0)
-        act(kP, kI, AF.Identity, bias=-7.0, scale=8.0)
-        act(kS24, kS, scale=24.0)
+        for e, n in ((kE0, NC), (kE1, M // PER)):
+            act(e, kC, AF.Relu, bias=-HUGE * 2.0 ** 12 * (n - 1), scale=HUGE * 2.0 ** 12)
+        put(A("dn", 0, W3), W3, -HUGE)
+        for k, e in ((kT0, kE0), (kT1, kE1)):
+            act(k, e, AF.Identity, bias=4096.0)
+        act(kSn, kS, scale=-1.0)
         act(kIb, kI, AF.Identity, bias=0.02, scale=-16.0 / TG)
-        put(A("cm", 0, W3), W3, 0.0)
-        act(kBi, kBj, AF.Identity, bias=float(C))
+        put(A("dn", 0, W3, 8), W3 // 8, -HUGE * 2.0 ** 15)
+        put(A("dn", 1, W3, 8), W3 // 8, -HUGE / 2)
+        put(A("ab", W3, 128), 128 - W3, 0.0)
+        put(A("on", 0, 128), 128, 0.0)
+        put(A("wt", 0, W3), W3, 0.0)
         act(A("tagq", 0, 24), A("li4", 0, 24), AF.Identity, bias=kIb, scale=16.0 / TG)
-        for u in range(PER):
-            n = (M - u + PER - 1) // PER
-            put(A("cm", 32 * u, 32 * u + n), n, 1.0 / HUGE)
-        act(A("posc", 0, C), A("posi", 0, C), AF.Identity, bias=0.002, scale=1.0 / 24)
+
+    def own_planes():
+        for b in range(4):
+            if (b, 0) not in GA or (b, 1) not in GA:
+                act(A("fb%d" % b, 0, C), A(OWN[b], 0, C))
+
+    def score_list():
+        act(A("ssp", 0, C), I(A("ssb", 0, C), A("prm", 0, 24)))
+        dma("s", A("sn", 0, 24), every("ssp", 0, 16, C), 2400.0)
 
     trios = _trios()
     for t in range(R):
@@ -445,74 +487,80 @@ def rank_program(g, core, T, topo):
             for a, e in PIECES:
                 scores(0, a, e)
             step_constants()
-        sent = [send(T["lc%d" % t][:, 0:C].bitcast(dt.uint8), U8("qx%d" % t, 0, C), "arx%d" % t),
-                send(T["ls%d" % t][:, 0:C], sx, "arx%d" % t)]
-        landing("arx%d" % t, 2 * width, [("lc%d" % t, 0, C, 1), ("ls%d" % t, 0, C, 1)], sent, 11000.0 if t else 8500.0)
-        if t == 0:
-            later_on_g()
-        else:
+        if t:
             planes(qx, sx, OWN)
         ts(A("ll", 0, 48), A("llr", 0, 48), 511, O.bitwise_and)
-        tt(A("f0", 1, 48, 2), A("ll", 24, 48), A("ll", 0, 24), O.subtract)
-        tc(A("f1", 1, 48, 2), A("ll", 0, 24))
+        tt(A("kd", 2, 72, 3), A("ll", 24, 48), A("ll", 0, 24), O.subtract)
+        ts(A("cl", 77, CL, 48), A("ll", 0, 24), -192.0, O.add)
         tc(A("lu", 0, 48), A("ll", 0, 48))
         for a, e in PIECES:
-            tt(A("smd", a, e), S(a, e), A("md", a, e), O.mult)
+            ts(A("fl", a, e), S(a, e), 0.0, O.is_gt)
             act(A("ssb", a, e), S(a, e))
         for a, e in PIECES:
-            scan(A("sn", a, e), A("r16b", a, e), A("smd", a, e), O.mult, O.add)
-        ts(A("f1", 0, 48, 2), A("sn", 15, C, 16), 0.0, O.is_gt)
-        scan(A("f2", 0, 48), A("f0", 0, 48), A("f1", 0, 48), O.mult, O.add)
-        tc(A("cu", 0, 24), A("f2", 1, 48, 2))
+            listed(A("cl", 3 * a, 3 * e, 3), A("fl", a, e), e - a)
+        scan(A("cm", 0, 72), A("kd", 0, 72), A("cl", 45, CL, 16), O.mult, O.add)
+        ts(A("cu", 0, 24), A("cm", 2, 72, 3), 192.1, O.add)
         if t == 0:
+            small_constants()
+        score_list()
+        codes = U8("qx%d" % t, 0, C)
+        sent = [send(T["lc%d" % t][:, 0:C].bitcast(dt.uint8), (codes[0], codes[1] + [("ssp", 0, C, 1)]), "arx%d" % t),
+                send(T["ls%d" % t][:, 0:C], sx, "arx%d" % t)]
+        landing("arx%d" % t, 2 * width, [("lc%d" % t, 0, C, 1), ("ls%d" % t, 0, C, 1)], sent, 9500.0 if t else 8000.0)
+        if t == 0:
+            later_on_g()
             meeting_constants()
-            put(A("z0", 0, C), C, 0.0)
-        else:
-            act(A("sp", 0, 768), I(A("ssb", 0, C), A("lu", 0, 48)))
+        act(A("sp", 0, 768), I(A("ssb", 0, C), A("lu", 0, 48)))
+        dma("s", carried(6), every("sp", 6, 16, 2 * C), 2200.0)
         for k in range(4):
             tt(A("v%d" % k, 0, C), I(A("v%d" % (k - 1) if k else "w0", 0, C), A("cu", 0, 24)), A("b%d" % k, 0, C), O.max)
             if t == 0:
                 unpacking(k)
-        if t == 0:
-            planes(qx, sx, OWN)
-            small_constants()
-        if t:
-            act(A("fb0", 0, C), A("pF0", 0, C))
         act(A("gg", 0, CUT), I(A("v3", 0, C), A("lu", 0, CUT // 16)), AF.Identity, bias=kOff)
         for a, e in ((CUT, C + 256), (C + 256, 2 * C)):
             ts(A("gg", a, e), I(A("v3", 0, C), A("lu", a // 16, e // 16)), kOff, O.add)
         if t == 0:
             count_constants()
-            rank_constants()
         for a, e in ((CUT, C + 256), (C + 256, 2 * C), (0, CUT)):
             turn((T.gt[:, a // 16:e // 16, :], [("gt", a, e, 1)]), A("gg", a, e))
+        act(A("g32", 0, 2 * C), A("gg", 0, 2 * C), AF.Identity, bias=kL)
+        for k in range(1, L + 1):
+            dma("s", carried(k), every("g32", k, 16, 2 * C), 2200.0)
         if t:
-            act(A("fb1", 0, C), A("pF1", 0, C))
-        for b in (2, 3) if t else ():
-            if (b, 0) not in GA or (b, 1) not in GA:
-                act(A("fb%d" % b, 0, C), A(OWN[b], 0, C))
-        if t == 0:
-            quant(A("qbd", 0, 128), A("sbd", 0, 128), A("bd", 0, 512))
+            stay[0] = "a"
+            own_planes()
+            stay[0] = False
+        else:
+            planes(qx, sx, OWN)
         for x, ((r, s), (r2, s2)) in enumerate(trios):
-            tt(A("ne", x, 24 * NB, NB // 3), (T.gt[:, 0:24, r:r + 2 * s + 1:s], [("gt", 0, C, 1)]),
-               (T.gt[:, 24:48, r2:r2 + 2 * s2 + 1:s2], [("gt", C, 2 * C, 1)]), O.not_equal)
-        if t == 0:
-            quant(A("qbd", 128, 256), A("sbd", 128, 256), A("bd", 512, 1024))
+            if x < NB // 3 - 1:
+                tt(A("ne", x, 24 * NB, NB // 3), (T.gt[:, 0:24, r:r + 2 * s + 1:s], [("gt", 0, C, 1)]),
+                   (T.gt[:, 24:48, r2:r2 + 2 * s2 + 1:s2], [("gt", C, 2 * C, 1)]), O.not_equal)
+            for k in range(2 if x == NB // 3 - 1 else 0):
+                tt(A("ne", x + NB // 3 * k, 24 * NB, NB), (T.gt[:, 0:24, r + k * s], [("gt", 0, C, 1)]),
+                   (T.gt[:, 24:48, r2 + k * s2], [("gt", C, 2 * C, 1)]), O.not_equal)
         for a, e in HALVES:
             a, e = a // 16 * NB, e // 16 * NB
-            scan(A("st", a, e), A("ne", a, e), A("d1k", 0, e - a), O.mult, O.add, -100.0)
+            for side in range(2):
+                at = 8 * NB * side
+                scan(A("zs", at + 16 * a, at + 16 * e, 16), A("ne", a, e), A("d1k", 12 * NB * side, 12 * NB * side + e - a),
+                     O.mult, O.add, -(L + 1.0) * HUGE)
         for a, e in HALVES:
-            ts(A("z0", a, e, 16), A("st", a // 16 * NB + NB - 2, e // 16 * NB, NB), -0.25, O.max, HUGE, O.mult)
-        for a, e in HALVES:
-            scan(A("ex", a, e), A("r16b", a, e), A("z0", a, e), O.mult, O.add)
+            scan(A("ex", a, e), A("r8b", a, e), A("zs", Z0 + NB * a, Z0 + NB * e, NB), O.mult, O.add)
         for a, e in HALVES:
             turn(A("kr", a, e), A("ex", a, e))
+            act(A("k32", a, e), A("kr", a, e))
+        dma("s", carried(0), every("k32", 0, 8, C), 2200.0)
         if t == 0:
+            for a in range(4, 16, 4):
+                dma("s", A("ends", a * C, (a + 4) * C), A("ends", 0, 4 * C), 3000.0)
+            late_loads()
             tc(A("blk", 0, 24), A("idr", 0, 24))
+            late_constants()
         for a, e in HALVES:
             listed(A("sk", a, e), A("kr", a, e), e - a)
         tt(A("ms", *PIECES[0]), S(*PIECES[0]), A("kr", *PIECES[0]), O.min)
-        tt(A("slm", 0, 24), A("sk", 15, C, 16), A("sn", 15, C, 16), O.min)
+        tt(A("slm", 0, 24), A("sk", 15, C, 16), A("sn", 0, 24), O.min)
         for a, e in PIECES[1:]:
             tt(A("ms", a, e), S(a, e), A("kr", a, e), O.min)
         spot, at = {}, 0
@@ -521,104 +569,104 @@ def rank_program(g, core, T, topo):
                 spot[c] = A("mt", at + i, at + 64 * min(c, 24), 4)
             at += 4 * w
         score = lambda c: A("slm", c, c + 1)
-        sg = lambda c: A("sg", C * (c % 6), C * (c % 6) + 16 * c)
-        for c in AROWS:
-            act(sg(c), A("ms", 0, 16 * c), AF.Sign, bias=score(c), scale=-1.0)
-        for c in AROWS:
-            act(spot[c], sg(c), AF.Relu, accum=A("cna", c, c + 1))
-        at, sums = 0, []
+        sg = lambda c: A("sg", 8 * c * (c - 1), 8 * c * (c + 1))
+        alone = [c for rows, w in TILES for c in rows if c < 24 and c not in XROWS + ZROWS]
+        for c, d in zip(alone + [None] * APART, [None] * APART + alone):
+            if c:
+                act(sg(c), A("ms", 0, 16 * c), AF.Sign, bias=score(c), scale=-1.0)
+            if d:
+                act(spot[d], sg(d), AF.Relu, accum=A("cna", d, d + 1))
+        at, sums, rows_left = 0, [], list(ZROWS)
+
+        def row_sums(n):
+            for c in rows_left[:n]:
+                e = C * (c - min(ZROWS) + 1)
+                scan(A("rs", e - 16 * c, e), A("ones", 0, 16 * c), spot[c], O.mult, O.add)
+            del rows_left[:n]
 
         def column_sums(k, at, w):
             a, s = at // 4, 128 if k == 0 else 0
             quant(A("qm", a, a + w), A("sm", a, a + w), A("mt", at, at + 4 * w))
             mm(A("pC", 0, w), A("qbd", s, s + 128), A("sbd", s, s + 128), A("qm", a, a + w), A("sm", a, a + w), k == 0, k == 5)
 
+        stay[0] = True
         for k, (rows, w) in enumerate(TILES):
             for c in sorted(rows, key=lambda c: c == 24):
                 if c == 24:
                     tt(spot[c], I(A("slm", 0, 24), A("blk", 0, 24)), A("ms", 0, C), O.is_gt)
-                elif c not in AROWS:
+                elif c not in alone:
                     ts(spot[c], A("ms", 0, 16 * c), score(c), O.is_lt)
-                    act(A("junk", C * (c % 4), C * (c % 4) + 16 * c), spot[c], AF.Identity, scale=kN, bias=kK, accum=A("cnt", c, c + 1))
-                if sums and c not in AROWS:
+                if t == 0 and c in (24, 20):
+                    a = 128 if c == 24 else 0
+                    quant(A("qbd", a, a + 128), A("sbd", a, a + 128), A("bd", 4 * a, 4 * a + 512))
+                if sums and c not in alone:
                     column_sums(*sums.pop(0))
-            for c in AROWS if k == 2 else ():
-                act(A("cnt", c, c + 1), A("cna", c, c + 1), AF.Identity, scale=kN, bias=A("npos", c, c + 1))
+            if k == 2:
+                scan(A("eqs", 0, C), A("kp", 0, C), spot[24], O.mult, O.add)
+            row_sums(ZN[k])
+            while sums:
+                column_sums(*sums.pop(0))
             sums.append((k, at, w))
             at += 4 * w
-        column_sums(*sums.pop())
-        scan(A("eqs", 0, C), A("kp", 0, C), spot[24], O.mult, O.add)
         if t == 0:
-            quant(A("qv", 0, 128), A("sv", 0, 128), A("vt", 0, 512))
-            late[0] = True
-            act(A("sp", 0, 768), I(A("ssb", 0, C), A("lu", 0, 48)))
-            late[0] = False
+            rank_constants()
+        for c in XROWS:
+            act(A("junk", C * (c % 2), C * (c % 2) + 16 * c), spot[c], AF.Identity, accum=A("cna", c, c + 1))
+        row_sums(ZN[6])
+        column_sums(*sums.pop())
+        row_sums(len(ZROWS))
+        tt(A("pre", 0, 24), A("npos", 0, 24), A("eqs", 15, C, 16), O.subtract)
+        tc(A("cna", min(ZROWS), max(ZROWS) + 1), A("rs", C - 1, C * len(ZROWS), C))
+        stay[0] = False
+        act(A("cnt", 0, 24), A("cna", 0, 24), AF.Identity, scale=kN)
+        if t == 0:
             slot_constants()
-            for b in range(4):
-                if (b, 0) not in GA or (b, 1) not in GA:
-                    act(A("fb%d" % b, 0, C), A(OWN[b], 0, C))
+            own_planes()
         listed(A("cs", 0, C), A("pC", 0, C), C)
-        tt(A("rk3", 0, 24), A("cnt", 0, 24), A("eqs", 15, C, 16), O.subtract)
+        tt(A("rk3", 0, 24), A("cnt", 0, 24), A("pre", 0, 24), O.add)
         tt(A("rk", 0, 24), A("rk3", 0, 24), A("cs", 15, C, 16), O.add)
         ts(A("rku", 0, 24), A("rk", 0, 24), kS, O.mult, kz, O.add)
-        scatter(A("order", 0, C), A("rku", 0, 24), A("idr", 0, C))
+        scatter(A("order", 0, C), A("rku", 0, 24), A("al", 0, C))
         if t == 0:
-            late_constants()
-            ts(A("fin", 0, 4), A("li3", 0, 4), kG, O.add)
+            last_constants()
         planes(A("lc%d" % t, 0, C), A("ls%d" % t, 0, C))
         for b in range(DB if t else 0):
             act(A("db%d" % b, 0, C), A("pF%d" % b, 0, C), scale=0.5)
         pieces = LASTP if last else PIECES
-        for u in range(PER):
-            listed(A("ol", 32 * u, 32 * u + 32), A("order", u, W3, PER), 32)
-        ou = A("ou", 0, 6)
-        ts(ou, A("ol", 15, W3, 16), kS, O.mult)
-        if t == 0:
-            act(s16(9), s16(4), AF.Identity, bias=512.0, scale=-512.0)
-        kai, on = A("kai", 0, W3), A("hb", 2 * W3, 3 * W3)
+        xt, on = A("xt", 0, W3), A("on", 7, W3, 16)
         calls = {
-            "s0": lambda: act(A("sc", 0, W3), I(A("sp", 0, C), ou)),
-            "s1": lambda: act(A("sc", W3, 2 * W3), I(A("sp", C, 2 * C), ou)),
-            "p": lambda: act(A("hf", 0, W3), I(A("gg", 0, C), ou), AF.Identity, bias=kBi, scale=kSc),
-            "q": lambda: act(A("hf", W3, 2 * W3), I(A("gg", C, 2 * C), ou), AF.Identity, bias=kBi, scale=kSc),
-            "kai": lambda: tt(kai, I(A("kr", 0, C), ou), A("cm", 0, W3), O.mult),
-            "jm": lambda: ts(A("jm", 0, W3), kai, 7, O.bitwise_and),
-            "keepp": lambda: ts(A("hb", 0, W3), kai, kP, O.is_ge, 8192.0, O.mult),
-            "keepq": lambda: ts(A("hb", W3, 2 * W3), A("jm", 0, W3), kI, O.is_ge, 8192.0, O.mult),
-            "on": lambda: tt(on, A("sc", W3, 2 * W3), A("sc", 0, W3), O.is_gt),
-            "hbt": lambda: turn(A("hbt", 0, 2 * W3), A("hb", 0, 2 * W3)),
-            "ont": lambda: turn(A("hbt", 2 * W3, 3 * W3), on),
-            "hft": lambda: turn(A("hft", 0, 2 * W3), A("hf", 0, 2 * W3)),
-            "inv": lambda: ts(A("inv", 0, W3), kai, 0.0, O.is_equal, 43.0, O.mult),
-            "lt": lambda: act(A("lt", 64, 96), I(A("hbt", 2 * W3, 3 * W3), A("fin", 0, 2)), AF.Identity, bias=-4096.0, scale=8192.0),
-            "db": lambda: [act(A("db%d" % b, 0, C), A("pF%d" % b, 0, C), scale=0.5)
-                           for b in range(DB if t else 0, min(DB + 2, 4) if t else 2)],
-            "ab": lambda: scan(A("ab", 0, 2 * W3), A("hbt", 0, 2 * W3), A("hft", 0, 2 * W3), O.max, O.min),
-            "lh": lambda: tc(A("lh", 0, 64), I(A("ab", 0, 2 * W3), A("fin", 0, 4))),
-            "wv": lambda: tt(A("wv", 0, W3), A("inv", 0, W3), on, O.subtract),
+            "t0": lambda: turn(A("xt", 0, 32), A("order", 0, W3, PER)),
+            "t1": lambda: turn(A("xt", 32, 64), A("order", 1, W3, PER)),
+            "t2": lambda: turn(A("xt", 64, 96), A("order", 2, W3, PER)),
+            "down": lambda: scan(A("hd", 0, W3), A("dn", 0, W3), xt, O.add, O.max),
+            "keep": lambda: [ts(A("hb", a, e), A("hd", a, e), k, O.is_gt, 8192.0, O.mult) for a, e, k in ((0, 32, kT0), (32, W3, kT1))],
+            "on": lambda: tt(on, A("xt", 14, W3, 16), A("xt", 6, W3, 16), O.is_gt),
+            "lt": lambda: act(A("lt", 64, 96), I(A("on", 0, 128), A("fon", 0, 2)), AF.Identity, bias=-3072.0, scale=6144.0),
+            "db": lambda: [act(A("db%d" % b, 0, C), A("pF%d" % b, 0, C), scale=0.5) for b in range(DB if t else 4, 4)],
+            "ab": lambda: scan(A("ab", 0, W3), A("hb", 0, W3), xt, O.max, O.min),
+            "lh": lambda: ts(A("lh", 0, 64), I(A("ab", 0, 128), A("fin", 0, 4)), float(C), O.max),
+            "side": lambda: act(A("side", 0, 6), on, AF.Identity, bias=1.0, scale=-2.0),
+            "wt": lambda: tt(A("wt", 0, W3, 16), A("ab", L, W3, 16), A("side", 0, 6), O.mult),
             "li": lambda: turn(A("li", 0, 64), A("lh", 0, 64)),
             "ltt": lambda: turn(A("ltt", 64, 96), A("lt", 64, 96)),
             "lj": lambda: ts(A("lj", 0, 64), A("li", 0, 64), 511, O.bitwise_and),
             "bd0": lambda: tt(A("bd0", 0, NC), A("li", 32, 32 + NC), A("ltt", 64, 64 + NC), O.add),
             "own": lambda: tc(A("own%d" % t, 0, 64), A("lj", 0, 64)),
             "bt": lambda: tt(A("bt", 0, NC), A("bd0", 0, NC), A("li", 0, NC), O.max),
-            "bl": lambda: ts(A("bl", 0, NC), A("bt", 0, NC), 15, O.bitwise_and),
             "bh": lambda: ts(A("bh", 0, NC), A("bt", 0, NC), 496, O.bitwise_and),
-            "bu": lambda: tc(A("bu", 0, NC), A("bl", 0, NC)),
-            "bo": lambda: tt(A("bo", 0, NC), A("bh", 0, NC), A("tagq", 0, NC), O.add),
-            "mrow": lambda: turn(A("mrow", 0, W3), A("ab", 0, W3)),
-            "ix": lambda: tt(A("ix", 0, W3), I(A("posc", 0, C), ou), A("wv", 0, W3), O.add)}
+            "bu": lambda: tc(A("bu", 0, NC), A("bt", 0, NC)),
+            "bo": lambda: tt(A("bo", 0, NC), A("bh", 0, NC), A("tagq", 0, NC), O.add)}
         stay[0] = True
         for name in SLOTS.split():
             calls[name]()
         stay[0] = False
         sent = [send(T["came%d" % t][:, 0:32 + NC], A("own%d" % t, 0, 32 + NC), "arl%d" % t)]
         landing("arl%d" % t, width, [("came%d" % t, 0, 64, 1)], sent, 1400.0)
+        if t == 0:
+            scan_constants()
         parts = [(a, min(a + TG // 16, NC)) for a in range(0, NC, TG // 16)]
-        for a, e in parts[VV:]:
-            act(A("val", 16 * a, 16 * e), I(s16(9), A("bu", a, e)), AF.Identity, bias=16.0 * a - UP * t)
-        for b in range(min(DB + 2, 4) if t else 2, 4):
-            act(A("db%d" % b, 0, C), A("pF%d" % b, 0, C), scale=0.5)
+        for a, e in parts:
+            act(A("val", 16 * a, 16 * e), I(A("ends", 0, 16 * C), A("bu", a, e)), AF.Identity, bias=16.0 * a - UP * t)
         tab = A("tab", 0, 25 * TG)
 
         def lower(k):
@@ -639,13 +687,12 @@ def rank_program(g, core, T, topo):
                 act(A("zb", SL * (3 - b), SL * (4 - b)), other)
                 tt(out, A("zb", SL * (3 - b), SL * (4 - b)), z, O.add)
 
-        calls = {"ix": lambda: tt(A("ix", 0, W3), I(A("posc", 0, C), ou), A("wv", 0, W3), O.add),
-                 "val": lambda: ts(A("val", 0, TG), I(s16(9), A("bu", 0, TG // 16)), -UP * t, O.add),
-                 "iy": lambda: listed(A("iy", 0, W3), A("ix", 0, W3), W3),
-                 "pu": lambda: ts(A("pu", 0, 6), A("iy", 15, W3, 16), kS24, O.mult),
-                 "mrow": lambda: turn(A("mrow", 0, W3), A("ab", 0, W3)),
-                 "links": lambda: scatter(A("lrep", 0, 1800), A("pu", 0, 6), A("mrow", 0, W3)),
-                 "back": lambda: dma("s", A("llr", 0, 48), row5, 2600.0),
+        calls = {"wx": lambda: act(A("wx", 0, W3), I(A("wt", 0, W3), A("upl", 0, 6))),
+                 "u0": lambda: turn(A("met", 0, W3, PER), A("wx", 0, 32)),
+                 "u1": lambda: turn(A("met", 1, W3, PER), A("wx", 32, 64)),
+                 "u2": lambda: turn(A("met", 2, W3, PER), A("wx", 64, 96)),
+                 "wn": lambda: act(A("wn", 0, C), I(A("met", 0, C), A("rku", 0, 24))),
+                 "db": lambda: [act(A("db%d" % b, 0, C), A("pF%d" % b, 0, C), scale=0.5) for b in range(0 if t else 4)],
                  "ofu": lambda: ts(A("ofu", 0, NC), A("bo", 0, NC), TG / 16.0, O.mult)}
         stay[0] = True
         for name in SEARCH.split():
@@ -663,7 +710,16 @@ def rank_program(g, core, T, topo):
         for a in (0, 12 * TG):
             scan(A("ste", a, a + 12 * TG), A("one", 0, 12 * TG), A("tab", a, a + 12 * TG), O.add, O.min)
         ts(A("eu", 0, 24), A("ste", TG - 1, 24 * TG, TG), UP * t, O.add, SL - 1.0, O.min)
+
+        def links():
+            for a in range(0, C, WLP):
+                listed(A("wl", a, a + WLP), A("wn", a, a + WLP), WLP)
+            ts(A("an", 0, 24), A("wl", 15, C, 16), kSn, O.mult, 0.0, O.max)
+            ts(A("an", 24, 48), A("wl", 15, C, 16), kS, O.mult, 0.0, O.max)
+            tt(A("llr", 0, 48), A("ll", 0, 48), A("an", 0, 48), O.max)
+
         if last:
+            links()
             ts(A("ll", 0, 48), A("llr", 0, 48), 511, O.bitwise_and)
             fill(A("lo", 48, 64), 0.0)
             tc(A("lo", 0, 48), A("ll", 0, 48))
@@ -677,17 +733,19 @@ def rank_program(g, core, T, topo):
         x = lambda b, a, e: A("x%d" % (t + 1), 4 * a + b, 4 * e, 4)
         h = lambda b, a, e: I(A("hs%d" % b, 0, SL), A("eu", a // 16, e // 16))
         for b, k in GA:
-            if k < len(pieces):
-                act(A("ga%d" % b, *pieces[k]), h(b, *pieces[k]))
+            act(A("ga%d" % b, *pieces[k]), h(b, *pieces[k]))
         for b, k in STATE:
-            if k < len(pieces) or k == 2:
-                a, e = (pieces + ((0, C),))[k]
-                if b == 4:
-                    scores(t + 1, a, e)
-                elif (b, k) in GA:
-                    tt(x(b, a, e), A(OWN[b], a, e), A("ga%d" % b, a, e), O.add)
-                else:
-                    tt(x(b, a, e), h(b, a, e), A("fb%d" % b, a, e), O.add)
+            a, e = (pieces + ((0, C),))[k]
+            if b == 4:
+                scores(t + 1, a, e)
+            elif (b, k) in GA:
+                tt(x(b, a, e), A(OWN[b], a, e), A("ga%d" % b, a, e), O.add)
+            else:
+                tt(x(b, a, e), h(b, a, e), A("fb%d" % b, a, e), O.add)
+        if t == 0:
+            quant(A("qv", 0, 128), A("sv", 0, 128), A("vt", 0, 512))
+        if not last:
+            links()
         for a, e in pieces if last else ():
             dma("s", ext(T.oc[:, 4 * a:4 * e]), U8("qx%d" % R, a, e))
             act(A("ys", a, e), S(a, e))

@@ -1,26 +1,29 @@
 from concourse.mybir import dt, AluOpType as O, ActivationFunctionType as AF, AxisListType as AX
 
 N, C, L, M, R = 4, 384, 5, 64, 3
-PER = 3
-NC = (M + PER - 1) // PER
-SL = 16 * NC
-W3 = 32 * PER
+SL = L * M
+WT = 160
 TYPES = (4, 0, 1, 2, 3, 4, 2, 1, 0, 1, 0, 3, 3, 2, 0, 1)
 MEET = [(i, j) for _, i, j in sorted(((i + j, i, j) for i in range(L) for j in range(L)), reverse=True)]
 MEET = MEET[:18] + [None] + MEET[18:] + [None]
 NB = len(MEET)
 Z0 = 16 * (NB - 2)
-TG = 96
+TG = 80
 UP = 1024.0
 CL = 3 * C + 32
 KB = 2.0 ** 17
 ZA = 1
+ZP = 192
 HUGE = 2.0 ** 80
-WAKE, SLACK, AHEAD = 200.0, 0.0, 40
+WAKE = 200.0
+AHEAD = 40
 XROWS = (23, 22)
-ZROWS = (21, 20, 19, 18, 17)
+ZROWS = (16, 18, 19, 20, 21)
+ZRUNS = ((16, 17), (18, 22))
+ARUNS = ((0, 16), (17, 18), (22, 24))
+FIRST = 16
 APART = 4
-ZN = (0, 0, 0, 1, 1, 0, 1)
+ZN = (0, 0, 1, 1, 1, 1, 0)
 TILES = [(rows, max(128, 16 * min(max(rows), 24))) for rows in ([24, 23, 22, 21], [20, 19, 18, 17], [16, 15, 14, 13],
                                                               [12, 11, 10, 9], [8, 7, 6, 5], [4, 3, 2, 1])]
 
@@ -56,9 +59,9 @@ def _pool(pool, dtype, spec):
     SCRATCH[pool] = ("sbuf", [128, at], dtype)
 
 
-_own(BF, "x0:1536 x1:1536 x2:1536 x3:1536 ut:512 vt:512 et:516 ones:516 za:1408 zb:704 zt:1408")
+_own(BF, "x0:1536 x1:1536 x2:1536 x3:1536 ut:512 vt:512 et:516 ones:516 za:1280 zb:640 zt:1280")
 _own(BF, "fb0:384 fb1:384 fb2:384 fb3:384 db0:400 db1:400 db2:400 db3:400 bd:1024 bd1:512 mt:5632")
-_own(F32, "hs0:352 hs1:352 hs2:352 hs3:352 ga0:384 ga1:384 ga2:384 ga3:384 ys:384 lot:64")
+_own(F32, "hs0:336 hs1:336 hs2:336 hs3:336 ga2:384 ga3:384 ys:384 lot:64")
 _own(I32, "llr:48")
 _own(F32, "al:384 g32:768 k32:384 sp:768 ssp:384 sn:24 met:384")
 for _n, _k in (("w", 512), ("v", 128), ("u0", 128), ("u", 128), ("e", 512), ("z", SL), ("bd", 256), ("m", 1408)):
@@ -67,39 +70,38 @@ for _n, _k in (("w", 512), ("v", 128), ("u0", 128), ("u", 128), ("e", 512), ("z"
 for _t in range(R):
     _own(COD, "lc%d:384" % _t)
     _own("uint8", "ls%d:384" % _t)
-    _own(U16, "own%d:64 came%d:64" % (_t, _t))
+    _own(U16, "own%d:40 came%d:40" % (_t, _t))
 for _t in range(R + 1):
     _own(COD, "qx%d:384" % _t)
     _own("uint8", "sx%d:384" % _t)
 SCRATCH["gt"] = ("sbuf", [128, 48, 16], BF)
-_pool("poolf", F32, "col:32 s16:176 kd:72 cm:72 idr:384 b0:384 b1:384 b2:384 b3:384 w0:384 slm:24 pre:24 "
-      "npos:24 tagq:24 li2:24 li4:24 v0:384 v1:384 v2:384 v3:384 ssb:384 ms:384 "
-      "cnt:24 cna:24 rk:24 rk3:24 cs:384 order:384 xt:96 hd:96 ab:128 lt:96 ltt:96 bd0:24 bo:24 "
-      "side:6 wt:96 wx:96 wn:384 wl:384 lo:64")
-_pool("poolb", BF, "kt:384 kr:384 fl:384 cl:1184 r8b:384 kp:384 sk:384 gg:768 d1k:648 ne:648 ex:384 sg:3072 "
-      "eqs:384 junk:768 hb:96 on:128 dn:96 val:384 tmp:384")
-_own(BF, "tab:3200 one:3072 z0:384 zs:10768 ends:6144")
-_pool("pooli", I32, "pi:4 li5:8 li3:4 ll:48 an:48 lh:64 li:64 lj:64 bt:24 bh:24")
-_pool("poolu", U16, "upl:8 irep:26 blk:24 fin:4 fon:2 lu:48 cu:24 rku:24 prm:24 bu:24 ofu:24 eu:24")
-_pool("poolh", F16, "ste:3072 rs:2688")
+_pool("poolf", F32, "col:32 s16:176 kd:72 cm:72 idr:768 dd:768 slm:24 pre:24 "
+      "npos:24 tagq:24 li2:24 li4:24 ssb:384 ms:384 "
+      "cnt:24 cna:24 rk:24 rk3:24 cs:384 order:400 xt:160 xu:160 hd:160 ab:160 lt:32 bd0:24 bo:24 fr:256 fs:256 "
+      "side:8 wt:64 wx:64 wn:384 wl:384 lo:64")
+_pool("poolb", BF, "kt:384 kr:384 fp:768 v0:768 v1:384 v2:384 v3:384 p0:384 b0:384 b1:384 b2:384 b3:384 cl:1184 r8b:384 kp:384 sk:384 gg:768 d1k:648 ne:648 ex:384 sg:3072 "
+      "eqs:384 junk:768 on:160 dn:160 val:384 tmp:384")
+_own(BF, "tab:2000 one:960 z0:384 zs:10768 ends:6144")
+_pool("pooli", I32, "pi:4 li5:8 ll:48 an:48 lh:96 lj:40 bt:24 bh:24")
+_pool("poolu", U16, "upl:8 irep:26 blk:24 fin:8 lu:48 cu:24 cu2:24 du:24 rku:24 prm:24 bu:24 ofu:24 eu:24")
+_pool("poolh", F16, "ste:1920 rs:2688")
 PSUM = ("pS", "pC", "pF0", "pF1", "pF2", "pF3", "pG2", "pG3")
 OWN = ("pF0", "pF1", "pG2", "pG3")
-HALVES = ((0, 192), (192, C))
-PIECES = ((0, 256), (256, C))
-LATE = (200.0, 0.0)
-SLOTS = "t0 t1 t2 down on keep lt side ab lh ltt db li wt lj bd0 own bt bh bu bo"
-SEARCH = "ofu wx db s0 u0 u1 l1 u2 wn s1 l2 s2 l3 s3 z0 z1 z2 z3"
-WLP = 96
+PIECES = ((0, 128), (128, 256), (256, C))
+LATE = 200.0
+FIRSTS = "l0 l1 v0 l2 v1 m0 v2 w0 u0"
+KEYS = "s0 s1 m0 s2 m1 l0 m2"
+SLOTS = "c0 ta tb c1 down up on c2 lt side ab node lh wt wx db lj bd0 own bt met bh bu bo"
+SEARCH = "wa v0 wb v1 ofu v2 v3 db s0 w0 w1 l1 an s1 lr ll l2 lu s2 du z0 l3 z1 s3 z2 z3"
+ZS = (5, 10, 9)
 PE = 1.0
-LASTP = ((0, 256), (256, C))
 DB = 2
 CUT = 384
-CROSS = 200.0
-GA = ((3, 0), (2, 1), (3, 1))
-STATE = ((0, 2), (1, 2), (2, 0), (3, 0), (4, 0), (2, 1), (3, 1), (4, 1))
+GA = ((3, 0, 128), (3, 128, 256), (3, 256, C))
+STATE = ((0, 0, C), (1, 0, C), (2, 0, C), (3, 0, 128), (3, 128, 256), (4, 0, 128), (3, 256, C), (4, 128, 256), (4, 256, C))
 for _n in PSUM:
     SCRATCH[_n] = ("psum", [128, 512], F32)
-NDMA = 69
+NDMA = 71
 SEMAPHORES = (["qv_", "qa_", "qt_", "qp_", "lsent"] + ["arx%d" % t for t in range(R)] + ["arl%d" % t for t in range(R)]
               + ["d%d" % k for k in range(NDMA)])
 
@@ -116,7 +118,7 @@ def rank_program(g, core, T, topo):
     semof = {"v": "qv_", "a": "qa_", "t": "qt_", "p": "qp_"}
     count, known = {}, {q: {} for q in eng}
     clocks, hist, met, ops = {}, {}, {}, []
-    ndma, stay = [0], [False]
+    ndma, stay = [0], [""]
 
     def need(q, src, val):
         if known[q].get(src, 0) >= val:
@@ -166,13 +168,13 @@ def rank_program(g, core, T, topo):
         while len(out) < n:
             due, q = min((max(earliest[l[0]], free[q]), q) for q, l in line.items() if l and not left[l[0]])
             fits = [j for j in line[q][1:AHEAD] if not left[j] and ops[j]["kind"] == "call" and (q != "v" or ops[j]["hold"] < 250)
-                    and max(earliest[j], free[q]) < due and max(earliest[j], free[q]) + ops[j]["hold"] <= due + SLACK]
+                    and max(earliest[j], free[q]) < due and max(earliest[j], free[q]) + ops[j]["hold"] <= due]
             i = fits[0] if fits else line[q][0]
             line[q].remove(i)
             out.append(i)
             free[q] = max(earliest[i], free[q]) + ops[i]["hold"]
             for j in users[i]:
-                earliest[j] = max(earliest[j], free[q] + ops[i]["more"] + ((WAKE if ops[j]["q"] == q else CROSS) if ops[j]["deps"][i] else 0.0))
+                earliest[j] = max(earliest[j], free[q] + ops[i]["more"] + (WAKE if ops[j]["deps"][i] else 0.0))
                 left[j] -= 1
         return out
 
@@ -216,11 +218,11 @@ def rank_program(g, core, T, topo):
             hold = max(64.0, n * (rate if both else 1.0) * (1.0 if any(wide(r) for r in reads + writes if size(r) > 1) else 0.5))
         else:
             hold = max(64.0, n * rate) + 20.0 * (len(writes) - 1)
-        more = LATE[0] if isinstance(writes[0], list) else LATE[1] if any(isinstance(r, list) for r in reads) else 0.0
-        record(q, "kept" if stay[0] in (q, True) and q in ("v", stay[0]) else "call", fn, [tuple(r) for r in reads], [tuple(r) for r in writes], hold, more)
+        more = LATE if isinstance(writes[0], list) else 0.0
+        record(q, "kept" if q in stay[0] else "call", fn, [tuple(r) for r in reads], [tuple(r) for r in writes], hold, more)
 
     def dma(q, out, in_, more=3600.0):
-        record(q, "dma", lambda: eng[q].dma_start(out[0], in_[0]), in_[1], out[1], 1000.0 if q == "p" else 50.0, more)
+        record(q, "dma", lambda: eng[q].dma_start(out[0], in_[0]), in_[1], out[1], 50.0, more)
 
     def send(out, in_, sem):
         return record("p", "send", lambda: g.remote_dma(out, in_[0], T.sem[sem], T.sem.lsent, pid, rid, mask), in_[1], [], 1800.0 if sem == "arx0" else 1000.0)
@@ -282,8 +284,8 @@ def rank_program(g, core, T, topo):
     def fill(out, k):
         emit("v", lambda: V.memset(out[0], k), [], out[1])
 
-    def quant(q, s, x):
-        record("v", "call", lambda: V.quantize_mx(q[0], s[0], x[0]), rd(x), q[1] + s[1], 15.0 + 0.27 * size(x[1][0]))
+    def quant(q, s, x, kind="call"):
+        record("v", kind, lambda: V.quantize_mx(q[0], s[0], x[0]), rd(x), q[1] + s[1], 15.0 + 0.27 * size(x[1][0]))
 
     def act(out, in_, func=AF.Copy, bias=None, scale=None, accum=None):
         kw = {}
@@ -308,16 +310,16 @@ def rank_program(g, core, T, topo):
         record("p", "kept", lambda: g.affine_select(out[0], in_[0], pattern, cmp, 0.0, base, cm), in_[1], out[1],
                170.0 + 2 * size(out[1][0]))
 
-    (kI, kType, kG, kB0, kB1, kB2, kB3, kOff, kL, kU, kS, kSn, kK, kIb, kz, kKm, kN, kC, kT0, kT1, kE0, kE1) = [
-        A("col", k, k + 1) for k in range(22)]
+    (kI, kType, kD, kL, kS, kSn, kK, kIb, kz, kKm, kN, kOdd, kEven) = [A("col", k, k + 1) for k in range(13)]
+    begins = lambda k: {"scale": A("col", 16 + k, 17 + k), "bias": A("col", 21 + k, 22 + k)}
     s16 = lambda k: A("s16", 16 * k, 16 * k + 16)
     every = lambda n, r, s, w: (T[n][r:128:s, 0:w], [(n, 0, w, 1)])
     carried = lambda r: (T.al[r:128:8, 0:C], [("al", r, C, 8)])
 
-    dma("s", A("ut", 0, 512), ext(T.u[:, :]), 1500.0)
-    for q, (a, e) in zip("as", PIECES):
-        dma(q, A("x0", 4 * a, 4 * e), ext(T.x[:, 4 * a:4 * e]), 2000.0)
-    dma("a", A("llr", 0, 48), ext(T.nb[:, :]), 2400.0)
+    dma("s", A("ut", 0, 512), ext(T.u[:, :]), 3000.0)
+    for q, (a, e) in zip("as", ((0, 256), (256, C))):
+        dma(q, A("x0", 4 * a, 4 * e), ext(T.x[:, 4 * a:4 * e]), 3500.0)
+    dma("a", A("llr", 0, 48), ext(T.nb[:, :]), 3000.0)
 
     def late_loads():
         dma("s", U8("qw", 0, 512), ext(T.wc[:, :]))
@@ -332,7 +334,6 @@ def rank_program(g, core, T, topo):
     fill(A("ones", 0, 516), 1.0)
     iota(A("wn", 0, C), [[1, 16], [16, 24]], 0, 0, True)
     choose(A("et", 0, 516), A("ones", 0, 516), [[1, 516]], O.is_equal, -3, -4)
-
     choose(A("r8b", 0, C), A("ones", 0, C), [[0, C // 8], [1, 8]], O.not_equal, 0, 0)
     choose(half, ones, [[-16, 8], [0, 64]], O.is_ge, 0, 1)
     choose(blocks, half, [[16, 8], [0, 64]], O.is_ge, 15, -1)
@@ -340,8 +341,14 @@ def rank_program(g, core, T, topo):
     iota(A("li2", 0, 24), [[16, 24]], 0, 0, True)
 
     def later_on_g():
-        iota(A("li3", 0, 4), [[8, 2], [16, 2]], 1, 0)
-        iota(A("li4", 0, 24), [[0, 384 // TG], [-16, TG // 16]], TG - 1, 0, True)
+        for odd, (first, step) in enumerate(((96, -64), (16, 96))):
+            at = 128 * odd
+            for side in range(2):
+                iota(A("fr", at + 20 * side, at + 20 * side + 20), [[1, L], [32, 2], [step, 2]], first + 8 * side + 1, 0, True)
+                iota(A("fr", at + 40 + 24 * side, at + 64 + 24 * side), [[32, 2], [step, 2], [1, 6]], first + 8 * side + 1, 0, True)
+            iota(A("fr", at + 96, at + 120), [[32, 2], [step, 2], [0, 6]], first + 7, 0, True)
+        iota(A("idr", C, 2 * C), [[1, C]], C, 0, True)
+        iota(A("li4", 0, 24), [[0, 4], [-1, 6]], TG - 1, 0, True)
         for b in range(4):
             iota(A("db%d" % b, C, C + 16), [[0, 16]], 0, 0, True)
         iota(A("tab", 0, 25 * TG), [[0, 25 * TG]], 512, 0, True)
@@ -377,46 +384,43 @@ def rank_program(g, core, T, topo):
             zeros = A("z0", 0, e - a)
             dma("s", A("mt", a, e), (zeros[0], zeros[1] + [("x0", 0, 4 * C, 1)]), 2400.0)
         at += 4 * w
-    act(A("w0", 0, C), A("idr", 0, C), AF.Identity, bias=UP)
     put(A("met", 0, C), C, 0.0)
-    dma("s", carried(7), every("met", 7, 8, C), 2200.0)
+    dma("s", carried(6), every("met", 6, 8, C), 2200.0)
     ts(kS, kI, 14.5, O.is_gt, 1.0 / KB, O.max)
-    for side in range(2):
-        fill(A("d1k", 12 * NB * side, 12 * NB * (side + 1)), (1 - 2 * side) * HUGE)
-    for k, bias in enumerate((kB0, kB1, kB2, kB3)):
-        ts(bias, kType, L - 1.5 - k, O.is_lt, UP * (k + 2), O.mult)
+    for k in range(L):
+        ts(begins(k)["scale"], kType, L - 1.0 - k, O.is_equal)
     tc(A("kt", 0, C), I(s16(10), A("irep", 0, 24)))
     fill(A("kd", 0, 72, 3), 0.0)
     fill(A("cl", 61, CL, 48), 0.0)
+    for k in range(L):
+        ts(begins(k)["bias"], begins(k)["scale"], 808.0, O.mult, -1000.0, O.add)
+    ts(kD, begins(0)["scale"], -float(C), O.mult)
     listed(A("cs", 0, C), A("wn", 0, C), C)
     ts(A("kd", 1, 72, 3), A("ones", 0, 24), kS, O.mult)
 
     def small_constants():
         ts(A("prm", 0, 24), A("cs", 15, C, 16), kS, O.mult)
         ts(kKm, kI, 14.5, O.is_lt, KB - 1.0, O.mult)
-        ts(kOff, kType, UP, O.mult, -L * UP - 192.0, O.add)
+        for side in range(2):
+            fill(A("d1k", 12 * NB * side, 12 * NB * (side + 1)), (1 - 2 * side) * HUGE)
 
     def step_constants():
-        for k, bias in enumerate((kB0, kB1, kB2, kB3)):
-            act(A("b%d" % k, 0, C), A("idr", 0, C), AF.Identity, bias=bias)
+        act(A("b0", 0, C), A("idr", 0, C), AF.Identity, **begins(1))
+        act(A("p0", 0, C), A("idr", 0, C), AF.Identity, **begins(0))
+        for k in range(1, 4):
+            act(A("b%d" % k, 0, C), A("idr", 0, C), AF.Identity, **begins(k + 1))
 
     def late_constants():
-        ts(A("pi", 2, 3), A("pi", 0, 1), 31, O.bitwise_and)
-        ts(A("pi", 3, 4), kI, 1.0 / L, O.mult, -0.4, O.add)
-        tc(kC, A("pi", 2, 3))
-        ts(kG, A("pi", 3, 4), 32.0 - L, O.mult, kI, O.add)
-        ts(kU, A("pi", 3, 4), 32.0, O.mult, 6.0, O.add)
+        tc(A("blk", 0, 24), A("idr", 0, 24))
+        ts(A("pi", 2, 3), A("pi", 0, 1), 4, O.logical_shift_right, 1, O.bitwise_and)
+        tc(kOdd, A("pi", 2, 3))
 
-    def last_constants():
-        ts(A("fon", 0, 2), A("li3", 0, 2), kU, O.add)
-        ts(A("fin", 0, 4), A("li3", 0, 4), kG, O.add)
-
-    quant(A("qu0", 0, 128), A("su0", 0, 128), A("ut", 0, 512))
+    quant(A("qu0", 0, 128), A("su0", 0, 128), A("ut", 0, 512), "kept")
     tc(U32("qu", 0, 128), I(U32("qu0", 0, 128), A("upl", 0, 8)))
     act(A("su", 0, 128), I(A("su0", 0, 128), A("upl", 0, 8)))
     unpacking = lambda b: quant(A("qe", 128 * b, 128 * b + 128), A("se", 128 * b, 128 * b + 128), A("et", 3 - b, 515 - b))
 
-    S = lambda a, e: A("pC" if a else "pS", 0, e - a)
+    S = lambda a, e: A(("pS", "pF2", "pC")[a // 128], 0, e - a)
 
     def scores(t, a, e):
         qx, sx, w = A("qx%d" % t, a, e), A("sx%d" % t, a, e), "v" if t == R else "u"
@@ -456,28 +460,54 @@ def rank_program(g, core, T, topo):
         act(A("npos", 0, 24), A("li2", 0, 24), AF.Identity, scale=kK)
 
     def slot_constants():
-        for e, n in ((kE0, NC), (kE1, M // PER)):
-            act(e, kC, AF.Relu, bias=-HUGE * 2.0 ** 12 * (n - 1), scale=HUGE * 2.0 ** 12)
-        put(A("dn", 0, W3), W3, -HUGE)
-        for k, e in ((kT0, kE0), (kT1, kE1)):
-            act(k, e, AF.Identity, bias=4096.0)
+        act(kEven, kOdd, AF.Identity, bias=1.0, scale=-1.0)
+        for at in (0, 128):
+            put(A("fr", at + 88, at + 96), 8, 6.0)
+            put(A("fr", at + 120, at + 128), 8, 6.0)
+        put(A("order", 0, 16), 16, 0.0)
+        act(A("fs", 128, 256), A("fr", 128, 256), scale=kOdd)
+        act(A("fs", 0, 128), A("fr", 0, 128), scale=kEven)
+        put(A("dn", 0, WT), WT, -HUGE)
         act(kSn, kS, scale=-1.0)
-        act(kIb, kI, AF.Identity, bias=0.02, scale=-16.0 / TG)
-        put(A("dn", 0, W3, 8), W3 // 8, -HUGE * 2.0 ** 15)
-        put(A("dn", 1, W3, 8), W3 // 8, -HUGE / 2)
-        put(A("ab", W3, 128), 128 - W3, 0.0)
-        put(A("on", 0, 128), 128, 0.0)
-        put(A("wt", 0, W3), W3, 0.0)
+        act(kIb, kI, AF.Identity, bias=0.02, scale=-16.0 * L / TG)
+        put(A("dn", 0, WT, 8), WT // 8, -HUGE * 2.0 ** 15)
+        put(A("dn", 1, WT, 8), WT // 8, -HUGE / 2)
+        put(A("on", 0, WT), WT, 0.0)
+        put(A("dd", 0, 2 * C, 2), C, 0.0)
+        put(A("wt", 0, M), M, 0.0)
         act(A("tagq", 0, 24), A("li4", 0, 24), AF.Identity, bias=kIb, scale=16.0 / TG)
+        for b in range(4):
+            put(A("hs%d" % b, SL, SL + 16), 16, 0.0)
 
     def own_planes():
         for b in range(4):
-            if (b, 0) not in GA or (b, 1) not in GA:
+            if sum(e - a for k, a, e in GA if k == b) < C:
                 act(A("fb%d" % b, 0, C), A(OWN[b], 0, C))
 
-    def score_list():
-        act(A("ssp", 0, C), I(A("ssb", 0, C), A("prm", 0, 24)))
-        dma("s", A("sn", 0, 24), every("ssp", 0, 16, C), 2400.0)
+    def their_planes(first, end):
+        for b in range(first, end):
+            act(A("db%d" % b, 0, C), A("pF%d" % b, 0, C), scale=0.5)
+
+    def plain_links():
+        ts(A("ll", 0, 48), A("llr", 0, 48), 511, O.bitwise_and)
+
+    def link_lists():
+        tt(A("kd", 2, 72, 3), A("ll", 24, 48), A("ll", 0, 24), O.subtract)
+        tc(A("lu", 0, 48), A("ll", 0, 48))
+        ts(A("cl", 77, CL, 48), A("ll", 0, 24), -192.0, O.add)
+
+    def link_rows():
+        act(A("p0", 0, C), I(A("idr", 0, C), A("lu", 0, 24)), AF.Identity, **begins(0))
+        act(A("dd", 1, 2 * C, 2), I(A("idr", 0, 2 * C), A("du", 0, 24)), AF.Identity, scale=begins(0)["scale"], bias=kD)
+
+    def links_out():
+        turn(A("lot", 0, 64), A("lo", 0, 64))
+        for h in range(2):
+            dma("s", ext(T.ol[h:8:2, 0:512]), A("lot", 16 * h, 16 * h + 16))
+        for a in range(4):
+            for h in range(2):
+                dma("s", ext(T.ol[2 * a + h:2 * a + h + 1, 512:768]),
+                    (T.lot[32 * a:32 * a + 16, 32 + 16 * h:48 + 16 * h], [("lot", 32, 64, 1)]))
 
     trios = _trios()
     for t in range(R):
@@ -486,23 +516,29 @@ def rank_program(g, core, T, topo):
         if t == 0:
             for a, e in PIECES:
                 scores(0, a, e)
+            plain_links()
+            link_lists()
             step_constants()
-        if t:
+        else:
             planes(qx, sx, OWN)
-        ts(A("ll", 0, 48), A("llr", 0, 48), 511, O.bitwise_and)
-        tt(A("kd", 2, 72, 3), A("ll", 24, 48), A("ll", 0, 24), O.subtract)
-        ts(A("cl", 77, CL, 48), A("ll", 0, 24), -192.0, O.add)
-        tc(A("lu", 0, 48), A("ll", 0, 48))
         for a, e in PIECES:
-            ts(A("fl", a, e), S(a, e), 0.0, O.is_gt)
+            ts(A("fp", 2 * a, 2 * e, 2), S(a, e), 0.0, O.is_gt)
             act(A("ssb", a, e), S(a, e))
-        for a, e in PIECES:
-            listed(A("cl", 3 * a, 3 * e, 3), A("fl", a, e), e - a)
-        scan(A("cm", 0, 72), A("kd", 0, 72), A("cl", 45, CL, 16), O.mult, O.add)
-        ts(A("cu", 0, 24), A("cm", 2, 72, 3), 192.1, O.add)
+        calls = {
+            "l": lambda a, e: listed(A("cl", 3 * a, 3 * e, 3), A("fp", 2 * a, 2 * e, 2), e - a),
+            "v": lambda a, e: scan(A("v0", 2 * a, 2 * e), A("dd", 2 * a, 2 * e), A("fp", 2 * a, 2 * e), O.mult, O.add),
+            "m": lambda a, e: scan(A("cm", 0, 72), A("kd", 0, 72), A("cl", 45, CL, 16), O.mult, O.add),
+            "u": lambda a, e: ts(A("cu", 0, 24), A("cm", 2, 72, 3), 192.1, O.add),
+            "w": lambda a, e: ts(A("cu2", 0, 24), A("cm", 2, 72, 3), 2.0, O.mult, C + 1.1, O.add)}
+        stay[0] = "v" if t else ""
+        for name in FIRSTS.split():
+            if t or name[0] in "lmu":
+                calls[name[0]](*PIECES[int(name[1])])
+        stay[0] = ""
         if t == 0:
             small_constants()
-        score_list()
+        act(A("ssp", 0, C), I(A("ssb", 0, C), A("prm", 0, 24)))
+        dma("s", A("sn", 0, 24), every("ssp", 0, 16, C), 2400.0)
         codes = U8("qx%d" % t, 0, C)
         sent = [send(T["lc%d" % t][:, 0:C].bitcast(dt.uint8), (codes[0], codes[1] + [("ssp", 0, C, 1)]), "arx%d" % t),
                 send(T["ls%d" % t][:, 0:C], sx, "arx%d" % t)]
@@ -511,14 +547,15 @@ def rank_program(g, core, T, topo):
             later_on_g()
             meeting_constants()
         act(A("sp", 0, 768), I(A("ssb", 0, C), A("lu", 0, 48)))
-        dma("s", carried(6), every("sp", 6, 16, 2 * C), 2200.0)
-        for k in range(4):
-            tt(A("v%d" % k, 0, C), I(A("v%d" % (k - 1) if k else "w0", 0, C), A("cu", 0, 24)), A("b%d" % k, 0, C), O.max)
+        dma("s", carried(7), every("sp", 7, 16, 2 * C), 2200.0)
+        for k in range(1 if t else 0, 4):
+            win = I(A("v%d" % (k - 1) if k else "p0", 0, C), A("cu", 0, 24))
+            tt(A("v%d" % k, 0, C), I(A("v0", 0, 2 * C), A("cu2", 0, 24)) if t and k == 1 else win, A("b%d" % k, 0, C), O.max)
             if t == 0:
                 unpacking(k)
-        act(A("gg", 0, CUT), I(A("v3", 0, C), A("lu", 0, CUT // 16)), AF.Identity, bias=kOff)
+        act(A("gg", 0, CUT), I(A("v3", 0, C), A("lu", 0, CUT // 16)))
         for a, e in ((CUT, C + 256), (C + 256, 2 * C)):
-            ts(A("gg", a, e), I(A("v3", 0, C), A("lu", a // 16, e // 16)), kOff, O.add)
+            tc(A("gg", a, e), I(A("v3", 0, C), A("lu", a // 16, e // 16)))
         if t == 0:
             count_constants()
         for a, e in ((CUT, C + 256), (C + 256, 2 * C), (0, CUT)):
@@ -529,7 +566,7 @@ def rank_program(g, core, T, topo):
         if t:
             stay[0] = "a"
             own_planes()
-            stay[0] = False
+            stay[0] = ""
         else:
             planes(qx, sx, OWN)
         for x, ((r, s), (r2, s2)) in enumerate(trios):
@@ -539,15 +576,15 @@ def rank_program(g, core, T, topo):
             for k in range(2 if x == NB // 3 - 1 else 0):
                 tt(A("ne", x + NB // 3 * k, 24 * NB, NB), (T.gt[:, 0:24, r + k * s], [("gt", 0, C, 1)]),
                    (T.gt[:, 24:48, r2 + k * s2], [("gt", C, 2 * C, 1)]), O.not_equal)
-        for a, e in HALVES:
+        for a, e in PIECES:
             a, e = a // 16 * NB, e // 16 * NB
             for side in range(2):
                 at = 8 * NB * side
                 scan(A("zs", at + 16 * a, at + 16 * e, 16), A("ne", a, e), A("d1k", 12 * NB * side, 12 * NB * side + e - a),
                      O.mult, O.add, -(L + 1.0) * HUGE)
-        for a, e in HALVES:
+        for a, e in PIECES:
             scan(A("ex", a, e), A("r8b", a, e), A("zs", Z0 + NB * a, Z0 + NB * e, NB), O.mult, O.add)
-        for a, e in HALVES:
+        for a, e in PIECES:
             turn(A("kr", a, e), A("ex", a, e))
             act(A("k32", a, e), A("kr", a, e))
         dma("s", carried(0), every("k32", 0, 8, C), 2200.0)
@@ -555,14 +592,13 @@ def rank_program(g, core, T, topo):
             for a in range(4, 16, 4):
                 dma("s", A("ends", a * C, (a + 4) * C), A("ends", 0, 4 * C), 3000.0)
             late_loads()
-            tc(A("blk", 0, 24), A("idr", 0, 24))
             late_constants()
-        for a, e in HALVES:
-            listed(A("sk", a, e), A("kr", a, e), e - a)
-        tt(A("ms", *PIECES[0]), S(*PIECES[0]), A("kr", *PIECES[0]), O.min)
-        tt(A("slm", 0, 24), A("sk", 15, C, 16), A("sn", 0, 24), O.min)
-        for a, e in PIECES[1:]:
-            tt(A("ms", a, e), S(a, e), A("kr", a, e), O.min)
+        calls = {"s": lambda a, e: listed(A("sk", a, e), A("kr", a, e), e - a),
+                 "m": lambda a, e: tt(A("ms", a, e), S(a, e), A("kr", a, e), O.min),
+                 "l": lambda a, e: tt(A("slm", 0, 24), A("sk", 15, C, 16), A("sn", 0, 24), O.min)}
+        stay[0] = "v"
+        for name in KEYS.split():
+            calls[name[0]](*PIECES[int(name[1])])
         spot, at = {}, 0
         for rows, w in TILES:
             for i, c in enumerate(rows):
@@ -576,11 +612,12 @@ def rank_program(g, core, T, topo):
                 act(sg(c), A("ms", 0, 16 * c), AF.Sign, bias=score(c), scale=-1.0)
             if d:
                 act(spot[d], sg(d), AF.Relu, accum=A("cna", d, d + 1))
-        at, sums, rows_left = 0, [], list(ZROWS)
+        at, sums, rows_left = 0, [], sorted(ZROWS, reverse=True)
+        below = lambda c: ts(spot[c], A("ms", 0, 16 * c), score(c), O.is_lt)
 
         def row_sums(n):
             for c in rows_left[:n]:
-                e = C * (c - min(ZROWS) + 1)
+                e = C * (ZROWS.index(c) + 1)
                 scan(A("rs", e - 16 * c, e), A("ones", 0, 16 * c), spot[c], O.mult, O.add)
             del rows_left[:n]
 
@@ -589,20 +626,19 @@ def rank_program(g, core, T, topo):
             quant(A("qm", a, a + w), A("sm", a, a + w), A("mt", at, at + 4 * w))
             mm(A("pC", 0, w), A("qbd", s, s + 128), A("sbd", s, s + 128), A("qm", a, a + w), A("sm", a, a + w), k == 0, k == 5)
 
-        stay[0] = True
+        if FIRST not in alone:
+            below(FIRST)
         for k, (rows, w) in enumerate(TILES):
             for c in sorted(rows, key=lambda c: c == 24):
                 if c == 24:
                     tt(spot[c], I(A("slm", 0, 24), A("blk", 0, 24)), A("ms", 0, C), O.is_gt)
-                elif c not in alone:
-                    ts(spot[c], A("ms", 0, 16 * c), score(c), O.is_lt)
+                elif c not in alone and c != FIRST:
+                    below(c)
                 if t == 0 and c in (24, 20):
                     a = 128 if c == 24 else 0
                     quant(A("qbd", a, a + 128), A("sbd", a, a + 128), A("bd", 4 * a, 4 * a + 512))
-                if sums and c not in alone:
+                if sums and c not in alone and c != FIRST:
                     column_sums(*sums.pop(0))
-            if k == 2:
-                scan(A("eqs", 0, C), A("kp", 0, C), spot[24], O.mult, O.add)
             row_sums(ZN[k])
             while sums:
                 column_sums(*sums.pop(0))
@@ -615,10 +651,14 @@ def rank_program(g, core, T, topo):
         row_sums(ZN[6])
         column_sums(*sums.pop())
         row_sums(len(ZROWS))
+        scan(A("eqs", 0, C), A("kp", 0, C), spot[24], O.mult, O.add)
+        for a, e in ZRUNS:
+            k = ZROWS.index(a)
+            ts(A("cnt", a, e), A("rs", C * k + C - 1, C * (k + e - a), C), kN, O.mult)
         tt(A("pre", 0, 24), A("npos", 0, 24), A("eqs", 15, C, 16), O.subtract)
-        tc(A("cna", min(ZROWS), max(ZROWS) + 1), A("rs", C - 1, C * len(ZROWS), C))
-        stay[0] = False
-        act(A("cnt", 0, 24), A("cna", 0, 24), AF.Identity, scale=kN)
+        stay[0] = ""
+        for a, e in ARUNS:
+            act(A("cnt", a, e), A("cna", a, e), AF.Identity, scale=kN)
         if t == 0:
             slot_constants()
             own_planes()
@@ -626,133 +666,131 @@ def rank_program(g, core, T, topo):
         tt(A("rk3", 0, 24), A("cnt", 0, 24), A("pre", 0, 24), O.add)
         tt(A("rk", 0, 24), A("rk3", 0, 24), A("cs", 15, C, 16), O.add)
         ts(A("rku", 0, 24), A("rk", 0, 24), kS, O.mult, kz, O.add)
-        scatter(A("order", 0, C), A("rku", 0, 24), A("al", 0, C))
-        if t == 0:
-            last_constants()
+        scatter(A("order", 16, 16 + C), A("rku", 0, 24), A("al", 0, C))
         planes(A("lc%d" % t, 0, C), A("ls%d" % t, 0, C))
-        for b in range(DB if t else 0):
-            act(A("db%d" % b, 0, C), A("pF%d" % b, 0, C), scale=0.5)
-        pieces = LASTP if last else PIECES
-        xt, on = A("xt", 0, W3), A("on", 7, W3, 16)
+        their_planes(0, DB if t else 0)
+        xt, on = A("xt", 0, WT), A("on", 7, WT, 16)
         calls = {
-            "t0": lambda: turn(A("xt", 0, 32), A("order", 0, W3, PER)),
-            "t1": lambda: turn(A("xt", 32, 64), A("order", 1, W3, PER)),
-            "t2": lambda: turn(A("xt", 64, 96), A("order", 2, W3, PER)),
-            "down": lambda: scan(A("hd", 0, W3), A("dn", 0, W3), xt, O.add, O.max),
-            "keep": lambda: [ts(A("hb", a, e), A("hd", a, e), k, O.is_gt, 8192.0, O.mult) for a, e, k in ((0, 32, kT0), (32, W3, kT1))],
-            "on": lambda: tt(on, A("xt", 14, W3, 16), A("xt", 6, W3, 16), O.is_gt),
-            "lt": lambda: act(A("lt", 64, 96), I(A("on", 0, 128), A("fon", 0, 2)), AF.Identity, bias=-3072.0, scale=6144.0),
-            "db": lambda: [act(A("db%d" % b, 0, C), A("pF%d" % b, 0, C), scale=0.5) for b in range(DB if t else 4, 4)],
-            "ab": lambda: scan(A("ab", 0, W3), A("hb", 0, W3), xt, O.max, O.min),
-            "lh": lambda: ts(A("lh", 0, 64), I(A("ab", 0, 128), A("fin", 0, 4)), float(C), O.max),
-            "side": lambda: act(A("side", 0, 6), on, AF.Identity, bias=1.0, scale=-2.0),
-            "wt": lambda: tt(A("wt", 0, W3, 16), A("ab", L, W3, 16), A("side", 0, 6), O.mult),
-            "li": lambda: turn(A("li", 0, 64), A("lh", 0, 64)),
-            "ltt": lambda: turn(A("ltt", 64, 96), A("lt", 64, 96)),
-            "lj": lambda: ts(A("lj", 0, 64), A("li", 0, 64), 511, O.bitwise_and),
-            "bd0": lambda: tt(A("bd0", 0, NC), A("li", 32, 32 + NC), A("ltt", 64, 64 + NC), O.add),
-            "own": lambda: tc(A("own%d" % t, 0, 64), A("lj", 0, 64)),
-            "bt": lambda: tt(A("bt", 0, NC), A("bd0", 0, NC), A("li", 0, NC), O.max),
-            "bh": lambda: ts(A("bh", 0, NC), A("bt", 0, NC), 496, O.bitwise_and),
-            "bu": lambda: tc(A("bu", 0, NC), A("bt", 0, NC)),
-            "bo": lambda: tt(A("bo", 0, NC), A("bh", 0, NC), A("tagq", 0, NC), O.add)}
-        stay[0] = True
+            "c0": lambda: t or tt(A("fr", 0, 128), A("fs", 0, 128), A("fs", 128, 256), O.add),
+            "c1": lambda: t or listed(A("fs", 0, 128), A("fr", 0, 128), 128),
+            "c2": lambda: t or ts(A("fin", 0, 8), A("fs", 15, 128, 16), kS, O.mult),
+            "ta": lambda: turn(A("xt", 0, 96), A("order", 0, 96)),
+            "tb": lambda: turn(A("xt", 96, WT), A("order", 16, 80)),
+            "down": lambda: scan(A("hd", 0, WT), A("dn", 0, WT), xt, O.add, O.max),
+            "up": lambda: ts(A("xu", 0, WT), xt, 4096.0, O.add),
+            "on": lambda: tt(on, A("xt", 15, WT, 16), A("xt", 7, WT, 16), O.is_gt),
+            "lt": lambda: act(A("lt", 0, 32), I(A("on", 0, WT), A("fin", 6, 8)), AF.Identity, bias=-3072.0, scale=6144.0),
+            "db": lambda: their_planes(DB if t else 4, 4),
+            "ab": lambda: scan(A("ab", 0, WT), A("hd", 0, WT), A("xu", 0, WT), O.max, O.min),
+            "lh": lambda: ts(A("lh", 0, 96), I(A("ab", 0, WT), A("fin", 0, 6)), -4096.0, O.add, float(C), O.max),
+            "side": lambda: act(A("side", 0, 4), A("on", 103, WT, 16), AF.Identity, bias=1.0, scale=-2.0),
+            "node": lambda: act(A("side", 4, 8), A("ab", 96 + L, WT, 16), AF.Relu, bias=-4096.0),
+            "wt": lambda: tt(A("wt", 0, M, 16), A("side", 4, 8), A("side", 0, 4), O.mult),
+            "wx": lambda: act(A("wx", 0, M), I(A("wt", 0, M), A("upl", 0, 4))),
+            "met": lambda: turn(A("met", 0, M), A("wx", 0, M)),
+            "lj": lambda: ts(A("lj", 0, 40), A("lh", 0, 40), 511, O.bitwise_and),
+            "bd0": lambda: tt(A("bd0", 0, 24), A("lh", 64, 88), A("lt", 0, 24), O.add),
+            "own": lambda: tc(A("own%d" % t, 0, 40), A("lj", 0, 40)),
+            "bt": lambda: tt(A("bt", 0, 24), A("bd0", 0, 24), A("lh", 40, 64), O.max),
+            "bh": lambda: ts(A("bh", 0, 24), A("bt", 0, 24), 496, O.bitwise_and),
+            "bu": lambda: tc(A("bu", 0, 24), A("bt", 0, 24)),
+            "bo": lambda: tt(A("bo", 0, 24), A("bh", 0, 24), A("tagq", 0, 24), O.add)}
+        stay[0] = "v"
         for name in SLOTS.split():
             calls[name]()
-        stay[0] = False
-        sent = [send(T["came%d" % t][:, 0:32 + NC], A("own%d" % t, 0, 32 + NC), "arl%d" % t)]
-        landing("arl%d" % t, width, [("came%d" % t, 0, 64, 1)], sent, 1400.0)
+        stay[0] = ""
+        sent = [send(T["came%d" % t][:, 0:40], A("own%d" % t, 0, 40), "arl%d" % t)]
+        landing("arl%d" % t, width, [("came%d" % t, 0, 40, 1)], sent, 1400.0)
         if t == 0:
             scan_constants()
-        parts = [(a, min(a + TG // 16, NC)) for a in range(0, NC, TG // 16)]
-        for a, e in parts:
-            act(A("val", 16 * a, 16 * e), I(A("ends", 0, 16 * C), A("bu", a, e)), AF.Identity, bias=16.0 * a - UP * t)
+        piece = lambda n, k: A(n, TG * k, TG * k + TG)
+        part = lambda n, k: A(n, 6 * k, 6 * k + L)
         tab = A("tab", 0, 25 * TG)
 
+        def value(k):
+            act(piece("val", k), I(A("ends", 0, 16 * C), part("bu", k)), AF.Identity, bias=TG * k - UP * t)
+
         def lower(k):
-            a, e = parts[k]
-            tt(A("tmp", 16 * a, 16 * e), I(tab, A("ofu", a, e)), A("val", 16 * a, 16 * e), O.min)
+            tt(piece("tmp", k), I(tab, part("ofu", k)), piece("val", k), O.min)
 
         def store(k):
-            a, e = parts[k]
-            scatter(tab, A("ofu", a, e), A("tmp" if k else "val", 16 * a, 16 * e))
+            scatter(tab, part("ofu", k), piece("tmp" if k else "val", k))
 
         def z_plane(b):
             z, win = A("za", SL * b, SL * b + SL), A("db%d" % b, 0, C + 16)
-            act(z, I(win, A("came%d" % t, 0, NC)))
-            other, out = I(win, A("came%d" % t, 32, 32 + NC)), A("zt", b, 4 * SL, 4)
+            act(z, I(win, A("came%d" % t, 0, 20)))
+            other, out = I(win, A("came%d" % t, 20, 40)), A("zt", b, 4 * SL, 4)
             if b < 4 - ZA:
                 tt(out, other, z, O.add)
             else:
                 act(A("zb", SL * (3 - b), SL * (4 - b)), other)
                 tt(out, A("zb", SL * (3 - b), SL * (4 - b)), z, O.add)
 
-        calls = {"wx": lambda: act(A("wx", 0, W3), I(A("wt", 0, W3), A("upl", 0, 6))),
-                 "u0": lambda: turn(A("met", 0, W3, PER), A("wx", 0, 32)),
-                 "u1": lambda: turn(A("met", 1, W3, PER), A("wx", 32, 64)),
-                 "u2": lambda: turn(A("met", 2, W3, PER), A("wx", 64, 96)),
-                 "wn": lambda: act(A("wn", 0, C), I(A("met", 0, C), A("rku", 0, 24))),
-                 "db": lambda: [act(A("db%d" % b, 0, C), A("pF%d" % b, 0, C), scale=0.5) for b in range(0 if t else 4)],
-                 "ofu": lambda: ts(A("ofu", 0, NC), A("bo", 0, NC), TG / 16.0, O.mult)}
-        stay[0] = True
+        calls = {"wa": lambda: act(A("wn", 0, 192), I(A("met", 0, C), A("rku", 0, 12))),
+                 "wb": lambda: act(A("wn", 192, C), I(A("met", 0, C), A("rku", 12, 24))),
+                 "w0": lambda: listed(A("wl", 0, 192), A("wn", 0, 192), 192),
+                 "w1": lambda: listed(A("wl", 192, C), A("wn", 192, C), 192),
+                 "an": lambda: [ts(A("an", 0, 24), A("wl", 15, C, 16), kSn, O.mult, 0.0, O.max),
+                                ts(A("an", 24, 48), A("wl", 15, C, 16), kS, O.mult, 0.0, O.max)],
+                 "lr": lambda: tt(A("llr", 0, 48), A("ll", 0, 48), A("an", 0, 48), O.max),
+                 "ll": plain_links,
+                 "lu": lambda: last or link_lists(),
+                 "du": lambda: last or ts(A("du", 0, 24), A("kd", 2, 72, 3), float(C), O.add),
+                 "db": lambda: their_planes(0, 0 if t else 4),
+                 "ofu": lambda: ts(A("ofu", 0, 24), A("bo", 0, 24), TG / 16.0, O.mult)}
+        stay[0] = "v"
         for name in SEARCH.split():
             if name in calls:
                 calls[name]()
             else:
-                {"l": lower, "s": store, "z": z_plane}[name[0]](int(name[1]))
-        stay[0] = False
-        quant(A("qz", 0, SL), A("sz", 0, SL), A("zt", 0, 4 * SL))
+                {"l": lower, "s": store, "z": z_plane, "v": value}[name[0]](int(name[1]))
+        stay[0] = ""
+        edges = [TG * sum(ZS[:k]) for k in range(len(ZS) + 1)]
+        least = lambda a, e: scan(A("ste", a, e), A("one", 0, e - a), A("tab", a, e), O.add, O.min)
+        least(edges[0], edges[1])
+        w = lambda b: (A("qw", 128 * b, 128 * b + 128), A("sw", 128 * b, 128 * b + 128))
+        for a, e, bank in ((0, ZP, "pF0"), (ZP, SL, "pS")):
+            quant(A("qz", a, e), A("sz", a, e), A("zt", 4 * a, 4 * e))
+            mm(A(bank, 0, e - a), *w(0), A("qz", a, e), A("sz", a, e))
+        if not last:
+            link_rows()
+        for b in range(1, 4):
+            mm(A("pF%d" % b, 0, SL), *w(b), A("qz", 0, SL), A("sz", 0, SL))
         for b in range(4):
-            mm(A("pF%d" % b, 0, SL), A("qw", 128 * b, 128 * b + 128), A("sw", 128 * b, 128 * b + 128),
-               A("qz", 0, SL), A("sz", 0, SL))
-        for b in range(4):
-            act(A("hs%d" % b, 0, SL), A("pF%d" % b, 0, SL), scale=0.03125)
-        for a in (0, 12 * TG):
-            scan(A("ste", a, a + 12 * TG), A("one", 0, 12 * TG), A("tab", a, a + 12 * TG), O.add, O.min)
-        ts(A("eu", 0, 24), A("ste", TG - 1, 24 * TG, TG), UP * t, O.add, SL - 1.0, O.min)
-
-        def links():
-            for a in range(0, C, WLP):
-                listed(A("wl", a, a + WLP), A("wn", a, a + WLP), WLP)
-            ts(A("an", 0, 24), A("wl", 15, C, 16), kSn, O.mult, 0.0, O.max)
-            ts(A("an", 24, 48), A("wl", 15, C, 16), kS, O.mult, 0.0, O.max)
-            tt(A("llr", 0, 48), A("ll", 0, 48), A("an", 0, 48), O.max)
-
-        if last:
-            links()
-            ts(A("ll", 0, 48), A("llr", 0, 48), 511, O.bitwise_and)
-            fill(A("lo", 48, 64), 0.0)
-            tc(A("lo", 0, 48), A("ll", 0, 48))
-            turn(A("lot", 0, 64), A("lo", 0, 64))
-            for h in range(2):
-                dma("s", ext(T.ol[h:8:2, 0:512]), A("lot", 16 * h, 16 * h + 16))
-            for a in range(4):
-                for h in range(2):
-                    dma("s", ext(T.ol[2 * a + h:2 * a + h + 1, 512:768]),
-                        (T.lot[32 * a:32 * a + 16, 32 + 16 * h:48 + 16 * h], [("lot", 32, 64, 1)]))
+            for k in range(L):
+                at = A("pS", M * k - ZP, M * k + M - ZP) if b == 0 and M * k >= ZP else A("pF%d" % b, M * k, M * k + M)
+                act(A("hs%d" % b, k, SL, L), at, scale=0.03125)
+        for a, e in zip(edges[1:], edges[2:]):
+            least(a, e)
+        ts(A("eu", 0, 24), A("ste", TG - 1, 24 * TG, TG), UP * t, O.add, float(SL), O.min)
         x = lambda b, a, e: A("x%d" % (t + 1), 4 * a + b, 4 * e, 4)
-        h = lambda b, a, e: I(A("hs%d" % b, 0, SL), A("eu", a // 16, e // 16))
-        for b, k in GA:
-            act(A("ga%d" % b, *pieces[k]), h(b, *pieces[k]))
-        for b, k in STATE:
-            a, e = (pieces + ((0, C),))[k]
+        h = lambda b, a, e: I(A("hs%d" % b, 0, SL + 16), A("eu", a // 16, e // 16))
+        for b, a, e in GA:
+            act(A("ga%d" % b, a, e), h(b, a, e))
+        for b, a, e in STATE:
             if b == 4:
                 scores(t + 1, a, e)
-            elif (b, k) in GA:
+            elif (b, a, e) in GA:
                 tt(x(b, a, e), A(OWN[b], a, e), A("ga%d" % b, a, e), O.add)
             else:
                 tt(x(b, a, e), h(b, a, e), A("fb%d" % b, a, e), O.add)
+            if last and b == 0:
+                fill(A("lo", 48, 64), 0.0)
+                tc(A("lo", 0, 48), A("ll", 0, 48))
+            if last and b == 1:
+                links_out()
         if t == 0:
             quant(A("qv", 0, 128), A("sv", 0, 128), A("vt", 0, 512))
-        if not last:
-            links()
-        for a, e in pieces if last else ():
+        for a, e in ((0, 192), (192, C)) if not last else ():
+            tt(A("fp", 2 * a + 1, 2 * e, 2), A("p0", a, e), A("b0", a, e), O.max)
+        for a, e in PIECES if last else ():
             dma("s", ext(T.oc[:, 4 * a:4 * e]), U8("qx%d" % R, a, e))
             act(A("ys", a, e), S(a, e))
-            dma("a", ext(T.y[:, a:e]), A("ys", a, e))
+        for k in range(4 if last else 0):
+            dma("s", ext(T.osc[4 * k:4 * k + 4, :]), (T["sx%d" % R][32 * k:32 * k + 4, 0:C], [("sx%d" % R, 0, C, 1)]))
+        for a, e in PIECES if last else ():
+            dma("a" if e == C else "s", ext(T.y[:, a:e]), A("ys", a, e))
 
-    for k in range(4):
-        dma("s", ext(T.osc[4 * k:4 * k + 4, :]), (T["sx%d" % R][32 * k:32 * k + 4, 0:C], [("sx%d" % R, 0, C, 1)]))
     issue()
     g.wait_ge(T.sem.lsent, R * 3 * width)
     for t in range(R):

from concourse.mybir import dt, AluOpType as O, ActivationFunctionType as AF, AxisListType as AX

N, C, L, M, R = 4, 384, 5, 64, 3
SL = L * M
WT = 160
TYPES = (4, 0, 1, 2, 3, 4, 2, 1, 0, 1, 0, 3, 3, 2, 0, 1)
MEET = [(i, j) for _, i, j in sorted(((i + j, i, j) for i in range(L) for j in range(L)), reverse=True)]
MEET = MEET[:18] + [None] + MEET[18:] + [None]
NB = len(MEET)
Z0 = 16 * (NB - 2)
TG = 80
UP = 1024.0
CL = 3 * C + 32
KB = 2.0 ** 17
ZA = 1
ZP = 192
HUGE = 2.0 ** 80
WAKE = 200.0
AHEAD = 40
XROWS = (23, 22)
ZROWS = (16, 18, 19, 20, 21)
ZRUNS = ((16, 17), (18, 22))
ARUNS = ((0, 16), (17, 18), (22, 24))
FIRST = 16
APART = 4
ZN = (0, 0, 1, 1, 1, 1, 0)
TILES = [(rows, max(128, 16 * min(max(rows), 24))) for rows in ([24, 23, 22, 21], [20, 19, 18, 17], [16, 15, 14, 13],
                                                              [12, 11, 10, 9], [8, 7, 6, 5], [4, 3, 2, 1])]


def _trios():
    runs = {tuple(TYPES[r + s * k] for k in range(3)): (r, s) for s in range(1, 8) for r in range(16 - 2 * s)}
    out = []
    for x in range(NB // 3):
        at = [x + NB // 3 * k for k in range(3)]
        fit = [(a, b) for a in runs for b in runs
               if all(MEET[e] == (a[k], b[k]) if MEET[e] else e == NB - 1 or MEET.index((a[k], b[k])) > e
                      for k, e in enumerate(at))]
        out.append((runs[fit[0][0]], runs[fit[0][1]]))
    return out


F32, BF, I32, U16, F16, COD = "float32", "bfloat16", "int32", "uint16", "float16", "float8_e4m3fn_x4"
SCRATCH, PLACE = {}, {}


def _own(dtype, spec):
    for item in spec.split():
        name, cols = item.split(":")
        SCRATCH[name] = ("sbuf", [128, int(cols)], dtype)


def _pool(pool, dtype, spec):
    at = 0
    for item in spec.split():
        name, cols = item.split(":")
        PLACE[name] = (pool, at)
        at += (int(cols) + 31) // 32 * 32
    SCRATCH[pool] = ("sbuf", [128, at], dtype)


_own(BF, "x0:1536 x1:1536 x2:1536 x3:1536 ut:512 vt:512 et:516 ones:516 za:1280 zb:640 zt:1280")
_own(BF, "fb0:384 fb1:384 fb2:384 fb3:384 db0:400 db1:400 db2:400 db3:400 bd:1024 bd1:512 mt:5632")
_own(F32, "hs0:336 hs1:336 hs2:336 hs3:336 ga2:384 ga3:384 ys:384 lot:64")
_own(I32, "llr:48")
_own(F32, "al:384 g32:768 k32:384 sp:768 ssp:384 sn:24 met:384")
for _n, _k in (("w", 512), ("v", 128), ("u0", 128), ("u", 128), ("e", 512), ("z", SL), ("bd", 256), ("m", 1408)):
    _own(COD, "q%s:%d" % (_n, _k))
    _own("uint8", "s%s:%d" % (_n, _k))
for _t in range(R):
    _own(COD, "lc%d:384" % _t)
    _own("uint8", "ls%d:384" % _t)
    _own(U16, "own%d:40 came%d:40" % (_t, _t))
for _t in range(R + 1):
    _own(COD, "qx%d:384" % _t)
    _own("uint8", "sx%d:384" % _t)
SCRATCH["gt"] = ("sbuf", [128, 48, 16], BF)
_pool("poolf", F32, "col:32 s16:176 kd:72 cm:72 idr:768 dd:768 slm:24 pre:24 "
      "npos:24 tagq:24 li2:24 li4:24 ssb:384 ms:384 "
      "cnt:24 cna:24 rk:24 rk3:24 cs:384 order:400 xt:160 xu:160 hd:160 ab:160 lt:32 bd0:24 bo:24 fr:256 fs:256 "
      "side:8 wt:64 wx:64 wn:384 wl:384 lo:64")
_pool("poolb", BF, "kt:384 kr:384 fp:768 v0:768 v1:384 v2:384 v3:384 p0:384 b0:384 b1:384 b2:384 b3:384 cl:1184 r8b:384 kp:384 sk:384 gg:768 d1k:648 ne:648 ex:384 sg:3072 "
      "eqs:384 junk:768 on:160 dn:160 val:384 tmp:384")
_own(BF, "tab:2000 one:960 z0:384 zs:10768 ends:6144")
_pool("pooli", I32, "pi:4 li5:8 ll:48 an:48 lh:96 lj:40 bt:24 bh:24")
_pool("poolu", U16, "upl:8 irep:26 blk:24 fin:8 lu:48 cu:24 cu2:24 du:24 rku:24 prm:24 bu:24 ofu:24 eu:24")
_pool("poolh", F16, "ste:1920 rs:2688")
PSUM = ("pS", "pC", "pF0", "pF1", "pF2", "pF3", "pG2", "pG3")
OWN = ("pF0", "pF1", "pG2", "pG3")
PIECES = ((0, 128), (128, 256), (256, C))
LATE = 200.0
FIRSTS = "l0 l1 v0 l2 v1 m0 v2 w0 u0"
KEYS = "s0 s1 m0 s2 m1 l0 m2"
SLOTS = "c0 ta tb c1 down up on c2 lt side ab node lh wt wx db lj bd0 own bt met bh bu bo"
SEARCH = "wa v0 wb v1 ofu v2 v3 db s0 w0 w1 l1 an s1 lr ll l2 lu s2 du z0 l3 z1 s3 z2 z3"
ZS = (5, 10, 9)
PE = 1.0
DB = 2
CUT = 384
GA = ((3, 0, 128), (3, 128, 256), (3, 256, C))
STATE = ((0, 0, C), (1, 0, C), (2, 0, C), (3, 0, 128), (3, 128, 256), (4, 0, 128), (3, 256, C), (4, 128, 256), (4, 256, C))
for _n in PSUM:
    SCRATCH[_n] = ("psum", [128, 512], F32)
NDMA = 71
SEMAPHORES = (["qv_", "qa_", "qt_", "qp_", "lsent"] + ["arx%d" % t for t in range(R)] + ["arl%d" % t for t in range(R)]
              + ["d%d" % k for k in range(NDMA)])


def rank_program(g, core, T, topo):
    rank = T.rank_of(core)
    if rank is None:
        return
    nxt = T.cores[(rank + 1) % N]
    rid, pid = topo.addr(nxt)[:2]
    mask, width = topo.mask(core, nxt), len(topo.engines(core, nxt))

    eng = {"v": g.vector, "a": g.scalar, "t": g.tensor, "p": g, "s": g.sync}
    semof = {"v": "qv_", "a": "qa_", "t": "qt_", "p": "qp_"}
    count, known = {}, {q: {} for q in eng}
    clocks, hist, met, ops = {}, {}, {}, []
    ndma, stay = [0], [""]

    def need(q, src, val):
        if known[q].get(src, 0) >= val:
            return
        eng[q].wait_ge(T.sem[src], val)
        for s, n in clocks.get((src, val), {src: val}).items():
            if n > known[q].get(s, 0):
                known[q][s] = n

    def meet(x, y):
        if x[0] >= y[1] or y[0] >= x[1] or x[2] == y[2] and (x[0] - y[0]) % x[2]:
            return False
        if (x, y) not in met:
            met[(x, y)] = min(x[2], y[2]) == 1 and max(x[1] - x[0], y[1] - y[0]) > 32 or bool(set(range(*x)) & set(range(*y)))
        return met[(x, y)]

    def covers(x, y):
        return x[0] <= y[0] and y[1] <= x[1] and (x[2] == 1 or x[2] == y[2] and (x[0] - y[0]) % x[2] == 0)

    def record(q, kind, fn, reads, writes, hold, more=0.0, after=()):
        deps = {i: True for i in after}
        for r, w in [(r, False) for r in reads] + [(r, True) for r in writes]:
            for piece, i, wrote in hist.get(r[0], ()):
                if (meet(r[1:], piece) and (w or wrote)) or (r[0] in PSUM and ops[i]["q"] != q):
                    deps[i] = True
        if kind == "sum":
            deps = {i: ops[i]["q"] != q for i in deps}
        me = len(ops)
        ops.append({"q": q, "kind": kind, "fn": fn, "deps": deps, "hold": hold, "more": more})
        for r in writes:
            hist[r[0]] = [x for x in hist.get(r[0], ()) if not covers(r[1:], x[0])] + [(r[1:], me, True)]
        for r in reads:
            if r not in writes:
                hist[r[0]] = hist.get(r[0], []) + [(r[1:], me, False)]
        return me

    def arrange():
        n = len(ops)
        users = [[] for _ in range(n)]
        for j, o in enumerate(ops):
            for i in o["deps"]:
                users[i].append(j)
        left = [len(o["deps"]) for o in ops]
        earliest, out = [0.0] * n, []
        line = {q: [i for i in range(n) if ops[i]["q"] == q] for q in "vatpsr"}
        free = {q: 0.0 for q in line}
        while len(out) < n:
            due, q = min((max(earliest[l[0]], free[q]), q) for q, l in line.items() if l and not left[l[0]])
            fits = [j for j in line[q][1:AHEAD] if not left[j] and ops[j]["kind"] == "call" and (q != "v" or ops[j]["hold"] < 250)
                    and max(earliest[j], free[q]) < due and max(earliest[j], free[q]) + ops[j]["hold"] <= due]
            i = fits[0] if fits else line[q][0]
            line[q].remove(i)
            out.append(i)
            free[q] = max(earliest[i], free[q]) + ops[i]["hold"]
            for j in users[i]:
                earliest[j] = max(earliest[j], free[q] + ops[i]["more"] + (WAKE if ops[j]["deps"][i] else 0.0))
                left[j] -= 1
        return out

    def issue():
        mark = {}
        for i in arrange():
            o = ops[i]
            q, todo = o["q"], {}
            if o["kind"] == "landing":
                mark[i] = o["fn"]
                continue
            for j, wait in o["deps"].items():
                if wait and j in mark:
                    todo[mark[j][0]] = max(todo.get(mark[j][0], 0), mark[j][1])
            for src in sorted(todo, key=lambda s: s != semof.get(q)):
                need(q, src, todo[src])
            if o["kind"] == "send":
                o["fn"]()
                continue
            src, step = semof.get(q), 1
            if o["kind"] == "dma":
                src, step = "d%d" % ndma[0], 16
                ndma[0] += 1
            count[src] = count.get(src, 0) + step
            o["fn"]().then_inc(T.sem[src], step)
            clocks[(src, count[src])] = {**known[q], src: count[src]}
            mark[i] = (src, count[src])

    def size(piece):
        return len(range(*piece[1:]))

    def wide(piece):
        return SCRATCH[PLACE.get(piece[0], piece)[0]][2] not in (BF, F16, U16)

    def emit(q, fn, reads, writes, rate=1.0, n=None):
        n = size(writes[0]) if n is None else n
        if any(isinstance(r, list) for r in reads + writes):
            hold = (60.0 if q == "v" else 80.0) + n * (3.8 if isinstance(writes[0], list) else 1.56)
        elif q == "v":
            both = all(r[0] not in PSUM for r in reads)
            hold = max(64.0, n * (rate if both else 1.0) * (1.0 if any(wide(r) for r in reads + writes if size(r) > 1) else 0.5))
        else:
            hold = max(64.0, n * rate) + 20.0 * (len(writes) - 1)
        more = LATE if isinstance(writes[0], list) else 0.0
        record(q, "kept" if q in stay[0] else "call", fn, [tuple(r) for r in reads], [tuple(r) for r in writes], hold, more)

    def dma(q, out, in_, more=3600.0):
        record(q, "dma", lambda: eng[q].dma_start(out[0], in_[0]), in_[1], out[1], 50.0, more)

    def send(out, in_, sem):
        return record("p", "send", lambda: g.remote_dma(out, in_[0], T.sem[sem], T.sem.lsent, pid, rid, mask), in_[1], [], 1800.0 if sem == "arx0" else 1000.0)

    def landing(sem, val, pieces, after, more):
        record("r", "landing", (sem, val), [], pieces, 0.0, more, after)

    def A(n, a, b, s=1):
        buf, o = PLACE.get(n, (n, 0))
        return (T[buf][:, o + a:o + b:s] if s > 1 else T[buf][:, o + a:o + b], [(n, a, b, s)])

    def U8(n, a, b):
        return (T[n][:, a:b].bitcast(dt.uint8), [(n, a, b, 1)])

    def U32(n, a, b):
        return (T[n][:, a:b].bitcast(dt.uint32), [(n, a, b, 1)])

    def I(win, off):
        return (win[0].indirect(off[0]), [list(win[1][0])] + off[1])

    def ext(v):
        return (v, [])

    def ap(x):
        return x[0] if isinstance(x, tuple) else x

    def rd(*xs):
        return [r for x in xs if isinstance(x, tuple) for r in x[1]]

    V = g.vector

    def tc(out, in_):
        emit("v", lambda: V.tensor_copy(out[0], in_[0]), rd(in_), out[1])

    def scatter(win, off, in_):
        emit("v", lambda: V.tensor_copy(win[0].indirect(off[0]), in_[0]), rd(off, in_), [list(win[1][0])], 1.0, size(in_[1][0]))

    def tt(out, a, b, op):
        emit("v", lambda: V.tensor_tensor(out[0], a[0], b[0], op), rd(a, b), out[1], 2.0)

    def ts(out, a, s1, op0, s2=None, op1=None):
        if op1 is None:
            emit("v", lambda: V.tensor_scalar(out[0], a[0], ap(s1), None, op0), rd(a, s1), out[1])
        else:
            emit("v", lambda: V.tensor_scalar(out[0], a[0], ap(s1), ap(s2), op0, op1), rd(a, s1, s2), out[1])

    def scan(out, d0, d1, op0, op1, first=0.0):
        emit("v", lambda: V.tensor_tensor_scan(out[0], d0[0], d1[0], first, op0, op1), rd(d0, d1), out[1])

    def listed(out, rep, n):
        scan(out, A("kt", 0, n), rep, O.mult, O.add)

    def total(out, in_):
        emit("v", lambda: V.tensor_reduce(out[0], in_[0], AX.X, O.add), rd(in_), out[1])

    def turn(out, in_):
        emit("v", lambda: V.transpose(out[0], in_[0]), rd(in_), out[1])

    def fill(out, k):
        emit("v", lambda: V.memset(out[0], k), [], out[1])

    def quant(q, s, x, kind="call"):
        record("v", kind, lambda: V.quantize_mx(q[0], s[0], x[0]), rd(x), q[1] + s[1], 15.0 + 0.27 * size(x[1][0]))

    def act(out, in_, func=AF.Copy, bias=None, scale=None, accum=None):
        kw = {}
        if bias is not None:
            kw["bias"] = ap(bias)
        if scale is not None:
            kw["scale"] = ap(scale)
        if accum is not None:
            kw["accum_out"] = accum[0]
        emit("a", lambda: g.scalar.activation(out[0], in_[0], func, **kw), rd(in_, bias, scale),
             out[1] + (accum[1] if accum is not None else []))

    def mm(out, w, ws, x, xs, start=True, stop=True):
        record("t", "call" if start else "sum", lambda: g.tensor.matmul_mx(out[0], w[0], ws[0], x[0], xs[0], start, stop),
               rd(w, ws, x, xs), out[1], PE * (16 + size(out[1][0])))

    def iota(out, pattern, base, cm, flag=False):
        kw = {"allow_small_or_imprecise_dtypes": True} if flag else {}
        record("p", "kept", lambda: g.iota(out[0], pattern, base, cm, **kw), [], out[1], 130.0 + 2 * size(out[1][0]))

    def choose(out, in_, pattern, cmp, base, cm):
        record("p", "kept", lambda: g.affine_select(out[0], in_[0], pattern, cmp, 0.0, base, cm), in_[1], out[1],
               170.0 + 2 * size(out[1][0]))

    (kI, kType, kD, kL, kS, kSn, kK, kIb, kz, kKm, kN, kOdd, kEven) = [A("col", k, k + 1) for k in range(13)]
    begins = lambda k: {"scale": A("col", 16 + k, 17 + k), "bias": A("col", 21 + k, 22 + k)}
    s16 = lambda k: A("s16", 16 * k, 16 * k + 16)
    every = lambda n, r, s, w: (T[n][r:128:s, 0:w], [(n, 0, w, 1)])
    carried = lambda r: (T.al[r:128:8, 0:C], [("al", r, C, 8)])

    dma("s", A("ut", 0, 512), ext(T.u[:, :]), 3000.0)
    for q, (a, e) in zip("as", ((0, 256), (256, C))):
        dma(q, A("x0", 4 * a, 4 * e), ext(T.x[:, 4 * a:4 * e]), 3500.0)
    dma("a", A("llr", 0, 48), ext(T.nb[:, :]), 3000.0)

    def late_loads():
        dma("s", U8("qw", 0, 512), ext(T.wc[:, :]))
        dma("s", A("sw", 0, 512), ext(T.ws[:, :]))
        dma("s", A("vt", 0, 512), ext(T.v[:, :]), 6000.0)

    ones, half, blocks = A("ones", 0, 512), A("bd1", 0, 512), A("bd", 0, 512)
    iota(A("pi", 0, 1), [[1, 1]], 0, 1)
    iota(s16(0), [[1, 16]], 0, 0, True)
    iota(A("li5", 0, 8), [[16, 8]], 0, 0)
    iota(A("idr", 0, C), [[1, C]], 0, 0, True)
    fill(A("ones", 0, 516), 1.0)
    iota(A("wn", 0, C), [[1, 16], [16, 24]], 0, 0, True)
    choose(A("et", 0, 516), A("ones", 0, 516), [[1, 516]], O.is_equal, -3, -4)
    choose(A("r8b", 0, C), A("ones", 0, C), [[0, C // 8], [1, 8]], O.not_equal, 0, 0)
    choose(half, ones, [[-16, 8], [0, 64]], O.is_ge, 0, 1)
    choose(blocks, half, [[16, 8], [0, 64]], O.is_ge, 15, -1)
    choose(A("bd", 512, 1024), blocks, [[-1, 128], [1000, 4]], O.is_ge, -1, 1)
    iota(A("li2", 0, 24), [[16, 24]], 0, 0, True)

    def later_on_g():
        for odd, (first, step) in enumerate(((96, -64), (16, 96))):
            at = 128 * odd
            for side in range(2):
                iota(A("fr", at + 20 * side, at + 20 * side + 20), [[1, L], [32, 2], [step, 2]], first + 8 * side + 1, 0, True)
                iota(A("fr", at + 40 + 24 * side, at + 64 + 24 * side), [[32, 2], [step, 2], [1, 6]], first + 8 * side + 1, 0, True)
            iota(A("fr", at + 96, at + 120), [[32, 2], [step, 2], [0, 6]], first + 7, 0, True)
        iota(A("idr", C, 2 * C), [[1, C]], C, 0, True)
        iota(A("li4", 0, 24), [[0, 4], [-1, 6]], TG - 1, 0, True)
        for b in range(4):
            iota(A("db%d" % b, C, C + 16), [[0, 16]], 0, 0, True)
        iota(A("tab", 0, 25 * TG), [[0, 25 * TG]], 512, 0, True)

    def scan_constants():
        iota(A("one", 0, 12 * TG), [[0, 12 * TG]], 1, 0, True)
        iota(A("one", 0, 12 * TG, TG), [[0, 12]], 4096, 0, True)

    def put(out, n, k):
        act(out, A("ones", 0, n), AF.Identity, bias=k, scale=0.0)

    for k in range(L):
        rows = [r for r in range(16) if TYPES[r] == k]
        for a, b in zip(rows[0::2], rows[1::2] + [None]):
            act(A("s16", 16 + a, 16 + (b or a) + 1, b - a if b else 1), A("s16", 0, 2 if b else 1), AF.Identity,
                bias=float(k), scale=0.0)
    ts(A("pi", 1, 2), A("pi", 0, 1), 15, O.bitwise_and)
    tc(kI, A("pi", 1, 2))
    tc(A("upl", 0, 8), A("li5", 0, 8))
    ts(s16(4), s16(0), kI, O.is_equal)
    ts(s16(3), s16(0), kI, O.subtract)
    ts(A("irep", 0, 24), A("ones", 0, 24), 0.0, O.mult, kI, O.add)
    ts(s16(6), s16(3), 0.0, O.not_equal)
    ts(s16(7), s16(3), 1.0, O.is_equal, KB, O.mult)
    tt(s16(8), s16(4), s16(1), O.mult)
    tt(s16(10), s16(6), s16(7), O.max)
    total(kType, s16(8))
    put(A("z0", 0, C), C, 0.0)
    at = 0
    for rows, w in TILES:
        for a in range(at + 64 * min(rows), at + 4 * w, C):
            e = min(a + C, at + 4 * w)
            zeros = A("z0", 0, e - a)
            dma("s", A("mt", a, e), (zeros[0], zeros[1] + [("x0", 0, 4 * C, 1)]), 2400.0)
        at += 4 * w
    put(A("met", 0, C), C, 0.0)
    dma("s", carried(6), every("met", 6, 8, C), 2200.0)
    ts(kS, kI, 14.5, O.is_gt, 1.0 / KB, O.max)
    for k in range(L):
        ts(begins(k)["scale"], kType, L - 1.0 - k, O.is_equal)
    tc(A("kt", 0, C), I(s16(10), A("irep", 0, 24)))
    fill(A("kd", 0, 72, 3), 0.0)
    fill(A("cl", 61, CL, 48), 0.0)
    for k in range(L):
        ts(begins(k)["bias"], begins(k)["scale"], 808.0, O.mult, -1000.0, O.add)
    ts(kD, begins(0)["scale"], -float(C), O.mult)
    listed(A("cs", 0, C), A("wn", 0, C), C)
    ts(A("kd", 1, 72, 3), A("ones", 0, 24), kS, O.mult)

    def small_constants():
        ts(A("prm", 0, 24), A("cs", 15, C, 16), kS, O.mult)
        ts(kKm, kI, 14.5, O.is_lt, KB - 1.0, O.mult)
        for side in range(2):
            fill(A("d1k", 12 * NB * side, 12 * NB * (side + 1)), (1 - 2 * side) * HUGE)

    def step_constants():
        act(A("b0", 0, C), A("idr", 0, C), AF.Identity, **begins(1))
        act(A("p0", 0, C), A("idr", 0, C), AF.Identity, **begins(0))
        for k in range(1, 4):
            act(A("b%d" % k, 0, C), A("idr", 0, C), AF.Identity, **begins(k + 1))

    def late_constants():
        tc(A("blk", 0, 24), A("idr", 0, 24))
        ts(A("pi", 2, 3), A("pi", 0, 1), 4, O.logical_shift_right, 1, O.bitwise_and)
        tc(kOdd, A("pi", 2, 3))

    quant(A("qu0", 0, 128), A("su0", 0, 128), A("ut", 0, 512), "kept")
    tc(U32("qu", 0, 128), I(U32("qu0", 0, 128), A("upl", 0, 8)))
    act(A("su", 0, 128), I(A("su0", 0, 128), A("upl", 0, 8)))
    unpacking = lambda b: quant(A("qe", 128 * b, 128 * b + 128), A("se", 128 * b, 128 * b + 128), A("et", 3 - b, 515 - b))

    S = lambda a, e: A(("pS", "pF2", "pC")[a // 128], 0, e - a)

    def scores(t, a, e):
        qx, sx, w = A("qx%d" % t, a, e), A("sx%d" % t, a, e), "v" if t == R else "u"
        quant(qx, sx, A("x%d" % t, 4 * a, 4 * e))
        mm(S(a, e), A("q" + w, 0, 128), A("s" + w, 0, 128), qx, sx)

    def planes(codes, plane, banks=PSUM[2:6]):
        for b in range(4):
            mm(A(banks[b], 0, C), A("qe", 128 * b, 128 * b + 128), A("se", 128 * b, 128 * b + 128), codes, plane)

    def meeting_constants():
        put(A("zs", Z0, Z0 + NB * C, NB), C, 0.0)
        put(A("ne", NB - 1, 24 * NB, NB), 24, 0.0)
        for side in range(2):
            f = [m[side] + 1.0 if m else None for m in MEET]
            f[NB - 2] = -1.0
            f = [f[e] if f[e] is not None or e == NB - 1 else f[e + 1] for e in range(NB)]
            steps = [f[e] - f[e + 1] for e in range(NB - 2)] + [f[NB - 2], -1.0 - f[0]]
            for e in range(NB):
                if steps[e] != 1 - 2 * side:
                    put(A("d1k", 12 * NB * side + e, 12 * NB * (side + 1), NB), 12, steps[e] * HUGE)

    def count_constants():
        act(s16(5), s16(4), AF.Identity, bias=1.0, scale=kKm)
        act(kL, kI, AF.Identity, bias=192.0, scale=512.0)
        put(A("s16", 80, 81), 1, 0.0)
        put(A("cna", 0, 1), 1, 0.0)
        act(A("kp", 0, C), I(s16(5), A("irep", 0, 24)))
        act(A("ends", 0, C), I(s16(4), A("irep", 0, 24)), AF.Identity, bias=512.0, scale=-512.0)
        for a in range(1, 4):
            dma("s", A("ends", a * C, (a + 1) * C), A("ends", 0, C), 2400.0)

    def rank_constants():
        act(kz, kI, AF.Identity, bias=0.2)
        act(kK, kKm, AF.Identity, bias=1.0)
        act(kN, kKm, AF.Identity, bias=-1.0, scale=-1.0)
        act(A("npos", 0, 24), A("li2", 0, 24), AF.Identity, scale=kK)

    def slot_constants():
        act(kEven, kOdd, AF.Identity, bias=1.0, scale=-1.0)
        for at in (0, 128):
            put(A("fr", at + 88, at + 96), 8, 6.0)
            put(A("fr", at + 120, at + 128), 8, 6.0)
        put(A("order", 0, 16), 16, 0.0)
        act(A("fs", 128, 256), A("fr", 128, 256), scale=kOdd)
        act(A("fs", 0, 128), A("fr", 0, 128), scale=kEven)
        put(A("dn", 0, WT), WT, -HUGE)
        act(kSn, kS, scale=-1.0)
        act(kIb, kI, AF.Identity, bias=0.02, scale=-16.0 * L / TG)
        put(A("dn", 0, WT, 8), WT // 8, -HUGE * 2.0 ** 15)
        put(A("dn", 1, WT, 8), WT // 8, -HUGE / 2)
        put(A("on", 0, WT), WT, 0.0)
        put(A("dd", 0, 2 * C, 2), C, 0.0)
        put(A("wt", 0, M), M, 0.0)
        act(A("tagq", 0, 24), A("li4", 0, 24), AF.Identity, bias=kIb, scale=16.0 / TG)
        for b in range(4):
            put(A("hs%d" % b, SL, SL + 16), 16, 0.0)

    def own_planes():
        for b in range(4):
            if sum(e - a for k, a, e in GA if k == b) < C:
                act(A("fb%d" % b, 0, C), A(OWN[b], 0, C))

    def their_planes(first, end):
        for b in range(first, end):
            act(A("db%d" % b, 0, C), A("pF%d" % b, 0, C), scale=0.5)

    def plain_links():
        ts(A("ll", 0, 48), A("llr", 0, 48), 511, O.bitwise_and)

    def link_lists():
        tt(A("kd", 2, 72, 3), A("ll", 24, 48), A("ll", 0, 24), O.subtract)
        tc(A("lu", 0, 48), A("ll", 0, 48))
        ts(A("cl", 77, CL, 48), A("ll", 0, 24), -192.0, O.add)

    def link_rows():
        act(A("p0", 0, C), I(A("idr", 0, C), A("lu", 0, 24)), AF.Identity, **begins(0))
        act(A("dd", 1, 2 * C, 2), I(A("idr", 0, 2 * C), A("du", 0, 24)), AF.Identity, scale=begins(0)["scale"], bias=kD)

    def links_out():
        turn(A("lot", 0, 64), A("lo", 0, 64))
        for h in range(2):
            dma("s", ext(T.ol[h:8:2, 0:512]), A("lot", 16 * h, 16 * h + 16))
        for a in range(4):
            for h in range(2):
                dma("s", ext(T.ol[2 * a + h:2 * a + h + 1, 512:768]),
                    (T.lot[32 * a:32 * a + 16, 32 + 16 * h:48 + 16 * h], [("lot", 32, 64, 1)]))

    trios = _trios()
    for t in range(R):
        last = t == R - 1
        qx, sx = A("qx%d" % t, 0, C), A("sx%d" % t, 0, C)
        if t == 0:
            for a, e in PIECES:
                scores(0, a, e)
            plain_links()
            link_lists()
            step_constants()
        else:
            planes(qx, sx, OWN)
        for a, e in PIECES:
            ts(A("fp", 2 * a, 2 * e, 2), S(a, e), 0.0, O.is_gt)
            act(A("ssb", a, e), S(a, e))
        calls = {
            "l": lambda a, e: listed(A("cl", 3 * a, 3 * e, 3), A("fp", 2 * a, 2 * e, 2), e - a),
            "v": lambda a, e: scan(A("v0", 2 * a, 2 * e), A("dd", 2 * a, 2 * e), A("fp", 2 * a, 2 * e), O.mult, O.add),
            "m": lambda a, e: scan(A("cm", 0, 72), A("kd", 0, 72), A("cl", 45, CL, 16), O.mult, O.add),
            "u": lambda a, e: ts(A("cu", 0, 24), A("cm", 2, 72, 3), 192.1, O.add),
            "w": lambda a, e: ts(A("cu2", 0, 24), A("cm", 2, 72, 3), 2.0, O.mult, C + 1.1, O.add)}
        stay[0] = "v" if t else ""
        for name in FIRSTS.split():
            if t or name[0] in "lmu":
                calls[name[0]](*PIECES[int(name[1])])
        stay[0] = ""
        if t == 0:
            small_constants()
        act(A("ssp", 0, C), I(A("ssb", 0, C), A("prm", 0, 24)))
        dma("s", A("sn", 0, 24), every("ssp", 0, 16, C), 2400.0)
        codes = U8("qx%d" % t, 0, C)
        sent = [send(T["lc%d" % t][:, 0:C].bitcast(dt.uint8), (codes[0], codes[1] + [("ssp", 0, C, 1)]), "arx%d" % t),
                send(T["ls%d" % t][:, 0:C], sx, "arx%d" % t)]
        landing("arx%d" % t, 2 * width, [("lc%d" % t, 0, C, 1), ("ls%d" % t, 0, C, 1)], sent, 9500.0 if t else 8000.0)
        if t == 0:
            later_on_g()
            meeting_constants()
        act(A("sp", 0, 768), I(A("ssb", 0, C), A("lu", 0, 48)))
        dma("s", carried(7), every("sp", 7, 16, 2 * C), 2200.0)
        for k in range(1 if t else 0, 4):
            win = I(A("v%d" % (k - 1) if k else "p0", 0, C), A("cu", 0, 24))
            tt(A("v%d" % k, 0, C), I(A("v0", 0, 2 * C), A("cu2", 0, 24)) if t and k == 1 else win, A("b%d" % k, 0, C), O.max)
            if t == 0:
                unpacking(k)
        act(A("gg", 0, CUT), I(A("v3", 0, C), A("lu", 0, CUT // 16)))
        for a, e in ((CUT, C + 256), (C + 256, 2 * C)):
            tc(A("gg", a, e), I(A("v3", 0, C), A("lu", a // 16, e // 16)))
        if t == 0:
            count_constants()
        for a, e in ((CUT, C + 256), (C + 256, 2 * C), (0, CUT)):
            turn((T.gt[:, a // 16:e // 16, :], [("gt", a, e, 1)]), A("gg", a, e))
        act(A("g32", 0, 2 * C), A("gg", 0, 2 * C), AF.Identity, bias=kL)
        for k in range(1, L + 1):
            dma("s", carried(k), every("g32", k, 16, 2 * C), 2200.0)
        if t:
            stay[0] = "a"
            own_planes()
            stay[0] = ""
        else:
            planes(qx, sx, OWN)
        for x, ((r, s), (r2, s2)) in enumerate(trios):
            if x < NB // 3 - 1:
                tt(A("ne", x, 24 * NB, NB // 3), (T.gt[:, 0:24, r:r + 2 * s + 1:s], [("gt", 0, C, 1)]),
                   (T.gt[:, 24:48, r2:r2 + 2 * s2 + 1:s2], [("gt", C, 2 * C, 1)]), O.not_equal)
            for k in range(2 if x == NB // 3 - 1 else 0):
                tt(A("ne", x + NB // 3 * k, 24 * NB, NB), (T.gt[:, 0:24, r + k * s], [("gt", 0, C, 1)]),
                   (T.gt[:, 24:48, r2 + k * s2], [("gt", C, 2 * C, 1)]), O.not_equal)
        for a, e in PIECES:
            a, e = a // 16 * NB, e // 16 * NB
            for side in range(2):
                at = 8 * NB * side
                scan(A("zs", at + 16 * a, at + 16 * e, 16), A("ne", a, e), A("d1k", 12 * NB * side, 12 * NB * side + e - a),
                     O.mult, O.add, -(L + 1.0) * HUGE)
        for a, e in PIECES:
            scan(A("ex", a, e), A("r8b", a, e), A("zs", Z0 + NB * a, Z0 + NB * e, NB), O.mult, O.add)
        for a, e in PIECES:
            turn(A("kr", a, e), A("ex", a, e))
            act(A("k32", a, e), A("kr", a, e))
        dma("s", carried(0), every("k32", 0, 8, C), 2200.0)
        if t == 0:
            for a in range(4, 16, 4):
                dma("s", A("ends", a * C, (a + 4) * C), A("ends", 0, 4 * C), 3000.0)
            late_loads()
            late_constants()
        calls = {"s": lambda a, e: listed(A("sk", a, e), A("kr", a, e), e - a),
                 "m": lambda a, e: tt(A("ms", a, e), S(a, e), A("kr", a, e), O.min),
                 "l": lambda a, e: tt(A("slm", 0, 24), A("sk", 15, C, 16), A("sn", 0, 24), O.min)}
        stay[0] = "v"
        for name in KEYS.split():
            calls[name[0]](*PIECES[int(name[1])])
        spot, at = {}, 0
        for rows, w in TILES:
            for i, c in enumerate(rows):
                spot[c] = A("mt", at + i, at + 64 * min(c, 24), 4)
            at += 4 * w
        score = lambda c: A("slm", c, c + 1)
        sg = lambda c: A("sg", 8 * c * (c - 1), 8 * c * (c + 1))
        alone = [c for rows, w in TILES for c in rows if c < 24 and c not in XROWS + ZROWS]
        for c, d in zip(alone + [None] * APART, [None] * APART + alone):
            if c:
                act(sg(c), A("ms", 0, 16 * c), AF.Sign, bias=score(c), scale=-1.0)
            if d:
                act(spot[d], sg(d), AF.Relu, accum=A("cna", d, d + 1))
        at, sums, rows_left = 0, [], sorted(ZROWS, reverse=True)
        below = lambda c: ts(spot[c], A("ms", 0, 16 * c), score(c), O.is_lt)

        def row_sums(n):
            for c in rows_left[:n]:
                e = C * (ZROWS.index(c) + 1)
                scan(A("rs", e - 16 * c, e), A("ones", 0, 16 * c), spot[c], O.mult, O.add)
            del rows_left[:n]

        def column_sums(k, at, w):
            a, s = at // 4, 128 if k == 0 else 0
            quant(A("qm", a, a + w), A("sm", a, a + w), A("mt", at, at + 4 * w))
            mm(A("pC", 0, w), A("qbd", s, s + 128), A("sbd", s, s + 128), A("qm", a, a + w), A("sm", a, a + w), k == 0, k == 5)

        if FIRST not in alone:
            below(FIRST)
        for k, (rows, w) in enumerate(TILES):
            for c in sorted(rows, key=lambda c: c == 24):
                if c == 24:
                    tt(spot[c], I(A("slm", 0, 24), A("blk", 0, 24)), A("ms", 0, C), O.is_gt)
                elif c not in alone and c != FIRST:
                    below(c)
                if t == 0 and c in (24, 20):
                    a = 128 if c == 24 else 0
                    quant(A("qbd", a, a + 128), A("sbd", a, a + 128), A("bd", 4 * a, 4 * a + 512))
                if sums and c not in alone and c != FIRST:
                    column_sums(*sums.pop(0))
            row_sums(ZN[k])
            while sums:
                column_sums(*sums.pop(0))
            sums.append((k, at, w))
            at += 4 * w
        if t == 0:
            rank_constants()
        for c in XROWS:
            act(A("junk", C * (c % 2), C * (c % 2) + 16 * c), spot[c], AF.Identity, accum=A("cna", c, c + 1))
        row_sums(ZN[6])
        column_sums(*sums.pop())
        row_sums(len(ZROWS))
        scan(A("eqs", 0, C), A("kp", 0, C), spot[24], O.mult, O.add)
        for a, e in ZRUNS:
            k = ZROWS.index(a)
            ts(A("cnt", a, e), A("rs", C * k + C - 1, C * (k + e - a), C), kN, O.mult)
        tt(A("pre", 0, 24), A("npos", 0, 24), A("eqs", 15, C, 16), O.subtract)
        stay[0] = ""
        for a, e in ARUNS:
            act(A("cnt", a, e), A("cna", a, e), AF.Identity, scale=kN)
        if t == 0:
            slot_constants()
            own_planes()
        listed(A("cs", 0, C), A("pC", 0, C), C)
        tt(A("rk3", 0, 24), A("cnt", 0, 24), A("pre", 0, 24), O.add)
        tt(A("rk", 0, 24), A("rk3", 0, 24), A("cs", 15, C, 16), O.add)
        ts(A("rku", 0, 24), A("rk", 0, 24), kS, O.mult, kz, O.add)
        scatter(A("order", 16, 16 + C), A("rku", 0, 24), A("al", 0, C))
        planes(A("lc%d" % t, 0, C), A("ls%d" % t, 0, C))
        their_planes(0, DB if t else 0)
        xt, on = A("xt", 0, WT), A("on", 7, WT, 16)
        calls = {
            "c0": lambda: t or tt(A("fr", 0, 128), A("fs", 0, 128), A("fs", 128, 256), O.add),
            "c1": lambda: t or listed(A("fs", 0, 128), A("fr", 0, 128), 128),
            "c2": lambda: t or ts(A("fin", 0, 8), A("fs", 15, 128, 16), kS, O.mult),
            "ta": lambda: turn(A("xt", 0, 96), A("order", 0, 96)),
            "tb": lambda: turn(A("xt", 96, WT), A("order", 16, 80)),
            "down": lambda: scan(A("hd", 0, WT), A("dn", 0, WT), xt, O.add, O.max),
            "up": lambda: ts(A("xu", 0, WT), xt, 4096.0, O.add),
            "on": lambda: tt(on, A("xt", 15, WT, 16), A("xt", 7, WT, 16), O.is_gt),
            "lt": lambda: act(A("lt", 0, 32), I(A("on", 0, WT), A("fin", 6, 8)), AF.Identity, bias=-3072.0, scale=6144.0),
            "db": lambda: their_planes(DB if t else 4, 4),
            "ab": lambda: scan(A("ab", 0, WT), A("hd", 0, WT), A("xu", 0, WT), O.max, O.min),
            "lh": lambda: ts(A("lh", 0, 96), I(A("ab", 0, WT), A("fin", 0, 6)), -4096.0, O.add, float(C), O.max),
            "side": lambda: act(A("side", 0, 4), A("on", 103, WT, 16), AF.Identity, bias=1.0, scale=-2.0),
            "node": lambda: act(A("side", 4, 8), A("ab", 96 + L, WT, 16), AF.Relu, bias=-4096.0),
            "wt": lambda: tt(A("wt", 0, M, 16), A("side", 4, 8), A("side", 0, 4), O.mult),
            "wx": lambda: act(A("wx", 0, M), I(A("wt", 0, M), A("upl", 0, 4))),
            "met": lambda: turn(A("met", 0, M), A("wx", 0, M)),
            "lj": lambda: ts(A("lj", 0, 40), A("lh", 0, 40), 511, O.bitwise_and),
            "bd0": lambda: tt(A("bd0", 0, 24), A("lh", 64, 88), A("lt", 0, 24), O.add),
            "own": lambda: tc(A("own%d" % t, 0, 40), A("lj", 0, 40)),
            "bt": lambda: tt(A("bt", 0, 24), A("bd0", 0, 24), A("lh", 40, 64), O.max),
            "bh": lambda: ts(A("bh", 0, 24), A("bt", 0, 24), 496, O.bitwise_and),
            "bu": lambda: tc(A("bu", 0, 24), A("bt", 0, 24)),
            "bo": lambda: tt(A("bo", 0, 24), A("bh", 0, 24), A("tagq", 0, 24), O.add)}
        stay[0] = "v"
        for name in SLOTS.split():
            calls[name]()
        stay[0] = ""
        sent = [send(T["came%d" % t][:, 0:40], A("own%d" % t, 0, 40), "arl%d" % t)]
        landing("arl%d" % t, width, [("came%d" % t, 0, 40, 1)], sent, 1400.0)
        if t == 0:
            scan_constants()
        piece = lambda n, k: A(n, TG * k, TG * k + TG)
        part = lambda n, k: A(n, 6 * k, 6 * k + L)
        tab = A("tab", 0, 25 * TG)

        def value(k):
            act(piece("val", k), I(A("ends", 0, 16 * C), part("bu", k)), AF.Identity, bias=TG * k - UP * t)

        def lower(k):
            tt(piece("tmp", k), I(tab, part("ofu", k)), piece("val", k), O.min)

        def store(k):
            scatter(tab, part("ofu", k), piece("tmp" if k else "val", k))

        def z_plane(b):
            z, win = A("za", SL * b, SL * b + SL), A("db%d" % b, 0, C + 16)
            act(z, I(win, A("came%d" % t, 0, 20)))
            other, out = I(win, A("came%d" % t, 20, 40)), A("zt", b, 4 * SL, 4)
            if b < 4 - ZA:
                tt(out, other, z, O.add)
            else:
                act(A("zb", SL * (3 - b), SL * (4 - b)), other)
                tt(out, A("zb", SL * (3 - b), SL * (4 - b)), z, O.add)

        calls = {"wa": lambda: act(A("wn", 0, 192), I(A("met", 0, C), A("rku", 0, 12))),
                 "wb": lambda: act(A("wn", 192, C), I(A("met", 0, C), A("rku", 12, 24))),
                 "w0": lambda: listed(A("wl", 0, 192), A("wn", 0, 192), 192),
                 "w1": lambda: listed(A("wl", 192, C), A("wn", 192, C), 192),
                 "an": lambda: [ts(A("an", 0, 24), A("wl", 15, C, 16), kSn, O.mult, 0.0, O.max),
                                ts(A("an", 24, 48), A("wl", 15, C, 16), kS, O.mult, 0.0, O.max)],
                 "lr": lambda: tt(A("llr", 0, 48), A("ll", 0, 48), A("an", 0, 48), O.max),
                 "ll": plain_links,
                 "lu": lambda: last or link_lists(),
                 "du": lambda: last or ts(A("du", 0, 24), A("kd", 2, 72, 3), float(C), O.add),
                 "db": lambda: their_planes(0, 0 if t else 4),
                 "ofu": lambda: ts(A("ofu", 0, 24), A("bo", 0, 24), TG / 16.0, O.mult)}
        stay[0] = "v"
        for name in SEARCH.split():
            if name in calls:
                calls[name]()
            else:
                {"l": lower, "s": store, "z": z_plane, "v": value}[name[0]](int(name[1]))
        stay[0] = ""
        edges = [TG * sum(ZS[:k]) for k in range(len(ZS) + 1)]
        least = lambda a, e: scan(A("ste", a, e), A("one", 0, e - a), A("tab", a, e), O.add, O.min)
        least(edges[0], edges[1])
        w = lambda b: (A("qw", 128 * b, 128 * b + 128), A("sw", 128 * b, 128 * b + 128))
        for a, e, bank in ((0, ZP, "pF0"), (ZP, SL, "pS")):
            quant(A("qz", a, e), A("sz", a, e), A("zt", 4 * a, 4 * e))
            mm(A(bank, 0, e - a), *w(0), A("qz", a, e), A("sz", a, e))
        if not last:
            link_rows()
        for b in range(1, 4):
            mm(A("pF%d" % b, 0, SL), *w(b), A("qz", 0, SL), A("sz", 0, SL))
        for b in range(4):
            for k in range(L):
                at = A("pS", M * k - ZP, M * k + M - ZP) if b == 0 and M * k >= ZP else A("pF%d" % b, M * k, M * k + M)
                act(A("hs%d" % b, k, SL, L), at, scale=0.03125)
        for a, e in zip(edges[1:], edges[2:]):
            least(a, e)
        ts(A("eu", 0, 24), A("ste", TG - 1, 24 * TG, TG), UP * t, O.add, float(SL), O.min)
        x = lambda b, a, e: A("x%d" % (t + 1), 4 * a + b, 4 * e, 4)
        h = lambda b, a, e: I(A("hs%d" % b, 0, SL + 16), A("eu", a // 16, e // 16))
        for b, a, e in GA:
            act(A("ga%d" % b, a, e), h(b, a, e))
        for b, a, e in STATE:
            if b == 4:
                scores(t + 1, a, e)
            elif (b, a, e) in GA:
                tt(x(b, a, e), A(OWN[b], a, e), A("ga%d" % b, a, e), O.add)
            else:
                tt(x(b, a, e), h(b, a, e), A("fb%d" % b, a, e), O.add)
            if last and b == 0:
                fill(A("lo", 48, 64), 0.0)
                tc(A("lo", 0, 48), A("ll", 0, 48))
            if last and b == 1:
                links_out()
        if t == 0:
            quant(A("qv", 0, 128), A("sv", 0, 128), A("vt", 0, 512))
        for a, e in ((0, 192), (192, C)) if not last else ():
            tt(A("fp", 2 * a + 1, 2 * e, 2), A("p0", a, e), A("b0", a, e), O.max)
        for a, e in PIECES if last else ():
            dma("s", ext(T.oc[:, 4 * a:4 * e]), U8("qx%d" % R, a, e))
            act(A("ys", a, e), S(a, e))
        for k in range(4 if last else 0):
            dma("s", ext(T.osc[4 * k:4 * k + 4, :]), (T["sx%d" % R][32 * k:32 * k + 4, 0:C], [("sx%d" % R, 0, C, 1)]))
        for a, e in PIECES if last else ():
            dma("a" if e == C else "s", ext(T.y[:, a:e]), A("ys", a, e))

    issue()
    g.wait_ge(T.sem.lsent, R * 3 * width)
    for t in range(R):
        need("p", "arx%d" % t, 2 * width)
        need("p", "arl%d" % t, width)
    stores = ["d%d" % k for k in range(ndma[0])]
    for src in stores[:-2] + list(semof.values()) + stores[-2:]:
        need("p", src, count[src])
